import numpy as np, ml_dtypes
CORES = [25,29,65,69,153,157,193,197]
N = 8
BF = ml_dtypes.bfloat16
def gentries(a):
    return np.ascontiguousarray(a.reshape(8, 16, -1).transpose(0, 2, 1)).reshape(8, -1)
def gtable(e):
    e = np.asarray(e); return np.ascontiguousarray(e.reshape(8, -1, 16).transpose(0, 2, 1)).reshape(128, -1).astype(np.int32)
W, D, L, B, K, RO, Q = 4096, 32, 128, 32, 4096, 4, 3
def join(p, c):
    return (((p * c) >> 5) + p + 37 * c) & (W - 1)
def parts(rng):
    x = rng.integers(0, 256, (N, 8, 16, W)); p = rng.integers(0, W, (N, 8, D, L)); c = rng.integers(0, W, (N, 8, D, L))
    c = np.where(rng.random(c.shape) < 0.0625, p, c); s = rng.integers(1, 65, (N, 8, 1, L))
    n = (rng.integers(0, 256, (N, 8, 16, L)) * s * s) >> 12
    return x, p, c, n, rng.integers(0, 64, (N, 8, 16)), rng.integers(1100, 1800, (N, 8))
def pack(x, p, c, n, w, t):
    return {"lit": np.ascontiguousarray(x.reshape(N, 128, W)).astype(np.float32).astype(BF), "pn": np.stack([gtable(a) for a in p.reshape(N, 8, K)]), "cn": np.stack([gtable(a) for a in c.reshape(N, 8, K)]),
            "neg": np.ascontiguousarray(n.reshape(N, 128, L)).astype(np.float32).astype(BF), "wt": w.reshape(N, 128, 1).astype(np.int32), "th": t.reshape(N, 8, 1).astype(np.int32)}
def pat(rng, m):
    return ((np.arange(16)[:, None] * (2 * rng.integers(0, 8, m.shape) + 1) + rng.integers(0, 16, m.shape)) & 15) < m
def setup_inputs(rng):
    return pack(*parts(rng))
def setup_inputs_spread(rng):
    x, p, c, n, w, t = parts(rng)
    x = rng.integers(0, 256, x.shape) >> rng.integers(0, 8, (N, 8, 1, W)); n = rng.integers(0, 256, n.shape) >> rng.integers(0, 8, (N, 8, 1, L))
    p = np.minimum((W * rng.random(p.shape) ** 3).astype(np.int64), W - 1); c = np.minimum((W * rng.random(c.shape) ** 2).astype(np.int64), W - 1)
    w = w >> rng.integers(0, 6, w.shape); t = np.minimum(np.exp2(12 * rng.random((N, 8))).astype(np.int64), 4080)
    return pack(x, p, c, n, w, t)
def setup_inputs_ends(rng):
    cho = np.array([0, 1, 7, 8, 9, 10, 15, 16])
    x = 255 * pat(rng, rng.choice(cho, (N, 8, 1, W))); n = 255 * pat(rng, rng.choice(cho, (N, 8, 1, L)))
    p = (W - 1) * rng.integers(0, 2, (N, 8, D, L)); c = (W - 1) * rng.integers(0, 2, (N, 8, D, L))
    w = 63 * rng.integers(0, 2, (N, 8, 16)); w[:, 0] = 0; w[:, 7] = 63
    t = 4080 * ((np.arange(8)[None, :] + np.arange(N)[:, None] + N + 1) & 1)
    x[:, 1::2, :, 0] = 0; x[:, 1::2, :, W - 1] = 255; x[:, 2, :, 0] = 255; x[:, 2, :, W - 1] = 0
    x[:, 7, :, int(join(W - 1, W - 1))] = 255
    for i in (0, 1, L - 1): p[:, 7, :, i] = W - 1; c[:, 7, :, i] = W - 1; n[:, 7, :, i] = 255
    for i in (2, L - 2): p[:, 7, :, i] = W - 1; c[:, 7, :, i] = 0; n[:, 7, :, i] = 255
    return pack(x, p, c, n, w, t)
def setup_inputs_corners(rng):
    x, p, c, n, w, t = parts(rng)
    a = np.arange(W // 2); a = a[join(a, a) >= W // 2]; m = len(a) // 6; F = np.ascontiguousarray(a[:6 * m].reshape(m, 6).T)
    o = np.argsort(rng.random((N, 8, 16)), axis=-1)[..., None]; sh = (N, 8, 16, m); u = rng.random(sh)
    low = [u < 0, (o < 7) & (u < 2), (o < 7) & (u < 0.3), (o == rng.integers(7, 16, (N, 8, 1, m))), (o < 8) | (u < 0.3), u < 0.25]
    for f in range(6):
        hi = 100 + rng.integers(0, 156, sh) * rng.integers(0, 2, sh); lo = 99 - rng.integers(0, 100, sh) * rng.integers(0, 2, sh)
        x[..., F[f]] = np.where(low[f], lo, hi)
    x[..., W // 2:] = rng.integers(100, 256, (N, 8, 16, W - W // 2))
    ty = rng.integers(0, 6, (N, 8, 1, L)); j = np.arange(D)[None, None, :, None]; pl = rng.integers(0, D - 1, (N, 8, 1, L))
    fam = 2 * rng.integers(0, 2, (N, 8, D, L))
    fam = np.where((ty == 0) & (j == 0), 4, fam); fam = np.where(ty == 1, 0, fam)
    fam = np.where(((ty == 2) | (ty == 3)) & (j == pl), 1, fam); fam = np.where((ty == 2) & (j == D - 1), 3, fam)
    fam = np.where(ty == 4, 5, fam); fam = np.where(ty == 5, rng.integers(0, 4, fam.shape), fam)
    free = rng.random((N, 8, 1, L)) < 0.125
    p = F[fam, rng.integers(0, m, fam.shape)]; c = np.where(free, c, p); n = np.where(free, n, 100)
    w[:, 0] = 0; w[:, 1] = 63; w[:, 2::2] = 63 * rng.integers(0, 2, (N, 3, 16))
    t = rng.choice(np.array([0, 63, 1365, 4080]), (N, 8)); t[:, 3] = 0; t[:, 5] = 4080
    return pack(x, p, c, n, w, t)
def setup_inputs_ties(rng):
    x, p, c, n, w, t = parts(rng); h = W // 2
    t = rng.integers(200, 1600, (N, 8)); t[:, 3] = rng.choice(np.array([2048, 2051, 3000, 3001, 3003, 4016, 4063, 4064]), N); t[:, 5] = rng.integers(2048, 4079, N); t[:, 7] = 4079
    tot = t[..., None, None] + rng.integers(-1, 2, (N, 8, 1, h))
    d = (tot >> 4) + (np.arange(16)[:, None] < (tot & 15))
    u = np.minimum(rng.integers(0, 12, (N, 8, 8, h)), np.minimum(255 - d[:, :, 0::2], d[:, :, 1::2]))
    d[:, :, 0::2] += u; d[:, :, 1::2] -= u
    lo = (np.minimum(144, 256 - d) * rng.random(d.shape)).astype(np.int64); hi = lo + d; sg = rng.random(lo.shape) < 0.5
    x[..., 0::2] = np.where(sg, hi, lo); x[..., 1::2] = np.where(sg, lo, hi)
    free = rng.random((N, 8, 1, L)) < 0.125; a = 2 * rng.integers(0, h, (N, 8, D, L)); b = rng.integers(0, 2, (N, 8, D, L))
    p = np.where(free, p, a + b); c = np.where(free, c, a + 1 - b)
    v = np.full((N, 8, 16, L), 255)
    for k in range(2):
        e = [np.take_along_axis(x, i[:, :, None, :], 3) for i in (p[:, :, k], c[:, :, k], join(p[:, :, k], c[:, :, k]))]
        v = np.minimum(v, np.minimum(np.maximum(e[0], e[1]), e[2]))
    n = np.where(free, n, np.minimum(v + (rng.random(v.shape) < 0.3), 255))
    return pack(x, p, c, n, w, t)
def setup_inputs_crowd(rng):
    x, p, c, n, w, t = parts(rng); x = np.minimum(x, 254); top = np.array([7, 7, 7, 7, 3, 3, 3, 3])
    calm = np.where(pat(rng, np.full((N, 8, 1, L), 9)), 0, rng.integers(1, 256, n.shape))
    for q in range(N):
        for g in range(8):
            i = int(rng.integers(0, L)); col = rng.integers(0, W, 4)
            if g % 4 == 0: p[q, g] = col[0]; c[q, g] = col[1]
            if g % 4 == 1:
                own = p[q, g, :, i].copy(); p[q, g] = col[0]; p[q, g, :, i] = own
            if g % 4 == 2: p[q, g] = col[rng.integers(0, 4, (D, L))]; c[q, g] = col[rng.integers(0, 4, (D, L))]
        k = (3 - q) % 4; n[q] = calm[q] if k < 2 else 255
        g, i = int(rng.integers(0, 8)), int(rng.integers(0, L))
        if k == 1:
            x[q] = x[q] & top[:, None, None]; n[q] = np.minimum(n[q], top[:, None, None]); t[q] = np.maximum(16 * top - 63, 0)
            n[q, g, :, i] = top[g] + 1
        if k == 2: x[q] = 127 + (x[q] >> 1)
        if k == 3: n[q, g, :, i] = calm[q, g, :, i]
    c[:, :, 0] = p[:, :, 0]
    return pack(x, p, c, n, w, t)
def check_inputs(d):
    bad = []
    for k, lo, hi in (("lit", 0, 255), ("pn", 0, W - 1), ("cn", 0, W - 1), ("neg", 0, 255), ("wt", 0, 63), ("th", 0, 4080)):
        v = np.asarray(d[k]).astype(np.float64)
        if not np.all((v >= lo) & (v <= hi)): bad.append("range of " + k)
        elif np.any(v != np.floor(v)): bad.append("whole numbers in " + k)
    return bad
def pick(v, ix):
    return np.stack([v[g][:, ix[g]] for g in range(8)])
def reference(lit, pn, cn, neg, wt, th):
    X = lit.astype(np.float32).astype(np.int16).reshape(N, 8, 16, W); n = neg.astype(np.float32).astype(np.int16).reshape(N, 8, 16, L)
    P = np.stack([gentries(a) for a in pn]).astype(np.int64); C = np.stack([gentries(a) for a in cn]).astype(np.int64)
    w = wt.astype(np.int64).reshape(N, 8, 16, 1); lim = th.astype(np.int64).reshape(N, 8, 1); A = [0] * N
    j = np.arange(D)[None, :, None]
    for t in range(RO):
        newp, names, mins = [], [], []
        for r in range(N):
            h = join(P[r], C[r]); x, y, z = pick(X[r], P[r]), pick(X[r], C[r]), pick(X[r], h)
            ok = np.add.reduce(np.abs(x - y), axis=1, dtype=np.int64) <= lim[r] + (A[r] & 63)
            l = np.where(ok[:, None, :], np.minimum(np.maximum(x, y), z), np.int16(255)).reshape(8, 16, D, L)
            nm = np.where(ok, h, P[r]).reshape(8, D, L); fell = np.zeros((8, D, L), bool); esc = np.zeros((8, L), bool)
            for s in range(Q):
                M = np.minimum.accumulate(l, axis=2)
                blk = np.add.reduce(M >= n[r][:, :, None, :], axis=1, dtype=np.int64) < 9
                has = np.any(blk, axis=1)[:, None, :]; ks = np.argmax(blk, axis=1)[:, None, :]
                if s == 0: esc = ~has[:, 0]
                turn = has & (j <= ks); cut = has & (j > ks)
                nm = np.where(turn, np.concatenate([np.take_along_axis(nm, ks, 1), nm[:, :-1]], axis=1), nm)
                l = np.where(turn[:, None], np.concatenate([np.take_along_axis(l, ks[:, None], 2), l[:, :, :-1]], axis=2), l)
                l = np.where(cut[:, None], np.int16(255), l); fell = fell | cut
            m = np.minimum.reduce(l, axis=2)
            place = B * np.arange(L)[None, :] + (np.add.reduce(w[r] * m, axis=1) & (B - 1))
            val = (m + n[r]) >> 1
            for g in range(8): X[r, g][:, place[g]] = val[g]
            A[r] = int(np.count_nonzero(esc))
            newp.append(np.where(fell, C[r].reshape(8, D, L), nm).reshape(8, K))
            names.append(nm.reshape(8, K)); mins.append(np.where(esc[:, None, :], n[r], m))
        d = 1 + t % 3
        P = np.stack(newp); C = np.stack([names[(r - d) % N] for r in range(N)]); n = np.stack([mins[(r - d) % N] for r in range(N)])
    yx = np.add.reduce(X.reshape(N, 128, L, B), axis=3, dtype=np.int64).astype(np.float32)
    return {"yp": np.stack([gtable(a) for a in P]).astype(np.float32), "yc": np.stack([gtable(a) for a in C]).astype(np.float32), "yn": n.reshape(N, 128, L).astype(np.float32).astype(BF), "yx": yx}

@@ -1,0 +1,555 @@
+from concourse.mybir import AluOpType as A, AxisListType, ActivationFunctionType as F
+
+RO = 4
+BF, F32, I32, U16 = "bfloat16", "float32", "int32", "uint16"
+SCRATCH = {
+    "X": ("sbuf", [128, 4112], BF), "xg": ("sbuf", [128, 4096], BF), "dg": ("sbuf", [128, 4096], BF),
+    "rg": ("sbuf", [128, 4096], BF), "zg": ("sbuf", [128, 4096], BF), "ll": ("sbuf", [128, 4112], BF),
+    "pm": ("sbuf", [128, 4112], BF), "ind": ("sbuf", [128, 4096], BF),
+    "pin": ("sbuf", [128, 256], I32), "cin": ("sbuf", [128, 256], I32), "wi": ("sbuf", [128, 1], I32), "thi": ("sbuf", [8, 1], I32),
+    "ON": ("sbuf", [128, 2048], BF), "Bm": ("sbuf", [128, 2048], BF), "nS": ("sbuf", [64, 2048], BF),
+    "Pm": ("sbuf", [128, 1920], BF), "TB": ("sbuf", [8, 128], BF), "TR": ("sbuf", [8, 1024], BF), "OH": ("sbuf", [8, 256], BF),
+    "jo": ("sbuf", [128, 144], F32), "j16": ("sbuf", [128, 128], F32), "jb": ("sbuf", [128, 128], F32),
+    "em": ("sbuf", [128, 128], I32), "eb": ("sbuf", [128, 128], BF),
+    "ci": ("sbuf", [128, 8], I32), "cf": ("sbuf", [128, 24], F32),
+    "Id": ("sbuf", [128, 128], BF), "I64": ("sbuf", [128, 128], BF), "In": ("sbuf", [128, 128], BF),
+    "S2": ("sbuf", [128, 144], BF), "Sn": ("sbuf", [128, 144], BF), "Sw": ("sbuf", [128, 144], BF),
+    "dia": ("sbuf", [128, 128], F32), "c16": ("sbuf", [128, 128], F32), "ctl": ("sbuf", [128, 1024], BF),
+    "G1": ("sbuf", [128, 8], BF), "G64": ("sbuf", [128, 16], BF), "L1": ("sbuf", [128, 12], BF), "LE": ("sbuf", [128, 12], BF),
+    "RA": ("sbuf", [33, 72], BF), "RB": ("sbuf", [8, 48], BF),
+    "RUa": ("sbuf", [33, 256], BF), "RUb": ("sbuf", [33, 256], BF), "RX": ("sbuf", [33, 256], BF),
+    "RE": ("sbuf", [8, 256], BF), "RF": ("sbuf", [8, 256], BF),
+    "KT1": ("sbuf", [33, 256], BF), "KT2": ("sbuf", [33, 256], BF), "KT3": ("sbuf", [33, 256], BF),
+    "ONf": ("sbuf", [8, 128], F32), "G8": ("sbuf", [8, 128], F32), "thf": ("sbuf", [8, 2], F32),
+    "fpi": ("sbuf", [128, 8], F32), "fpl": ("sbuf", [128, 8], U16), "sb": ("sbuf", [128, 8], F32),
+    "Pu": ("sbuf", [128, 256], U16), "Hu": ("sbuf", [128, 256], U16), "pq": ("sbuf", [128, 256], F32),
+    "i1": ("sbuf", [128, 256], I32), "i2": ("sbuf", [128, 256], I32), "hh": ("sbuf", [128, 256], I32),
+    "i3": ("sbuf", [128, 256], I32), "i4": ("sbuf", [128, 256], I32), "Ni": ("sbuf", [128, 256], I32), "Pi": ("sbuf", [128, 256], I32),
+    "hp": ("sbuf", [128, 256], F32), "nk": ("sbuf", [128, 256], BF), "nk2": ("sbuf", [128, 256], BF), "Cf": ("sbuf", [128, 256], F32),
+    "AA": ("sbuf", [128, 272], F32), "A1": ("sbuf", [128, 264], F32), "A2": ("sbuf", [128, 264], F32), "A3": ("sbuf", [128, 272], F32),
+    "o1": ("sbuf", [128, 256], F32), "o2": ("sbuf", [128, 256], F32), "EE": ("sbuf", [128, 256], F32),
+    "nT": ("sbuf", [64, 256], BF), "mK": ("sbuf", [128, 256], BF),
+    "ct0": ("sbuf", [128, 1024], BF), "f1": ("sbuf", [128, 128], BF), "f2": ("sbuf", [128, 128], BF), "fa": ("sbuf", [128, 128], BF),
+    "bb": ("sbuf", [128, 128], BF), "sg": ("sbuf", [128, 1024], BF), "qq": ("sbuf", [128, 128], BF),
+    "e1": ("sbuf", [128, 128], BF), "e2": ("sbuf", [128, 128], BF),
+    "u1": ("sbuf", [128, 24], U16), "u2": ("sbuf", [128, 16], U16), "u3": ("sbuf", [128, 16], U16), "us": ("sbuf", [128, 8], U16),
+    "gd": ("sbuf", [128, 128], F32), "sa": ("sbuf", [128, 128], F32), "sc": ("sbuf", [128, 128], F32),
+    "fr": ("sbuf", [128, 40], F32), "si": ("sbuf", [128, 24], I32), "v1": ("sbuf", [128, 128], I32), "v2": ("sbuf", [128, 128], I32),
+    "ti": ("sbuf", [128, 2], I32), "op": ("sbuf", [128, 256], F32), "oc": ("sbuf", [128, 256], F32), "ox": ("sbuf", [128, 128], F32),
+}
+for _t in range(RO + 1):
+    SCRATCH["Cu%d" % _t] = ("sbuf", [128, 256], U16)
+    SCRATCH["nb%d" % _t] = ("sbuf", [128, 256], BF)
+for _t in range(RO):
+    SCRATCH["Nu%d" % _t] = ("sbuf", [128, 256], U16)
+    SCRATCH["mo%d" % _t] = ("sbuf", [128, 128], BF)
+for _b in range(8):
+    SCRATCH["B%d" % _b] = ("psum", [128, 512], F32)
+SEMAPHORES = (["sv", "ss", "sp", "sg", "sent"] + ["d%d" % i for i in range(16)]
+              + ["ac%d" % t for t in range(RO)] + ["an%d" % t for t in range(RO)])
+
+NENG = 8
+R_ON = "sssv"
+X_ON = "sssv"
+PH, PN = 0.0, 500.0
+MXB = ((0, 1, 2, 3), (0, 1, 2, 3))
+PK, PT, PO = 0.0, 4000.0, 500.0
+X_ON0, R_ON0 = "ssss", "vvsv"
+ORDER0 = {"v": "x0 x1 d0 r0 h d1 h2 nk0 r1 x2 d2 r2 nk1 x3 d3 r3 nk2 l0 l1 nk3 pm0 l2 l3 pm1 l4 l5 pm2 l6 l7 pm3 nkc tq AA",
+          "s": "x0 x1 x2 r0 x3 r1 z0 r2 nT Cf z1 r3 z2 z3 in0 in1 in2 in3 in4 in5 in6 in7"}
+PMB, PC, LOOK = (6, 4, 6, 4, 0, 1, 2, 3), 1000.0, 0.7
+ORDER = {"v": "x0 x1 x2 x3 hp d0 h d1 h2 nk0 d2 nk1 d3 r3 nk2 l0 l1 nk3 pm0 l2 l3 pm1 l4 l5 pm2 l6 l7 pm3 fs0 fs1 tq AA",
+         "s": "x0 x1 x2 x3 r0 nT Cf r1 z0 r2 z1 r3 z2 z3 in0 in1 in2 in3 in4 in5 in6 in7"}
+ORDER["p"] = ORDER0["p"] = ("su2a mx0 su2b mx1 su3a su3b mx2 mx3 nn0 nn1 mx4 mx5 pq0 pq1 mx6 nn2 pq2 mx7 nn3 pq3 "
+                            "nn4 pq4 nn5 pq5 nn6 nn7 pq6 pq7 ct0 ct1 ct2 ct3 ct4 ct5 ct6 ct7 k1m of0")
+FCH = ((0, 2), (2, 4), (4, 6), (6, 7), (7, 8))
+HOP, LAT, GC = 120.0, 5000.0, 1.56
+
+
+def engines_mask(topo, src, dst):
+    m = 0
+    for e in topo.engines(src, dst)[:NENG]:
+        m |= 1 << e
+    return m
+
+
+def helper_of(topo, cores, src, dst):
+    if topo.may_write(src, dst):
+        return None
+    for same in (True, False):
+        for h in topo.cores_of(src):
+            if h not in cores and (topo.die(h) == topo.die(src)) == same and topo.may_write(h, dst):
+                return h
+    return None
+
+
+def helper_program(g, core, T, topo):
+    cores = list(T.cores); n = len(cores); sent = 0
+    for t in range(RO):
+        for r in range(n):
+            dst = cores[(r + 1 + t % 3) % n]
+            if helper_of(topo, cores, cores[r], dst) != core:
+                continue
+            rid, pid = topo.addr(dst, core); mask = engines_mask(topo, core, dst)
+            for sem, ap in ((T.sem["ac%d" % t], T["Cu%d" % (t + 1)][:, 0:256]), (T.sem["an%d" % t], T["nb%d" % (t + 1)][:, 0:128])):
+                g.wait_ge(sem, NENG)
+                g.remote_dma(ap, ap, sem, T.sem.sent, pid, rid, mask)
+                sent += NENG
+    if sent:
+        g.wait_ge(T.sem.sent, sent)
+
+
+def run(ops, g, T):
+    n = len(ops)
+    lastw, reads, bank = {}, {}, {}
+    pre = [dict() for _ in range(n)]
+    for i, o in enumerate(ops):
+        e = o["e"]
+
+        def edge(j, raw):
+            if j != i:
+                need = ops[j]["e"] != e or ops[j]["sem"] is not None or e != "p"
+                pre[i][j] = pre[i].get(j, False) or need
+        for k in o["r"]:
+            if k in lastw: edge(lastw[k], True)
+        for k in o["w"]:
+            if k in lastw: edge(lastw[k], False)
+            for j in reads.get(k, []): edge(j, False)
+        for k in o["b"]:
+            if k in bank:
+                j = bank[k]
+                pre[i][j] = pre[i].get(j, False) or ops[j]["e"] != e
+            bank[k] = i
+        for j in o["after"]:
+            pre[i].setdefault(j, False)
+        for k in o["r"]: reads.setdefault(k, []).append(i)
+        for k in o["w"]:
+            lastw[k] = i; reads[k] = []
+    tags = {}
+    for i, o in enumerate(ops): tags.setdefault((o["tag"], o["e"]), []).append(i)
+    for t in range(RO):
+        for e, names in (ORDER0 if t == 0 else ORDER).items():
+            seq = [i for nm in names.split() for i in tags.get(((t, nm), e), [])]
+            for j, i in zip(seq, seq[1:]): pre[i].setdefault(j, False)
+    suc = [[] for _ in range(n)]
+    for i in range(n):
+        for j in pre[i]: suc[j].append(i)
+    left = [len(p) for p in pre]; topo_order = [i for i in range(n) if left[i] == 0]
+    for i in topo_order:
+        for j in suc[i]:
+            left[j] -= 1
+            if left[j] == 0: topo_order.append(j)
+    assert len(topo_order) == n
+    tail = [0.0] * n
+    for i in reversed(topo_order):
+        tail[i] = ops[i]["c"] + ops[i]["lat"] + max([tail[j] + HOP for j in suc[i]] + [0.0]) + ops[i]["pri"]
+    free, fin, left = {}, [0.0] * n, [len(p) for p in pre]
+    rdy = [0.0] * n
+    ready = [i for i in range(n) if left[i] == 0]
+    order = []
+    while ready:
+        st = {i: max(rdy[i], free.get(ops[i]["e"], 0.0)) for i in ready}
+        first = min(ready, key=lambda i: (st[i], -tail[i]))
+        e = ops[first]["e"]
+        cand = [i for i in ready if ops[i]["e"] == e and st[i] <= st[first] + LOOK * ops[first]["c"] and (st[i] <= st[first] or tail[i] > tail[first] + ops[first]["c"])]
+        i = max(cand, key=lambda i: (tail[i], -i))
+        ready.remove(i); order.append(i)
+        free[e] = st[i] + ops[i]["c"]; fin[i] = free[e] + ops[i]["lat"]
+        for j in suc[i]:
+            rdy[j] = max(rdy[j], fin[i] + (HOP if pre[j][i] else 0.0)); left[j] -= 1
+            if left[j] == 0: ready.append(j)
+    pos, cnt = {}, {}
+    for i in order:
+        e = ops[i]["e"]; cnt[e] = cnt.get(e, 0) + 1; pos[i] = cnt[e]
+    know, clock, waits, sig, lastg = {}, {}, {}, set(), None
+    for i in order:
+        kn = know.setdefault(ops[i]["e"], {}); wl = []
+        if ops[i]["e"] == "g" and ops[i]["sem"] is None and not ops[i]["rem"]:
+            if lastg is not None: pre[i][lastg] = True
+            lastg = i
+        for j in sorted(pre[i], key=lambda j: -fin[j]):
+            if not pre[i][j]: continue
+            key = ("x", j) if ops[j]["sem"] is not None else ops[j]["e"]
+            val = 1 if ops[j]["sem"] is not None else pos[j]
+            if kn.get(key, 0) >= val: continue
+            wl.append(j); sig.add(j); kn[key] = val
+            for k2, v2 in clock[j].items():
+                if kn.get(k2, 0) < v2: kn[k2] = v2
+        waits[i] = wl; clock[i] = dict(kn) if ops[i]["e"] != "x" else {}
+    q = {"v": g.vector, "s": g.scalar, "p": g.tensor, "g": g, "y": g.sync}
+    sems = {"v": T.sem.sv, "s": T.sem.ss, "p": T.sem.sp, "g": T.sem.sg}
+    num, tot = {}, {}
+    for i in order:
+        o = ops[i]; e = o["e"]
+        if e == "x": continue
+        for j in waits[i]:
+            if ops[j]["sem"] is not None: q[e].wait_ge(ops[j]["sem"], ops[j]["val"])
+            else: q[e].wait_ge(sems[ops[j]["e"]], num[j])
+        ins = None
+        for f in o["f"]: ins = f()
+        if o["sem"] is not None:
+            ins.then_inc(o["sem"], 16)
+        elif i in sig:
+            tot[e] = tot.get(e, 0) + 1; num[i] = tot[e]; ins.then_inc(sems[e], 1)
+    for i in order:
+        if ops[i]["sem"] is not None and i not in sig: g.wait_ge(ops[i]["sem"], ops[i]["val"])
+
+
+def rank_program(g, core, T, topo):
+    rank = T.rank_of(core)
+    if rank is None:
+        helper_program(g, core, T, topo)
+        return
+    cores = list(T.cores); ops = []; nd = [0]; pri = [0.0]; rnd = [-1]
+
+    def tag_of(w, e):
+        k = w[0] if len(w) else ""
+        if k in ("pa", "pb", "pc"): return "hp"
+        if k in ("cm", "i1"): return "h"
+        if k in ("ib", "hh"): return "h2"
+        if k[:2] in ("hp", "Hu"): return "nk" + k[2:]
+        return k
+
+    V, S, P = g.vector, g.scalar, g.tensor
+    B = [T["B%d" % b] for b in range(8)]
+
+    def add(e, c, r, w, fs, b=(), lat=0.0, sem=None, val=0, after=(), rem=False):
+        ops.append({"e": e, "c": float(c), "r": list(r), "w": list(w), "f": fs, "b": list(b), "lat": lat, "sem": sem, "val": val, "after": list(after),
+                    "pri": pri[0], "rem": rem, "tag": (rnd[0], tag_of(w, e))})
+        return len(ops) - 1
+
+    def vc(n): return 20 + 0.83 * max(64, n)
+    def ts(out, in0, s1, s2, o0, o1, n, r, w, b=()):
+        if o1 is None: add("v", vc(n), r, w, [lambda: V.tensor_scalar(out, in0, s1, None, o0)], b)
+        else: add("v", vc(n), r, w, [lambda: V.tensor_scalar(out, in0, s1, s2, o0, o1)], b)
+    def tt(out, a, c, op, n, r, w, b=()): add("v", vc(n), r, w, [lambda: V.tensor_tensor(out, a, c, op)], b)
+    def cp(out, a, n, r, w, b=()): add("v", vc(n), r, w, [lambda: V.tensor_copy(out, a)], b)
+    def ms(out, val, n, w): add("v", vc(n), [], w, [lambda: V.memset(out, val)])
+    def scan(out, d0, d1, o0, o1, n, r, w): add("v", vc(n), r, w, [lambda: V.tensor_tensor_scan(out, d0, d1, 0.0, o0, o1)])
+    def act(out, a, fn, n, r, w, b=(), bias=0.0, scale=1.0):
+        add("s", 65 + 0.83 * n, r, w, [lambda: S.activation(out, a, fn, bias=bias, scale=scale)], b)
+    def mm(lst, cyc, r, w, b):
+        add("p", 20 + 0.42 * cyc, r, w, [(lambda x=x: P.matmul(x[0], x[1], x[2], x[3], x[4])) for x in lst], b)
+    def grp(out, pairs): return [(out, l, rr, i == 0, i == len(pairs) - 1) for i, (l, rr) in enumerate(pairs)]
+    def iota(out, pat, base, cm, n, w, flt=True, r=()):
+        if flt: add("g", 130 + 1.66 * n, r, w, [lambda: g.iota(out, pat, base, cm, allow_small_or_imprecise_dtypes=True)])
+        else: add("g", 130 + 1.66 * n, r, w, [lambda: g.iota(out, pat, base, cm)])
+    def asel(out, a, pat, op, fill, base, cm, n, r, w): add("g", 170 + 1.66 * n, r, w, [lambda: g.affine_select(out, a, pat, op, fill, base, cm)])
+    def dma(e, out, a, r, w, lat, slow=False):
+        sem = T.sem["d%d" % nd[0]]; nd[0] += 1
+        qq = {"g": g, "s": S, "y": g.sync}[e]
+        if slow: f = lambda: qq.dma_start(out, a, allow_slow_non_contiguous=True)
+        else: f = lambda: qq.dma_start(out, a)
+        add(e, 60, r, w, [f], lat=lat, sem=sem, val=16)
+
+    dma("y", T.pin[:], T.pn[:], [], ["pin"], 2200)
+    dma("s", T.X[:, 0:2048], T.lit[:, 0:2048], [], ["Xa"], 4500)
+    dma("y", T.X[:, 2048:4096], T.lit[:, 2048:4096], [], ["Xb"], 4500)
+    dma("s", T.cin[:], T.cn[:], [], ["cin"], 4500)
+    dma("y", T.nb0[:, 0:128], T.neg[:], [], ["n0"], 4500)
+    pri[0] = 1e6
+    dma("g", T.wi[:], T.wt[:], [], ["wi"], 3000, True)
+    dma("g", T.thi[:], T.th[:], [], ["thi"], 3000, True)
+    cf, ci = T.cf, T.ci
+    def col(j): return cf[:, j:j + 1]
+    iota(ci[:, 0:1], [[0, 1]], 0, 1, 1, ["ci0"], False)
+    iota(T.jo[:], [[1, 144]], 0, 0, 144, ["jo"])
+    iota(T.j16[:], [[0, 8], [1, 16]], 0, 0, 128, ["j16"])
+    iota(T.jb[:], [[16, 8], [0, 16]], 0, 0, 128, ["jb"])
+    iota(T.em[:], [[-1, 128]], 0, 1, 128, ["em"], False)
+    iota(T.fpi[:], [[2048, 2], [32, 4]], 31, 0, 8, ["fpi"])
+    iota(T.sb[:], [[512, 8]], 0, 0, 8, ["sb"])
+    pri[0] = 0.0
+    iota(T.ON[:], [[0, 2048]], 1, 0, 2048, ["ON"])
+    asel(T.Bm[:], T.ON[:], [[-1, 16], [-16, 8], [0, 16]], A.is_equal, 0.0, 0, 1, 2048, ["ON"], ["Bm"])
+    asel(T.nS[:], T.ON[0:64, :], [[-1, 16], [-16, 4], [0, 32]], A.is_equal, 0.0, 0, 1, 2048, ["ON"], ["nS"])
+    asel(T.ct0[:], T.ON[:, 0:1024], [[0, 32], [1, 32]], A.is_gt, 0.0, 0, 0, 1024, ["ON"], ["cz"])
+    asel(T.OH[:], T.ON[0:8, 0:256], [[-1, 8], [0, 32]], A.is_equal, 0.0, 0, 1, 256, ["ON"], ["OH"])
+    asel(T.TR[:], T.ON[0:8, 0:1024], [[-1, 8], [0, 128]], A.is_equal, 0.0, 0, 1, 1024, ["ON"], ["TR"])
+    ms(T.TB[:], 0.5, 64, ["TB"])
+    asel(T.TB[:], T.TB[:], [[0, 8], [-1, 16]], A.is_ge, -0.5, 14, -1, 128, ["TB"], ["TB"])
+    ms(T.ONf[:], 1.0, 128, ["ONf"])
+    asel(T.G8[:], T.ONf[:], [[-1, 8], [0, 16]], A.is_equal, 0.0, 0, 1, 128, ["ONf"], ["G8"])
+    ts(ci[:, 1:2], ci[:, 0:1], 15, None, A.bitwise_and, None, 1, ["ci0"], ["ci1"])
+    ts(ci[:, 2:3], ci[:, 0:1], 5, None, A.arith_shift_right, None, 1, ["ci0"], ["ci2"])
+    ts(ci[:, 3:4], ci[:, 0:1], 31, None, A.bitwise_and, None, 1, ["ci0"], ["ci3"])
+    cp(col(0), ci[:, 0:1], 1, ["ci0"], ["c0"])
+    cp(col(1), ci[:, 1:2], 1, ["ci1"], ["c1"])
+    tt(col(2), col(0), col(1), A.subtract, 1, ["c0", "c1"], ["c2"])
+    ts(col(3), col(2), 15.0, None, A.add, None, 1, ["c2"], ["c3"])
+    cp(col(4), T.wi[:], 1, ["wi"], ["c4"])
+    ts(col(5), ci[:, 2:3], 4.0, None, A.add, None, 1, ["ci2"], ["c5"])
+    ts(col(6), ci[:, 3:4], 31.0, 8192.0, A.is_equal, A.mult, 1, ["ci3"], ["c6"])
+    for j, off in ((8, 0.0), (9, 8191.0), (10, 16382.0)):
+        ts(col(j), col(1), 128.0, off, A.mult, A.add, 1, ["c1"], ["c%d" % j])
+    ts(col(13), col(1), 32.0, None, A.mult, None, 1, ["c1"], ["c13"])
+    ts(T.sb[:], T.sb[:], col(13), None, A.add, None, 8, ["sb", "c13"], ["sb"])
+    ts(T.fpl[:], T.fpi[:], col(8), None, A.add, None, 8, ["fpi", "c8"], ["fpl"])
+    ts(T.Id[:], T.jo[:, 0:128], col(0), None, A.is_equal, None, 128, ["jo", "c0"], ["Id"])
+    ts(T.I64[:], T.Id[:], 1.0 / 64, None, A.mult, None, 64, ["Id"], ["I64"])
+    ts(T.In[:], T.Id[:], -1.0, None, A.mult, None, 64, ["Id"], ["In"])
+    ts(T.S2[:], T.jo[:], col(3), 2.0, A.is_equal, A.mult, 144, ["jo", "c3"], ["S2"])
+    ts(T.Sn[:], T.S2[:], -0.5, None, A.mult, None, 72, ["S2"], ["Sn"])
+    ts(T.Sw[:], T.S2[:], 0.5, col(4), A.mult, A.mult, 72, ["S2", "c4"], ["Sw"])
+    ts(T.dia[:], T.j16[:], col(1), None, A.is_equal, None, 128, ["j16", "c1"], ["dia"])
+    ts(T.c16[:], T.j16[:], 0.0, None, A.is_gt, None, 128, ["j16"], ["c16"])
+    ms(T.ctl[:], 0.0, 512, ["ctl"])
+    ms(T.ctl[:, 0:1024:32], 512.0, 32, ["ctl"])
+    ts(T.G1[:], T.jo[:, 0:128:16], col(2), None, A.is_equal, None, 8, ["jo", "c2"], ["G1"])
+    ts(T.G64[:, 0:8], T.G1[:], 64.0, None, A.mult, None, 8, ["G1"], ["G64a"])
+    ts(T.G64[:, 8:16], T.G1[:], -64.0 * 8192, None, A.mult, None, 8, ["G1"], ["G64b"])
+    ts(T.L1[:], T.jo[:, 0:12], col(5), None, A.is_equal, None, 12, ["jo", "c5"], ["L1"])
+    ts(T.LE[:], T.L1[:], col(6), None, A.mult, None, 12, ["L1", "c6"], ["LE"])
+    ts(T.v1[:], T.em[:], 15, None, A.bitwise_and, None, 128, ["em"], ["v1"])
+    ts(T.jb[:], T.jb[:], col(2), 16.0, A.not_equal, A.mult, 128, ["jb", "c2"], ["jb"])
+    tt(T.eb[:], T.v1[:], T.jb[:], A.add, 256, ["v1", "jb"], ["eb"])
+    for u in range(1, 16):
+        ts(T.Pm[:, 128 * (u - 1):128 * u], T.eb[:], float(u), None, A.is_equal, None, 64, ["eb"], ["Pm%d" % u])
+    pk = ["Pm%d" % u for u in range(1, 16)]
+    asel(T.Pm[:], T.Pm[:], [[0, 15], [-1, 128]], A.not_equal, -1.0, 0, 1, 1920, pk, pk + ["Pm"])
+    oh = T.Id[0:8, 0:8]
+    ms(T.RA[:], 0.0, 36, ["RA"])
+    for c in range(3):
+        for h in range(2):
+            cp(T.RA[0:8, 24 * c + 8 * h:24 * c + 8 * h + 8], oh, 8, ["Id", "RA"], ["RA%d%d" % (c, h)])
+        iota(T.RA[32:33, 24 * c:24 * c + 8], [[2048, 2], [32, 4]], 0, 0, 8, ["RAx%d" % c], r=["RA"])
+        iota(T.RA[32:33, 24 * c + 8:24 * c + 16], [[32, 8]], 0, 0, 8, ["RAy%d" % c], r=["RA"])
+        iota(T.RA[32:33, 24 * c + 16:24 * c + 24], [[16 if c == 0 else 0, 8]], 128 if c == 0 else c, 0, 8, ["RAz%d" % c], r=["RA"])
+    def rak(c): return ["RA%d0" % c, "RA%d1" % c, "RAx%d" % c, "RAy%d" % c, "RAz%d" % c]
+    for j, sc in enumerate((1.0, 1.0, -1.0 / 64, 1.0, 1.0, 1.0 / 8192)):
+        ts(T.RB[:, 8 * j:8 * j + 8], oh, sc, None, A.mult, None, 8, ["Id"], ["RB%d" % j])
+    for nm, sc in (("RUa", 32768.0), ("RUb", 32768.0), ("RX", 4.0)):
+        ms(T[nm][:], 0.0, 128, [nm + "0"])
+        ts(T[nm][0:8, :], T.OH[:], sc, None, A.mult, None, 128, ["OH", nm + "0"], [nm + "1"])
+    iota(T.RUa[32:33, :], [[0, 8], [-32768, 32]], 16384, 0, 256, ["RUa2"], r=["RUa0"])
+    iota(T.RUb[32:33, :], [[0, 8], [-32768, 32]], -16384, 0, 256, ["RUb2"], r=["RUb0"])
+    iota(T.RX[32:33, :], [[0, 256]], -16384, 0, 256, ["RX2"], r=["RX0"])
+    ts(T.RE[:], T.OH[:], -256.0, None, A.mult, None, 128, ["OH"], ["RE"])
+    ts(T.RF[:], T.OH[:], -4.0, None, A.mult, None, 128, ["OH"], ["RF"])
+    for c in (1, 2, 3):
+        ms(T["KT%d" % c][:], 0.0, 128, ["KT%d" % c, "K0%d" % c])
+        iota(T["KT%d" % c][32:33, :], [[0, 256]], 1, 0, 256, ["K1%d" % c], r=["K0%d" % c])
+    ms(T.X[:, 4096:4112], 255.0, 8, ["Xp"])
+    ms(T.ll[:, 4096:4112], 255.0, 8, ["lp"])
+    ms(T.pm[:, 4096:4112], 255.0, 8, ["pp"])
+    ms(T.AA[:, 0:8], 0.0, 8, ["A0"])
+    ms(T.AA[:, 264:272], 0.0, 8, ["Ap"])
+    cp(T.thf[:, 0:1], T.thi[:], 1, ["thi"], ["thf"])
+    mm(grp(B[6][:, 0:1], [(T.G8[:], T.thf[:, 0:1])]), 256, ["G8", "thf"], [], [6])
+    cp(col(11), B[6][:, 0:1], 1, [], ["c11"], [6])
+    cp(col(12), col(11), 1, ["c11"], ["thr"])
+    for r in range(8):
+        cp(T.Pu[:, 32 * r:32 * r + 32], T.pin[:, r:256:8], 32, ["pin"], ["Pu%d" % (r // 2) + "ab"[r % 2]])
+        cp(T.Cu0[:, 32 * r:32 * r + 32], T.cin[:, r:256:8], 32, ["cin"], ["Cu0_%d" % r])
+    pu = [["Pu%da" % qn, "Pu%db" % qn] for qn in range(4)]
+    allpu = [k for x in pu for k in x]
+    cp(T.Pi[:], T.Pu[:], 256, allpu, ["Pi"])
+    XK = ["Xa", "Xb", "Xp"]
+    Xw = T.X[:, 0:4112]
+    nsent = 0
+
+    for t in range(RO):
+        Cu, nb = T["Cu%d" % t], T["nb%d" % t]
+        ck = ["Cu0_%d" % r for r in range(8)] if t == 0 else ["C%d" % t]
+        nn, nkey, mkey = nb[:, 0:128], "n%d" % t, "M%d" % t
+        pri[0] = PH; rnd[0] = t
+        X_E, R_E = (X_ON0, R_ON0) if t == 0 else (X_ON, R_ON)
+        ts(B[7][:, 0:256], T.Pi[:], 1184.0, None, A.add, None, 256, ["Pi"], ["pa"], [7])
+        ts(T.i2[:], T.Pi[:], 63, None, A.bitwise_and, None, 256, ["Pi"], ["pb", "i2"])
+        ts(B[7][:, 256:512], T.i2[:], 2048.0, 27648.0, A.mult, A.add, 256, ["i2"], ["pc"], [7])
+        ts(T.Cf[:], Cu[:], -2016.0, None, A.add, None, 256, ck, ["cm", "Cf"])
+        tt(T.i1[:], B[7][:, 0:256], T.Cf[:], A.mult, 256, ["pa", "Cf"], ["i1"], [7])
+        tt(T.i2[:], B[7][:, 256:512], T.i1[:], A.add, 256, ["pc", "i1"], ["ib", "i2"], [7])
+        ts(T.hh[:], T.i2[:], 5, 4095, A.arith_shift_right, A.bitwise_and, 256, ["i2"], ["hh"])
+        pri[0] = 0.0
+        act(T.Cf[:], T.Cf[:], F.Identity, 256, ["Cf"], ["Cf"], bias=2016.0)
+        mm([(B[6][0:64, 128 * h:128 * h + 128], nb[:, 64 * h:64 * h + 64], T.Id[:], True, True) for h in range(2)], 256, [nkey, "Id"], [], [6])
+        act(T.nT[:], B[6][0:64, 0:256], F.Identity, 256, [], ["nT"], [6], scale=-1.0)
+        for qn in range(4):
+            e, li = slice(1024 * qn, 1024 * qn + 1024), slice(64 * qn, 64 * qn + 64)
+            xk, dk, rk = "x%d" % qn, "d%d" % qn, "r%d" % qn
+            if X_E[qn] == "s": act(T.xg[:, e], Xw.indirect(T.Pu[:, li]), F.Copy, 1024 * GC, XK + pu[qn], [xk])
+            else: cp(T.xg[:, e], Xw.indirect(T.Pu[:, li]), 1024 * GC + 40, XK + pu[qn], [xk])
+            ym = R_E[qn] == "y"
+            tt(T.dg[:, e], Xw.indirect(Cu[:, li]), T.xg[:, e], A.max if ym else A.subtract, 1024 * GC + 40, XK + ck + [xk], [dk])
+            if ym: act(T.rg[:, e], Xw.indirect(Cu[:, li]), F.Copy, 1024 * GC, XK + ck, [rk])
+            elif R_E[qn] == "s": act(T.rg[:, e], T.dg[:, e], F.Relu, 1024, [dk], [rk])
+            else: ts(T.rg[:, e], T.dg[:, e], 0.0, None, A.max, None, 512, [dk], [rk])
+            bk = 4 + qn % 2
+            so = B[bk][:, 0:64]
+            terms = ((T.Sn, T.xg, xk), (T.Sn, T.rg, rk), (T.S2, T.dg, dk)) if ym else ((T.Sn, T.dg, dk), (T.S2, T.rg, rk))
+            gl = grp(so, [(a[:, 15 - s:143 - s], c[:, 1024 * qn + s:1024 * qn + 1024:16]) for a, c, k in terms for s in range(16)])
+            for j, (a, c, k) in enumerate(terms):
+                mm(gl[16 * j:16 * j + 16], 1024, [k, "Sn", "S2"], ["su%d%s" % (qn, "ab"[j == len(terms) - 1])], [bk])
+            pri[0] = PN
+            ts(T.nk[:, li], so, col(12), 4096.0, A.is_gt, A.mult, 64, ["thr"], ["nk%d" % qn], [bk])
+            tt(T.hp[:, li], T.hh[:, li], T.nk[:, li], A.max, 128, ["hh", "nk%d" % qn], ["hp%d" % qn])
+            cp(T.Hu[:, li], T.hp[:, li], 64, ["hp%d" % qn], ["Hu%d" % qn])
+            pri[0] = 0.0
+            act(T.zg[:, e], Xw.indirect(T.Hu[:, li]), F.Copy, 1024 * GC, XK + ["Hu%d" % qn], ["z%d" % qn])
+        nks, hps = ["nk%d" % i for i in range(4)], ["hp%d" % i for i in range(4)]
+        for h in range(2):
+            qa, qb = 2 * h, 2 * h + 1
+            for sb4 in range(4):
+                bk = MXB[h][sb4]; lst = []
+                for s in range(4 * sb4, 4 * sb4 + 4):
+                    st = slice(2048 * h + s, 2048 * h + 2048, 16)
+                    lst += grp(B[bk][:, 128 * (s % 4):128 * (s % 4) + 128],
+                               ([(T.Id[:], T.dg[:, st])] if R_E[qa] == "y" else [(T.Id[:], T.xg[:, st]), (T.Id[:], T.rg[:, st])])
+                               + [(T.Bm[:, 128 * s:128 * s + 128], T.nk[:, 128 * h:128 * h + 128])])
+                mm(lst, 128 * len(lst), ["Id", "Bm"] + ["%s%d" % (a, x) for a in ("x", "r", "d", "nk") for x in (qa, qb)], ["mx%d" % (4 * h + sb4)], [bk])
+                fs = [(lambda s=s, bk=bk, h=h: V.tensor_tensor(T.ll[:, 2048 * h + 128 * s:2048 * h + 128 * s + 128], B[bk][:, 128 * (s % 4):128 * (s % 4) + 128],
+                                                              T.zg[:, 2048 * h + s:2048 * h + 2048:16], A.min)) for s in range(4 * sb4, 4 * sb4 + 4)]
+                add("v", 4 * vc(128), ["z%d" % qa, "z%d" % qb], ["l%d" % (4 * h + sb4)], fs, [bk])
+            for c in range(2):
+                e = slice(2048 * h + 1024 * c, 2048 * h + 1024 * c + 1024)
+                scan(T.pm[:, e], T.ctl[:], T.ll[:, e], A.add, A.min, 512, ["ctl", "l%d" % (4 * h + 2 * c), "l%d" % (4 * h + 2 * c + 1)], ["pm%d" % (2 * h + c)])
+            for c in range(4):
+                i8 = 4 * h + c; bk = PMB[i8]; e = slice(512 * i8, 512 * i8 + 512)
+                gl = grp(B[bk][:], [(T.nT[:, 128 * h:128 * h + 128], T.nS[:, 512 * c:512 * c + 512]), (T.Id[:], T.pm[:, e])])
+                mm(gl[:1], 512, ["nT", "nS"], ["nn%d" % i8], [bk])
+                mm(gl[1:], 512, ["Id", "pm%d" % (i8 // 2)], ["pq%d" % i8], [bk])
+                act(T.ind[:, e], B[bk][:], F.Sign, 512, [], ["in%d" % i8], [bk], bias=0.5)
+                pri[0] = PC / 5
+                mm([(B[5][:, 256 + 128 * h + s:256 + 128 * h + 128:16], T.ind[:, 2048 * h + 128 * s:2048 * h + 128 * s + 128], T.G1[:], True, True)
+                    for s in range(4 * c, 4 * c + 4)], 256, ["in%d" % i8, "G1"], ["ct%d" % i8], [5])
+                pri[0] = 0.0
+            pri[0] = PC
+            ts(T.mK[:, 128 * h:128 * h + 128], B[5][:, 256 + 128 * h:256 + 128 * h + 128], 0.0, None, A.is_gt, None, 128, [], ["mK%d" % h], [5])
+            pri[0] = 0.0
+        lk, pmk = ["l%d" % i for i in range(8)] + ["lp"], ["pm%d" % i for i in range(4)] + ["pp"]
+        for j, (a0, a1) in enumerate(FCH):
+            e = slice(512 * a0, 512 * a1)
+            scan(T.zg[:, e], T.ct0[:, 0:512 * (a1 - a0)], T.ind[:, e], A.mult, A.add, 256 * (a1 - a0),
+                 ["cz"] + ["in%d" % i for i in range(a0, a1)], ["fs%d" % j, "z%d" % (a0 // 2)])
+        act(T.f1[:], T.zg[:, 0:4096].indirect(T.fpl[:]), F.Identity, 128 * GC, ["fpl"] + ["z%d" % i for i in range(4)], ["f1"], bias=17.0, scale=0.5)
+        act(T.nk2[:], T.nk[:], F.Identity, 256, nks, ["nkc"], bias=2912.0, scale=-1.0)
+        tt(B[7][:, 0:256], B[7][:, 0:256], T.nk2[:], A.add, 256, ["pa", "nkc"], ["tq"], [7])
+        tt(T.AA[:, 8:264], B[7][:, 0:256], T.hp[:], A.min, 256, hps + ["tq"], ["AA"], [7])
+        act(T.A3[:], T.AA[:], F.Identity, 272, ["AA", "A0", "Ap"], ["A3"], bias=12288.0)
+        act(T.A1[:], T.AA[:, 0:264], F.Identity, 264, ["AA", "A0"], ["A1"], bias=4096.0)
+        act(T.A2[:], T.AA[:, 0:264], F.Identity, 264, ["AA", "A0"], ["A2"], bias=8192.0)
+        KT = [T.KT1, T.KT2, T.KT3]; uu = [T.u1, T.u2, T.u3]
+
+        def offsets(c):
+            o = B[7][:, 32 * c:32 * c + 24]; rb = 0 if c == 0 else 24
+            lst = [(o, KT[c][0:33, 0:128], T.RA[:, 24 * c:24 * c + 24], True, False)]
+            if c == 1: lst.append((B[7][:, 32:48], T.KT1[0:8, 128:256], T.RB[:, 0:16], False, False))
+            lst.append((o, KT[c][0:8, 128:256], T.RB[:, rb:rb + 24], False, True))
+            pri[0] = PO if c == 0 else 0.0
+            mm(lst, 192, ["KT%d" % (c + 1), "K1%d" % (c + 1), "KT1"] + rak(c) + ["RB%d" % j for j in range(6)], ["of%d" % c], [7])
+            pri[0] = 0.0
+            ts(uu[c][:, 0:8], B[7][:, 32 * c:32 * c + 8], col(8 + c), 4096.0, A.add, A.min, 8, ["c%d" % (8 + c)], ["ul%d" % c], [7])
+            ts(uu[c][:, 8:16], B[7][:, 32 * c + 8:32 * c + 16], (8.0, 8199.0, 16390.0)[c], 264.0, A.add, A.min, 8, [], ["un%d" % c], [7])
+
+        def front(c, dst):
+            tt(T.gd[:], T.A3[:, 0:272].indirect(uu[c][:, 8:16]), T.dia[:], A.mult, 128 * GC + 40, ["A3", "un%d" % c, "dia"], ["gd"])
+            scan(dst[:], T.c16[:], T.gd[:], A.mult, A.add, 128, ["c16", "gd"], ["s%d" % min(c, 1)])
+
+        def cut(src, sk, c):
+            for hb in range(2):
+                lst = [(B[hb][:], T.TB[:], T.TR[:, 512 * hb:512 * hb + 512], True, False)]
+                lst += [(B[hb][:, 128 * j:128 * j + 128], T.Pm[:, 128 * (4 * hb + j):128 * (4 * hb + j) + 128], src, False, j == 3) for j in range(4)]
+                mm(lst[:1], 512, ["TB", "TR"], [], [hb])
+                mm(lst[1:], 512, ["Pm", sk], [], [hb])
+            ts(T.sg[:, 0:512], B[0][:], 0.0, 2.0, A.is_gt, A.mult, 512, [], ["sg0"], [0])
+            act(T.sg[:, 512:1024], B[1][:], F.Sign, 512, [], ["sg1"], [1])
+            prs = [(T.Id[:], T.ON[:, 0:128]), (T.I64[:], src)]
+            prs += [(T.Pm[:, 128 * (14 - j):128 * (15 - j)] if j < 7 else T.In[:], T.sg[:, 128 * j:128 * j + 128]) for j in range(8)]
+            gl = grp(B[5][:, 0:128], prs)
+            mm(gl[:2], 256, ["Id", "ON", "I64", sk], [], [5])
+            mm(gl[2:6], 512, ["Pm", "sg0"], [], [5])
+            mm(gl[6:], 512, ["Pm", "In", "sg1"], [], [5])
+            ts(T.qq[:], B[5][:, 0:128], -40.0 / 64, 35.0 / 64, A.max, A.min, 128, [], ["qq"], [5])
+            mm([(B[4][0:8, s:256:16], T.qq[:, s:128:16], T.G64[:], True, True) for s in range(16)], 16 * 24, ["qq", "G64a", "G64b"], [], [4])
+            ts(KT[c][0:8, :], B[4][0:8, 0:256], -8192.0 * c, None, A.max, None, 256, [], ["KT%d" % (c + 1)], [4])
+            offsets(c)
+
+        lst = grp(B[4][0:8, 0:128], [(T.L1[:, 4 - 4 * h:12 - 4 * h], T.mK[:, 128 * h:128 * h + 128]) for h in range(2)])
+        lst += grp(B[4][0:8, 128:256], [(T.LE[:, 4 - 4 * h:12 - 4 * h], T.mK[:, 128 * h:128 * h + 128]) for h in range(2)])
+        pri[0] = PK
+        mm(lst, 512, ["L1", "LE", "mK0", "mK1"], ["k1m"], [4])
+        pri[0] = 0.0
+        cp(T.KT1[0:8, :], B[4][0:8, 0:256], 256, [], ["KT1"], [4])
+        offsets(0)
+        ts(T.u1[:, 16:24], B[7][:, 16:24], col(1), None, A.add, None, 8, ["c1"], ["um"], [7])
+        lw = T.ll[:, 0:4112]
+        tt(T.bb[:], lw.indirect(T.u1[:, 0:8]), nn, A.is_ge, 128 * GC + 40, lk + ["ul0", nkey], ["bb"])
+        tt(T.f2[:], T.bb[:], T.f1[:], A.mult, 256, ["bb", "f1"], ["f2"])
+        act(T.e1[:], lw.indirect(T.u1[:, 0:8]), F.Copy, 128 * GC, lk + ["ul0"], ["e1"])
+        ts(B[6][:, 384:512], T.f2[:], 1.0, 33.0, A.add, A.min, 128, ["f2"], ["fa"], [6])
+        lst = grp(B[2][:, 0:256], [(T.KT1[0:33, 0:128], T.RUa[:]), (T.KT1[0:8, 128:256], T.RE[:])])
+        lst += grp(B[2][:, 256:512], [(T.KT1[0:33, 128:256], T.RX[:])])
+        mm(lst, 768, ["KT1", "K11", "RUa1", "RUa2", "RE", "RX1", "RX2"], [], [2])
+        tt(B[2][:, 0:256], B[2][:, 0:256], T.A1[:, 7:263], A.min, 256, ["A1"], ["t1"], [2])
+        tt(T.o1[:], B[2][:, 0:256], T.AA[:, 8:264], A.max, 256, ["AA", "t1"], ["o1"], [2])
+        tt(B[2][:, 256:512], B[2][:, 256:512], T.A1[:, 8:264], A.min, 256, ["A1"], ["te"], [2])
+        tt(T.EE[:], B[2][:, 256:512], T.Cf[:], A.max, 256, ["Cf", "te"], ["EE"], [2])
+        front(0, T.sa)
+        a12 = T.sa[:, 15:128:16]; b0 = T.sc[:, 15:128:16]
+        ts(T.fr[:, 0:8], a12, -12288.0, None, A.add, None, 8, ["s0"], ["fr0"])
+        if t < RO - 1:
+            add("v", vc(128), ["KT1"], ["th1"], [lambda: V.tensor_reduce(T.thf[:, 1:2], T.KT1[0:8, 128:256], AxisListType.X, A.add)])
+            mm(grp(B[6][:, 256:257], [(T.ONf[:], T.thf[:, 1:2])]), 256, ["ONf", "th1"], [], [6])
+            ts(T.ti[:, 0:1], B[6][:, 256:257], 1.0 / 8192, None, A.mult, None, 1, [], ["ti0"], [6])
+            ts(T.ti[:, 1:2], T.ti[:, 0:1], 63, None, A.bitwise_and, None, 1, ["ti0"], ["ti1"])
+            pri[0] = PT
+            tt(col(12), T.ti[:, 1:2], col(11), A.add, 1, ["ti1", "c11"], ["thr"])
+            pri[0] = 0.0
+        cut(T.f2[:], "f2", 1)
+        tt(T.bb[:], lw.indirect(T.u2[:, 0:8]), nn, A.is_ge, 128 * GC + 40, lk + ["ul1", nkey], ["bb"])
+        tt(T.f1[:], B[6][:, 384:512], T.bb[:], A.mult, 128, ["bb", "fa"], ["f1"], [6])
+        tt(T.fr[:, 8:16], B[7][:, 48:56], T.fr[:, 0:8], A.mult, 8, ["fr0"], ["fr1"], [7])
+        tt(T.e2[:], lw.indirect(T.u2[:, 0:8]), T.e1[:], A.min, 128 * GC + 40, lk + ["ul1", "e1"], ["e2"])
+        mm(grp(B[3][:, 0:256], [(T.KT2[0:33, 0:128], T.RUa[:]), (T.KT1[0:8, 128:256], T.RE[:])]), 512, ["KT1", "KT2", "K12", "RUa1", "RUa2", "RE"], [], [3])
+        tt(B[3][:, 0:256], B[3][:, 0:256], T.A2[:, 6:262], A.min, 256, ["A2"], ["t2"], [3])
+        tt(T.o2[:], B[3][:, 0:256], T.o1[:], A.max, 256, ["o1", "t2"], ["o2"], [3])
+        front(1, T.sc)
+        tt(T.fr[:, 16:24], T.fr[:, 8:16], b0, A.add, 16, ["fr1", "s1"], ["fr2"])
+        cut(T.f1[:], "f1", 2)
+        Mm = nb[:, 128:256]
+        tt(Mm, T.pm[:, 0:4112].indirect(T.u3[:, 0:8]), T.e2[:], A.min, 128 * GC + 40, pmk + ["ul2", "e2"], [mkey])
+        tt(T.fr[:, 24:32], B[7][:, 80:88], T.fr[:, 0:8], A.mult, 8, ["fr0"], ["fr3"], [7])
+        mm(grp(B[3][:, 256:512], [(T.KT1[0:8, 128:256], T.RE[:]), (T.KT2[0:8, 128:256], T.RF[:]), (T.KT3[0:33, 0:128], T.RUb[:])]), 768,
+           ["KT1", "KT2", "KT3", "K13", "RUb1", "RUb2", "RE", "RF"], [], [3])
+        front(2, T.sc)
+        tt(T.fr[:, 32:40], T.fr[:, 24:32], b0, A.add, 16, ["fr3", "s1"], ["fr4"])
+        tt(B[2][:, 0:256], B[3][:, 256:512], T.A3[:, 5:261], A.min, 256, ["A3"], ["t3"], [2, 3])
+        for j, (src, sk) in enumerate(((T.fr[:, 32:40], "fr4"), (T.fr[:, 16:24], "fr2"), (a12, "s0"))):
+            tt(B[2][:, j:256:32], B[3][:, 256 + j:512:32], src, A.min, 8, [sk, "t3"], ["t3%d" % j], [2, 3])
+        t3 = ["t3", "t30", "t31", "t32"]
+        tt(T.i3[:], B[2][:, 0:256], T.o2[:], A.max, 256, t3 + ["o2"], ["i3"], [2])
+        tt(T.i4[:], B[2][:, 0:256], T.EE[:], A.max, 256, t3 + ["EE"], ["i4"], [2])
+        ts(T.Ni[:], T.i3[:], 4095, None, A.bitwise_and, None, 256, ["i3"], ["Ni"])
+        cp(T["Nu%d" % t][:], T.Ni[:], 256, ["Ni"], ["Nu%d" % t])
+        ts(T.Pi[:], T.i4[:], 4095, None, A.bitwise_and, None, 256, ["i4"], ["Pi"])
+        if t < RO - 1: cp(T.Pu[:], T.Pi[:], 256, ["Pi"], allpu)
+        else: cp(T.pq[:], T.Pi[:], 256, ["Pi"], ["pq"])
+        mm(grp(B[7][:, 128:136], [(T.Sw[:, 15 - s:143 - s], nb[:, 128 + s:256:16]) for s in range(16)]), 1024, ["Sw", mkey], [], [7])
+        cp(T.si[:, 0:8], B[7][:, 128:136], 8, [], ["si0"], [7])
+        ts(T.si[:, 8:16], T.si[:, 0:8], 31, None, A.bitwise_and, None, 8, ["si0"], ["si1"])
+        tt(T.si[:, 16:24], T.si[:, 8:16], T.sb[:], A.add, 16, ["si1", "sb"], ["si2"])
+        cp(T.us[:], T.si[:, 16:24], 8, ["si2"], ["us"])
+        tt(T.v1[:], Mm, nn, A.add, 256, [mkey, nkey], ["v1"])
+        ts(T.v2[:], T.v1[:], 1, None, A.arith_shift_right, None, 128, ["v1"], ["v2"])
+        cp(T.X[:, 0:4096].indirect(T.us[:]), T.v2[:], 128 * 3.8, ["us", "v2"], ["Xa", "Xb"])
+        act(T["mo%d" % t][:], nb[:, 0:256].indirect(T.u1[:, 16:24]), F.Copy, 128 * GC, ["um", mkey, nkey], ["mo%d" % t])
+        dst = cores[(rank + 1 + t % 3) % len(cores)]
+        hlp = helper_of(topo, cores, core, dst); to = dst if hlp is None else hlp
+        rid, pid = topo.addr(to, core); mask = engines_mask(topo, core, to)
+        for src, sk, land, wk, sem in ((T["Nu%d" % t][:], "Nu%d" % t, T["Cu%d" % (t + 1)][:, 0:256], "C%d" % (t + 1), T.sem["ac%d" % t]),
+                                       (T["mo%d" % t][:], "mo%d" % t, T["nb%d" % (t + 1)][:, 0:128], "n%d" % (t + 1), T.sem["an%d" % t])):
+            j = add("g", 300, [sk], [], [lambda src=src, land=land, sem=sem, rid=rid, pid=pid, mask=mask: g.remote_dma(land, src, sem, T.sem.sent, pid, rid, mask)], rem=True)
+            add("x", 0, [], [wk], [], lat=LAT, sem=sem, val=NENG, after=[j])
+            nsent += NENG
+    for r in range(8):
+        act(T.op[:, r:256:8], T.pq[:, 32 * r:32 * r + 32], F.Identity, 32, ["pq"], ["op%d" % r])
+        cp(T.oc[:, r:256:8], T["Cu%d" % RO][:, 32 * r:32 * r + 32], 32, ["C%d" % RO], ["oc%d" % r])
+    mm(grp(B[6][:, 0:128], [(T.Id[:], T.X[:, k:4096:32]) for k in range(32)]), 4096, ["Id", "Xa", "Xb"], [], [6])
+    act(T.ox[:], B[6][:, 0:128], F.Identity, 128, [], ["ox"], [6])
+    dma("y", T.yp[:], T.op[:], ["op%d" % r for r in range(8)], [], 2500)
+    dma("s", T.yx[:], T.ox[:], ["ox"], [], 2500)
+    dma("y", T.yc[:], T.oc[:], ["oc%d" % r for r in range(8)], [], 2500)
+    dma("y", T.yn[:], T["nb%d" % RO][:, 0:128], ["n%d" % RO], [], 2500)
+    run(ops, g, T)
+    g.wait_ge(T.sem.sent, nsent)

@@ -13,11 +13,11 @@ SCRATCH = {
     "em": ("sbuf", [128, 128], I32), "eb": ("sbuf", [128, 128], BF),
     "ci": ("sbuf", [128, 8], I32), "cf": ("sbuf", [128, 24], F32),
     "Id": ("sbuf", [128, 128], BF), "I64": ("sbuf", [128, 128], BF), "In": ("sbuf", [128, 128], BF),
-    "S2": ("sbuf", [128, 144], BF), "Sn": ("sbuf", [128, 144], BF), "Sw": ("sbuf", [128, 144], BF),
+    "S2": ("sbuf", [128, 144], BF), "Sn": ("sbuf", [128, 288], BF), "Sw": ("sbuf", [128, 288], BF),
     "dia": ("sbuf", [128, 128], F32), "c16": ("sbuf", [128, 128], F32), "ctl": ("sbuf", [128, 1024], BF),
-    "G1": ("sbuf", [128, 8], BF), "G64": ("sbuf", [128, 16], BF), "L1": ("sbuf", [128, 12], BF), "LE": ("sbuf", [128, 12], BF),
-    "RA": ("sbuf", [33, 72], BF), "RB": ("sbuf", [8, 48], BF),
-    "RUa": ("sbuf", [33, 256], BF), "RUb": ("sbuf", [33, 256], BF), "RX": ("sbuf", [33, 256], BF),
+    "G1": ("sbuf", [128, 8], BF), "G64": ("sbuf", [128, 16], BF), "L1": ("sbuf", [128, 12], BF), "LE": ("sbuf", [128, 16], BF),
+    "RA": ("sbuf", [33, 72], BF), "RB": ("sbuf", [8, 56], BF),
+    "RUa": ("sbuf", [33, 256], BF), "RUb": ("sbuf", [1, 520], BF), "RX": ("sbuf", [33, 256], BF),
     "RE": ("sbuf", [8, 256], BF), "RF": ("sbuf", [8, 256], BF),
     "KT1": ("sbuf", [33, 256], BF), "KT2": ("sbuf", [33, 256], BF), "KT3": ("sbuf", [33, 256], BF),
     "ONf": ("sbuf", [8, 128], F32), "G8": ("sbuf", [8, 128], F32), "thf": ("sbuf", [8, 2], F32),
@@ -32,7 +32,7 @@ SCRATCH = {
     "ct0": ("sbuf", [128, 1024], BF), "f1": ("sbuf", [128, 128], BF), "f2": ("sbuf", [128, 128], BF), "fa": ("sbuf", [128, 128], BF),
     "bb": ("sbuf", [128, 128], BF), "sg": ("sbuf", [128, 1024], BF), "qq": ("sbuf", [128, 128], BF),
     "e1": ("sbuf", [128, 128], BF), "e2": ("sbuf", [128, 128], BF),
-    "u1": ("sbuf", [128, 24], U16), "u2": ("sbuf", [128, 16], U16), "u3": ("sbuf", [128, 16], U16), "us": ("sbuf", [128, 8], U16),
+    "u1": ("sbuf", [128, 24], U16), "u2": ("sbuf", [128, 16], U16), "u3": ("sbuf", [128, 16], U16), "us": ("sbuf", [128, 16], U16),
     "gd": ("sbuf", [128, 128], F32), "sa": ("sbuf", [128, 128], F32), "sc": ("sbuf", [128, 128], F32),
     "fr": ("sbuf", [128, 40], F32), "si": ("sbuf", [128, 24], I32), "v1": ("sbuf", [128, 128], I32), "v2": ("sbuf", [128, 128], I32),
     "ti": ("sbuf", [128, 2], I32), "op": ("sbuf", [128, 256], F32), "oc": ("sbuf", [128, 256], F32), "ox": ("sbuf", [128, 128], F32),
@@ -55,15 +55,35 @@ PH, PN = 0.0, 500.0
 MXB = ((0, 1, 2, 3), (0, 1, 2, 3))
 PK, PT, PO = 0.0, 4000.0, 500.0
 X_ON0, R_ON0 = "ssss", "vvsv"
-ORDER0 = {"v": "x0 x1 d0 r0 h d1 h2 nk0 r1 x2 d2 r2 nk1 x3 d3 r3 nk2 l0 l1 nk3 pm0 l2 l3 pm1 l4 l5 pm2 l6 l7 pm3 nkc tq AA",
+ORDER0 = {"v": "x0 x1 d0 r0 h d1 h2 nk0 r1 x2 d2 r2 nk1 x3 d3 r3 nk2 l0 l1 nk3 pm0 l2 l3 pm1 l4 l5 pm2 l6 l7 pm3 fs0 mK0 fs1 tq fs2 AA fs3",
           "s": "x0 x1 x2 r0 x3 r1 z0 r2 nT Cf z1 r3 z2 z3 in0 in1 in2 in3 in4 in5 in6 in7"}
 PMB, PC, LOOK = (6, 4, 6, 4, 0, 1, 2, 3), 1000.0, 0.7
 ORDER = {"v": "x0 x1 x2 x3 hp d0 h d1 h2 nk0 d2 nk1 d3 r3 nk2 l0 l1 nk3 pm0 l2 l3 pm1 l4 l5 pm2 l6 l7 pm3 fs0 fs1 tq AA",
          "s": "x0 x1 x2 x3 r0 nT Cf r1 z0 r2 z1 r3 z2 z3 in0 in1 in2 in3 in4 in5 in6 in7"}
 ORDER["p"] = ORDER0["p"] = ("su2a mx0 su2b mx1 su3a su3b mx2 mx3 nn0 nn1 mx4 mx5 pq0 pq1 mx6 nn2 pq2 mx7 nn3 pq3 "
-                            "nn4 pq4 nn5 pq5 nn6 nn7 pq6 pq7 ct0 ct1 ct2 ct3 ct4 ct5 ct6 ct7 k1m of0")
+                            "nn4 pq4 nn5 pq5 ct0 ct1 nn6 ct2 nn7 ct3 pq6 pq7 ct4 ct5 ct6 ct7 TB@0#0 k1d k1m TB@1#0 of0")
 FCH = ((0, 2), (2, 4), (4, 6), (6, 7), (7, 8))
-HOP, LAT, GC = 120.0, 5000.0, 1.56
+KT_ON, GATE = "ssv", "v"
+TAIL = {"v": "mK1 ul0 bb#0 f2 un0 um gd#0 sg1#0 s0 fr0 t1 qq#0 o1 ud bb#1 f1 ul1 un1 gd#1 fr1 sg1#1 s1#0 fr2 t2 qq#1 o2 KT3 e2 "
+             "ul2 un2 t3 gd#2 t31 t32 s1#1 i3 fr3 Ni fr4 Nu%#0 Nu%#1 M% te v1 EE si0 t30 si1 i4 si2 v2 us Pi Xa Pu0a ti0 ti1 thr",
+        "s": "A1 A3 f1 KT1 fb sg0#0 fa A2 e1 KT2 f2 sg0#1 th1 mo%",
+        "p": "KT1@2 Pm@0#0 Pm@1#0 Id@5#0 K11@7#1 K11@4#0 Pm@5#0 Pm@5#1 TB@0#1 S64@7 qq@4#0 TB@1#1 of1 KT1@3#0 Pm@0#1 Pm@1#1 "
+             "K11@4#1 Id@5#1 Pm@5#2 Pm@5#3 qq@4#1 KT1@3#1 of2 KT3@3 KT1@6 Sw@7 ONf@6"}
+R_ON, X_ON = "spsv", "svsv"
+ORDER = {"v": "hp x3 x1 d0 d2 h h2 nk0 nk1 d3 r3 nk2 l0 l1 nk3 pm0 l3 l2 pm1 l5 l7 l4 l6 pm2 pm3 tq fs0 fs1 mK0 fs2 fs3 AA",
+         "s": "x0 x2 d1 r0 r1 r2 nT z0 z1 z2 Cf z3 in1 in0 nkc in2 in3 in5 in4 in6 in7",
+         "p": "su0a su0b su1a su1b su2a su2b nn0 mx1 mx0 su3a nn1 su3b mx3 mx2 mx5 pq1 pq0 mx7 mx4 mx6 nn2 pq2 ct0 nn3 nn5 pq3 nn4 pq5 ct1 pq4 "
+              "nn6 ct2 pq6 ct3 nn7 pq7 ct4 ct5 ct6 ct7 TB@0#0 k1d k1m TB@1#0 of0"}
+ORDER0 = {"v": "h d0 h2 r0 d1 nk0 r1 d2 nk1 d3 nk2 r3 l1 l0 nk3 pm0 l3 l2 pm1 l5 l4 pm2 l7 l6 pm3 fs1 tq fs0 mK0 AA fs2 fs3",
+          "s": "x0 nT x1 x3 x2 z0 r2 z1 z2 Cf z3 in0 in1 in2 in3 in4 in5 in6 in7",
+          "p": "su0a su0b su1a su1b su2a mx1 su2b mx2 su3a mx0 su3b nn0 nn1 mx3 mx5 mx4 pq0 mx7 pq1 nn2 nn5 pq2 ct0 mx6 nn3 pq3 nn4 pq4 pq5 ct1 ct2 "
+               "nn6 pq6 ct3 nn7 pq7 ct4 ct5 ct6 TB@1#0 ct7 TB@0#0 k1d k1m of0"}
+TAIL = {"v": "mK1 ul0 bb#0 f2 un0 um gd#0 sg1#0 t1 qq#0 s0 fr0 ud bb#1 f1 ul1 un1 o1 sg1#1 t2 gd#1 qq#1 s1#0 fr1 o2 KT3 fr2 e2 ul2 un2 t3 gd#2 "
+             "t31 t32 s1#1 i3 fr3 Ni fr4 Nu%#0 M% Nu%#1 te v1 EE si0 t30 si1 i4 si2 ti0 Pi us v2 Xa Pu0a ti1 thr",
+        "s": "A3 A1 f1 KT1 e1 sg0#0 th1 A2 fb fa KT2 f2 sg0#1 mo%",
+        "p": "Pm@0#0 Pm@1#0 KT1@2 Id@5#0 K11@7#1 Pm@5#0 Pm@5#1 K11@4#0 S64@7 qq@4#0 TB@1#1 TB@0#1 K11@4#1 of1 Pm@0#1 Pm@1#1 KT1@3#0 Id@5#1 "
+             "Pm@5#2 Pm@5#3 qq@4#1 KT1@6 KT1@3#1 of2 KT3@3 Sw@7 ONf@6"}
+HOP, LAT, GC = 130.0, 5600.0, 1.56
 
 
 def engines_mask(topo, src, dst):
@@ -129,7 +149,10 @@ def run(ops, g, T):
     for i, o in enumerate(ops): tags.setdefault((o["tag"], o["e"]), []).append(i)
     for t in range(RO):
         for e, names in (ORDER0 if t == 0 else ORDER).items():
-            seq = [i for nm in names.split() for i in tags.get(((t, nm), e), [])]
+            seq = []
+            for nm in (names + " " + TAIL[e]).replace("%", str(t)).split():
+                nm, _, k = nm.partition("#"); found = tags.get(((t, nm), e), [])
+                seq += found[int(k):int(k) + 1] if k else found
             for j, i in zip(seq, seq[1:]): pre[i].setdefault(j, False)
     suc = [[] for _ in range(n)]
     for i in range(n):
@@ -158,6 +181,8 @@ def run(ops, g, T):
         for j in suc[i]:
             rdy[j] = max(rdy[j], fin[i] + (HOP if pre[j][i] else 0.0)); left[j] -= 1
             if left[j] == 0: ready.append(j)
+    if g is None:
+        return max(fin)
     pos, cnt = {}, {}
     for i in order:
         e = ops[i]["e"]; cnt[e] = cnt.get(e, 0) + 1; pos[i] = cnt[e]
@@ -215,7 +240,7 @@ def rank_program(g, core, T, topo):
 
     def add(e, c, r, w, fs, b=(), lat=0.0, sem=None, val=0, after=(), rem=False):
         ops.append({"e": e, "c": float(c), "r": list(r), "w": list(w), "f": fs, "b": list(b), "lat": lat, "sem": sem, "val": val, "after": list(after),
-                    "pri": pri[0], "rem": rem, "tag": (rnd[0], tag_of(w, e))})
+                    "pri": pri[0], "rem": rem, "tag": (rnd[0], tag_of(w, e) if len(w) or not len(b) else "%s@%d" % (r[0], b[0]))})
         return len(ops) - 1
 
     def vc(n): return 20 + 0.83 * max(64, n)
@@ -280,7 +305,7 @@ def rank_program(g, core, T, topo):
     cp(col(4), T.wi[:], 1, ["wi"], ["c4"])
     ts(col(5), ci[:, 2:3], 4.0, None, A.add, None, 1, ["ci2"], ["c5"])
     ts(col(6), ci[:, 3:4], 31.0, 8192.0, A.is_equal, A.mult, 1, ["ci3"], ["c6"])
-    for j, off in ((8, 0.0), (9, 8191.0), (10, 16382.0)):
+    for j, off in ((7, -1.0), (8, 0.0), (9, -1.0), (10, -2.0)):
         ts(col(j), col(1), 128.0, off, A.mult, A.add, 1, ["c1"], ["c%d" % j])
     ts(col(13), col(1), 32.0, None, A.mult, None, 1, ["c1"], ["c13"])
     ts(T.sb[:], T.sb[:], col(13), None, A.add, None, 8, ["sb", "c13"], ["sb"])
@@ -289,8 +314,10 @@ def rank_program(g, core, T, topo):
     ts(T.I64[:], T.Id[:], 1.0 / 64, None, A.mult, None, 64, ["Id"], ["I64"])
     ts(T.In[:], T.Id[:], -1.0, None, A.mult, None, 64, ["Id"], ["In"])
     ts(T.S2[:], T.jo[:], col(3), 2.0, A.is_equal, A.mult, 144, ["jo", "c3"], ["S2"])
-    ts(T.Sn[:], T.S2[:], -0.5, None, A.mult, None, 72, ["S2"], ["Sn"])
-    ts(T.Sw[:], T.S2[:], 0.5, col(4), A.mult, A.mult, 72, ["S2", "c4"], ["Sw"])
+    ts(T.Sn[:, 0:144], T.S2[:], -0.5, None, A.mult, None, 72, ["S2"], ["Sn"])
+    ts(T.Sn[:, 144:288], T.S2[:], 0.5, None, A.mult, None, 72, ["S2"], ["S1"])
+    ts(T.Sw[:, 0:144], T.S2[:], 0.5, col(4), A.mult, A.mult, 72, ["S2", "c4"], ["Sw"])
+    ts(T.Sw[:, 144:288], T.S2[:], 32.0, None, A.mult, None, 72, ["S2"], ["S64"])
     ts(T.dia[:], T.j16[:], col(1), None, A.is_equal, None, 128, ["j16", "c1"], ["dia"])
     ts(T.c16[:], T.j16[:], 0.0, None, A.is_gt, None, 128, ["j16"], ["c16"])
     ms(T.ctl[:], 0.0, 512, ["ctl"])
@@ -299,10 +326,13 @@ def rank_program(g, core, T, topo):
     ts(T.G64[:, 0:8], T.G1[:], 64.0, None, A.mult, None, 8, ["G1"], ["G64a"])
     ts(T.G64[:, 8:16], T.G1[:], -64.0 * 8192, None, A.mult, None, 8, ["G1"], ["G64b"])
     ts(T.L1[:], T.jo[:, 0:12], col(5), None, A.is_equal, None, 12, ["jo", "c5"], ["L1"])
-    ts(T.LE[:], T.L1[:], col(6), None, A.mult, None, 12, ["L1", "c6"], ["LE"])
+    ts(T.LE[:, 0:12], T.L1[:], col(6), None, A.mult, None, 12, ["L1", "c6"], ["LE"])
+    tt(T.LE[:, 12:16], T.LE[:, 4:8], T.L1[:, 4:8], A.max, 8, ["L1", "LE"], ["LD"])
+    ts(T.RB[:, 48:56], T.Id[0:8, 0:8], -31.0 / 8192, None, A.mult, None, 8, ["Id"], ["RB6"])
     ts(T.v1[:], T.em[:], 15, None, A.bitwise_and, None, 128, ["em"], ["v1"])
     ts(T.jb[:], T.jb[:], col(2), 16.0, A.not_equal, A.mult, 128, ["jb", "c2"], ["jb"])
     tt(T.eb[:], T.v1[:], T.jb[:], A.add, 256, ["v1", "jb"], ["eb"])
+    if GATE != "v": cp(T.jb[:], T.Id[:], 128, ["Id"], ["jb"])
     for u in range(1, 16):
         ts(T.Pm[:, 128 * (u - 1):128 * u], T.eb[:], float(u), None, A.is_equal, None, 64, ["eb"], ["Pm%d" % u])
     pk = ["Pm%d" % u for u in range(1, 16)]
@@ -314,15 +344,16 @@ def rank_program(g, core, T, topo):
             cp(T.RA[0:8, 24 * c + 8 * h:24 * c + 8 * h + 8], oh, 8, ["Id", "RA"], ["RA%d%d" % (c, h)])
         iota(T.RA[32:33, 24 * c:24 * c + 8], [[2048, 2], [32, 4]], 0, 0, 8, ["RAx%d" % c], r=["RA"])
         iota(T.RA[32:33, 24 * c + 8:24 * c + 16], [[32, 8]], 0, 0, 8, ["RAy%d" % c], r=["RA"])
-        iota(T.RA[32:33, 24 * c + 16:24 * c + 24], [[16 if c == 0 else 0, 8]], 128 if c == 0 else c, 0, 8, ["RAz%d" % c], r=["RA"])
+        iota(T.RA[32:33, 24 * c + 16:24 * c + 24], [[16 if c == 0 else 0, 8]], 128 if c == 0 else 0, 0, 8, ["RAz%d" % c], r=["RA"])
     def rak(c): return ["RA%d0" % c, "RA%d1" % c, "RAx%d" % c, "RAy%d" % c, "RAz%d" % c]
     for j, sc in enumerate((1.0, 1.0, -1.0 / 64, 1.0, 1.0, 1.0 / 8192)):
         ts(T.RB[:, 8 * j:8 * j + 8], oh, sc, None, A.mult, None, 8, ["Id"], ["RB%d" % j])
-    for nm, sc in (("RUa", 32768.0), ("RUb", 32768.0), ("RX", 4.0)):
+    for nm, sc in (("RUa", 32768.0), ("RX", 4.0)):
         ms(T[nm][:], 0.0, 128, [nm + "0"])
         ts(T[nm][0:8, :], T.OH[:], sc, None, A.mult, None, 128, ["OH", nm + "0"], [nm + "1"])
     iota(T.RUa[32:33, :], [[0, 8], [-32768, 32]], 16384, 0, 256, ["RUa2"], r=["RUa0"])
-    iota(T.RUb[32:33, :], [[0, 8], [-32768, 32]], -16384, 0, 256, ["RUb2"], r=["RUb0"])
+    for c in (1, 2): iota(T.RUb[0:1, 256 * c - 256:256 * c], [[8192 * c, 2], [0, 128]], 0, 0, 256, ["RUb%d" % c])
+    iota(T.RUb[0:1, 512:520], [[2048, 2], [32, 4]], 0, 0, 8, ["RUb0"])
     iota(T.RX[32:33, :], [[0, 256]], -16384, 0, 256, ["RX2"], r=["RX0"])
     ts(T.RE[:], T.OH[:], -256.0, None, A.mult, None, 128, ["OH"], ["RE"])
     ts(T.RF[:], T.OH[:], -4.0, None, A.mult, None, 128, ["OH"], ["RF"])
@@ -371,16 +402,26 @@ def rank_program(g, core, T, topo):
             if X_E[qn] == "s": act(T.xg[:, e], Xw.indirect(T.Pu[:, li]), F.Copy, 1024 * GC, XK + pu[qn], [xk])
             else: cp(T.xg[:, e], Xw.indirect(T.Pu[:, li]), 1024 * GC + 40, XK + pu[qn], [xk])
             ym = R_E[qn] == "y"
-            tt(T.dg[:, e], Xw.indirect(Cu[:, li]), T.xg[:, e], A.max if ym else A.subtract, 1024 * GC + 40, XK + ck + [xk], [dk])
-            if ym: act(T.rg[:, e], Xw.indirect(Cu[:, li]), F.Copy, 1024 * GC, XK + ck, [rk])
+            pm_ = R_E[qn] == "p"
+            if pm_: act(T.dg[:, e], Xw.indirect(Cu[:, li]), F.Copy, 1024 * GC, XK + ck, [dk])
+            else: tt(T.dg[:, e], Xw.indirect(Cu[:, li]), T.xg[:, e], A.max if ym else A.subtract, 1024 * GC + 40, XK + ck + [xk], [dk])
+            if pm_:
+                for j in range(2):
+                    e2 = slice(1024 * qn + 512 * j, 1024 * qn + 512 * j + 512)
+                    mm([(B[j][:], T.In[:], T.xg[:, e2], True, False)], 512, ["In", xk], [], [j])
+                    mm([(B[j][:], T.Id[:], T.dg[:, e2], False, True)], 512, ["Id", dk], [], [j])
+                    act(T.rg[:, e2], B[j][:], F.Relu, 512, [], [rk], [j])
+            elif ym: act(T.rg[:, e], Xw.indirect(Cu[:, li]), F.Copy, 1024 * GC, XK + ck, [rk])
             elif R_E[qn] == "s": act(T.rg[:, e], T.dg[:, e], F.Relu, 1024, [dk], [rk])
             else: ts(T.rg[:, e], T.dg[:, e], 0.0, None, A.max, None, 512, [dk], [rk])
             bk = 4 + qn % 2
             so = B[bk][:, 0:64]
             terms = ((T.Sn, T.xg, xk), (T.Sn, T.rg, rk), (T.S2, T.dg, dk)) if ym else ((T.Sn, T.dg, dk), (T.S2, T.rg, rk))
-            gl = grp(so, [(a[:, 15 - s:143 - s], c[:, 1024 * qn + s:1024 * qn + 1024:16]) for a, c, k in terms for s in range(16)])
+            if pm_: terms = ((None, T.xg, xk),) + terms
+            gl = grp(so, [(T.Sn[:, 159 - s:287 - s] if a is None else a[:, 15 - s:143 - s], c[:, 1024 * qn + s:1024 * qn + 1024:16])
+                          for a, c, k in terms for s in range(16)])
             for j, (a, c, k) in enumerate(terms):
-                mm(gl[16 * j:16 * j + 16], 1024, [k, "Sn", "S2"], ["su%d%s" % (qn, "ab"[j == len(terms) - 1])], [bk])
+                mm(gl[16 * j:16 * j + 16], 1024, [k, "Sn", "S2", "S1"], ["su%d%s" % (qn, "ab"[j == len(terms) - 1])], [bk])
             pri[0] = PN
             ts(T.nk[:, li], so, col(12), 4096.0, A.is_gt, A.mult, 64, ["thr"], ["nk%d" % qn], [bk])
             tt(T.hp[:, li], T.hh[:, li], T.nk[:, li], A.max, 128, ["hh", "nk%d" % qn], ["hp%d" % qn])
@@ -435,12 +476,13 @@ def rank_program(g, core, T, topo):
             o = B[7][:, 32 * c:32 * c + 24]; rb = 0 if c == 0 else 24
             lst = [(o, KT[c][0:33, 0:128], T.RA[:, 24 * c:24 * c + 24], True, False)]
             if c == 1: lst.append((B[7][:, 32:48], T.KT1[0:8, 128:256], T.RB[:, 0:16], False, False))
+            if c == 2: lst.append((B[7][:, 72:80], T.KT1[0:8, 128:256], T.RB[:, 48:56], False, False))
             lst.append((o, KT[c][0:8, 128:256], T.RB[:, rb:rb + 24], False, True))
             pri[0] = PO if c == 0 else 0.0
-            mm(lst, 192, ["KT%d" % (c + 1), "K1%d" % (c + 1), "KT1"] + rak(c) + ["RB%d" % j for j in range(6)], ["of%d" % c], [7])
+            mm(lst, 192, ["KT%d" % (c + 1), "K1%d" % (c + 1), "KT1"] + rak(c) + ["RB%d" % j for j in range(7)], ["of%d" % c], [7])
             pri[0] = 0.0
-            ts(uu[c][:, 0:8], B[7][:, 32 * c:32 * c + 8], col(8 + c), 4096.0, A.add, A.min, 8, ["c%d" % (8 + c)], ["ul%d" % c], [7])
-            ts(uu[c][:, 8:16], B[7][:, 32 * c + 8:32 * c + 16], (8.0, 8199.0, 16390.0)[c], 264.0, A.add, A.min, 8, [], ["un%d" % c], [7])
+            if c: ts(uu[c][:, 0:8], B[7][:, 32 * c:32 * c + 8], col(8 + c), 4096.0, A.add, A.min, 8, ["c%d" % (8 + c)], ["ul%d" % c], [7])
+            ts(uu[c][:, 8:16], B[7][:, 32 * c + 8:32 * c + 16], (8.0, 7.0, 6.0)[c], 264.0, A.add, A.min, 8, [], ["un%d" % c], [7])
 
         def front(c, dst):
             tt(T.gd[:], T.A3[:, 0:272].indirect(uu[c][:, 8:16]), T.dia[:], A.mult, 128 * GC + 40, ["A3", "un%d" % c, "dia"], ["gd"])
@@ -452,57 +494,71 @@ def rank_program(g, core, T, topo):
                 lst += [(B[hb][:, 128 * j:128 * j + 128], T.Pm[:, 128 * (4 * hb + j):128 * (4 * hb + j) + 128], src, False, j == 3) for j in range(4)]
                 mm(lst[:1], 512, ["TB", "TR"], [], [hb])
                 mm(lst[1:], 512, ["Pm", sk], [], [hb])
-            ts(T.sg[:, 0:512], B[0][:], 0.0, 2.0, A.is_gt, A.mult, 512, [], ["sg0"], [0])
-            act(T.sg[:, 512:1024], B[1][:], F.Sign, 512, [], ["sg1"], [1])
-            prs = [(T.Id[:], T.ON[:, 0:128]), (T.I64[:], src)]
+            prs = [(T.Id[:], T.ON[:, 0:128])]
+            if c == 2:
+                act(T.f2[:], src, F.Relu, 128, [sk], ["f2"], bias=-1.0); src, sk = T.f2[:], "f2"
+                prs.append((T.I64[:], T.ON[:, 0:128]))
+            act(T.sg[:, 0:512], B[0][:], F.Sign, 512, [], ["sg0"], [0])
+            ts(T.sg[:, 512:1024], B[1][:], 0.0, 2.0, A.is_gt, A.mult, 512, [], ["sg1"], [1])
+            prs.append((T.Id[:], T.ON[:, 0:128]))
+            prs.append((T.I64[:], src))
             prs += [(T.Pm[:, 128 * (14 - j):128 * (15 - j)] if j < 7 else T.In[:], T.sg[:, 128 * j:128 * j + 128]) for j in range(8)]
             gl = grp(B[5][:, 0:128], prs)
-            mm(gl[:2], 256, ["Id", "ON", "I64", sk], [], [5])
-            mm(gl[2:6], 512, ["Pm", "sg0"], [], [5])
-            mm(gl[6:], 512, ["Pm", "In", "sg1"], [], [5])
+            mm(gl[:-8], 384, ["Id", "ON", "I64", sk], [], [5])
+            mm(gl[-8:-4], 512, ["Pm", "sg0"], [], [5])
+            mm(gl[-4:], 512, ["Pm", "In", "sg1"], [], [5])
             ts(T.qq[:], B[5][:, 0:128], -40.0 / 64, 35.0 / 64, A.max, A.min, 128, [], ["qq"], [5])
-            mm([(B[4][0:8, s:256:16], T.qq[:, s:128:16], T.G64[:], True, True) for s in range(16)], 16 * 24, ["qq", "G64a", "G64b"], [], [4])
-            ts(KT[c][0:8, :], B[4][0:8, 0:256], -8192.0 * c, None, A.max, None, 256, [], ["KT%d" % (c + 1)], [4])
+            if c == 1:
+                gl = grp(B[7][:, 104:112], [(T.ON[0:1, 0:128], T.RUb[0:1, 512:520]), (T.KT1[0:8, 128:256], T.RB[:, 0:8])]
+                         + [(T.Sw[:, 159 - s:287 - s], T.qq[:, s:128:16]) for s in range(16)])
+                mm(gl[:2], 128, ["K11", "ON", "RUb0", "KT1", "RB0"], [], [7])
+                mm(gl[2:], 1024, ["S64", "qq"], [], [7])
+                ts(T.us[:, 8:16], B[7][:, 104:112], col(7), 4096.0, A.add, A.min, 8, ["c7"], ["ud"], [7])
+            mm([(B[4][0:8, 0:256], T.ON[0:1, 0:8], T.RUb[0:1, 256 * c - 256:256 * c], True, False)], 256, ["K11", "ON", "RUb%d" % c], [], [4])
+            mm([(B[4][0:8, s:256:16], T.qq[:, s:128:16], T.G64[:], False, s == 15) for s in range(16)], 16 * 24, ["qq", "G64a", "G64b"], [], [4])
+            if KT_ON[c] == "s": act(KT[c][0:8, :], B[4][0:8, 0:256], F.Relu, 256, [], ["KT%d" % (c + 1)], [4])
+            else: ts(KT[c][0:8, :], B[4][0:8, 0:256], 0.0, None, A.max, None, 256, [], ["KT%d" % (c + 1)], [4])
             offsets(c)
 
         lst = grp(B[4][0:8, 0:128], [(T.L1[:, 4 - 4 * h:12 - 4 * h], T.mK[:, 128 * h:128 * h + 128]) for h in range(2)])
         lst += grp(B[4][0:8, 128:256], [(T.LE[:, 4 - 4 * h:12 - 4 * h], T.mK[:, 128 * h:128 * h + 128]) for h in range(2)])
+        mm([(B[7][:, 96:104], T.ON[0:1, 0:128], T.RUb[0:1, 512:520], True, False), (B[7][:, 96:100], T.mK[:, 0:128], T.LE[:, 12:16], False, False)],
+           128, ["K11", "ON", "RUb0", "LD", "mK0"], [], [7])
+        mm([(B[7][:, 100:104], T.mK[:, 128:256], T.LE[:, 12:16], False, True)], 64, ["LD", "mK1"], ["k1d"], [7])
+        ts(T.u1[:, 0:8], B[7][:, 96:104], col(8), 4096.0, A.add, A.min, 8, ["c8"], ["ul0"], [7])
         pri[0] = PK
         mm(lst, 512, ["L1", "LE", "mK0", "mK1"], ["k1m"], [4])
         pri[0] = 0.0
-        cp(T.KT1[0:8, :], B[4][0:8, 0:256], 256, [], ["KT1"], [4])
+        act(T.KT1[0:8, :], B[4][0:8, 0:256], F.Identity, 256, [], ["KT1"], [4])
         offsets(0)
         ts(T.u1[:, 16:24], B[7][:, 16:24], col(1), None, A.add, None, 8, ["c1"], ["um"], [7])
         lw = T.ll[:, 0:4112]
         tt(T.bb[:], lw.indirect(T.u1[:, 0:8]), nn, A.is_ge, 128 * GC + 40, lk + ["ul0", nkey], ["bb"])
         tt(T.f2[:], T.bb[:], T.f1[:], A.mult, 256, ["bb", "f1"], ["f2"])
         act(T.e1[:], lw.indirect(T.u1[:, 0:8]), F.Copy, 128 * GC, lk + ["ul0"], ["e1"])
-        ts(B[6][:, 384:512], T.f2[:], 1.0, 33.0, A.add, A.min, 128, ["f2"], ["fa"], [6])
+        act(T.fa[:], T.f2[:], F.Relu, 128, ["f2"], ["fb"], bias=32.0, scale=-1.0)
+        act(B[6][:, 384:512], T.fa[:], F.Identity, 128, ["fb"], ["fa"], [6], bias=33.0, scale=-1.0)
         lst = grp(B[2][:, 0:256], [(T.KT1[0:33, 0:128], T.RUa[:]), (T.KT1[0:8, 128:256], T.RE[:])])
-        lst += grp(B[2][:, 256:512], [(T.KT1[0:33, 128:256], T.RX[:])])
-        mm(lst, 768, ["KT1", "K11", "RUa1", "RUa2", "RE", "RX1", "RX2"], [], [2])
-        tt(B[2][:, 0:256], B[2][:, 0:256], T.A1[:, 7:263], A.min, 256, ["A1"], ["t1"], [2])
+        mm(lst, 512, ["KT1", "K11", "RUa1", "RUa2", "RE"], [], [2])
+
+        def gate(reg, bk, src, sk, pen, pk, key):
+            if GATE == "v":
+                tt(reg, reg, src, A.min, 256, [sk], [key], [bk])
+            else:
+                act(pen, reg, F.Relu, 256, [], [pk], [bk], scale=-1.0)
+                mm(grp(reg, [(T.jb[:], src), (T.In[:], pen)]), 1280, [sk, pk, "jb", "In"], [key], [bk])
+        gate(B[2][:, 0:256], 2, T.A1[:, 7:263], "A1", T.nk2[:], "nkc", "t1")
         tt(T.o1[:], B[2][:, 0:256], T.AA[:, 8:264], A.max, 256, ["AA", "t1"], ["o1"], [2])
-        tt(B[2][:, 256:512], B[2][:, 256:512], T.A1[:, 8:264], A.min, 256, ["A1"], ["te"], [2])
-        tt(T.EE[:], B[2][:, 256:512], T.Cf[:], A.max, 256, ["Cf", "te"], ["EE"], [2])
         front(0, T.sa)
         a12 = T.sa[:, 15:128:16]; b0 = T.sc[:, 15:128:16]
         ts(T.fr[:, 0:8], a12, -12288.0, None, A.add, None, 8, ["s0"], ["fr0"])
-        if t < RO - 1:
-            add("v", vc(128), ["KT1"], ["th1"], [lambda: V.tensor_reduce(T.thf[:, 1:2], T.KT1[0:8, 128:256], AxisListType.X, A.add)])
-            mm(grp(B[6][:, 256:257], [(T.ONf[:], T.thf[:, 1:2])]), 256, ["ONf", "th1"], [], [6])
-            ts(T.ti[:, 0:1], B[6][:, 256:257], 1.0 / 8192, None, A.mult, None, 1, [], ["ti0"], [6])
-            ts(T.ti[:, 1:2], T.ti[:, 0:1], 63, None, A.bitwise_and, None, 1, ["ti0"], ["ti1"])
-            pri[0] = PT
-            tt(col(12), T.ti[:, 1:2], col(11), A.add, 1, ["ti1", "c11"], ["thr"])
-            pri[0] = 0.0
         cut(T.f2[:], "f2", 1)
-        tt(T.bb[:], lw.indirect(T.u2[:, 0:8]), nn, A.is_ge, 128 * GC + 40, lk + ["ul1", nkey], ["bb"])
+        tt(T.bb[:], lw.indirect(T.us[:, 8:16]), nn, A.is_ge, 128 * GC + 40, lk + ["ud", nkey], ["bb"])
         tt(T.f1[:], B[6][:, 384:512], T.bb[:], A.mult, 128, ["bb", "fa"], ["f1"], [6])
         tt(T.fr[:, 8:16], B[7][:, 48:56], T.fr[:, 0:8], A.mult, 8, ["fr0"], ["fr1"], [7])
         tt(T.e2[:], lw.indirect(T.u2[:, 0:8]), T.e1[:], A.min, 128 * GC + 40, lk + ["ul1", "e1"], ["e2"])
         mm(grp(B[3][:, 0:256], [(T.KT2[0:33, 0:128], T.RUa[:]), (T.KT1[0:8, 128:256], T.RE[:])]), 512, ["KT1", "KT2", "K12", "RUa1", "RUa2", "RE"], [], [3])
-        tt(B[3][:, 0:256], B[3][:, 0:256], T.A2[:, 6:262], A.min, 256, ["A2"], ["t2"], [3])
+        gate(B[3][:, 0:256], 3, T.A2[:, 6:262], "A2", T.nk2[:], "nkc", "t2")
         tt(T.o2[:], B[3][:, 0:256], T.o1[:], A.max, 256, ["o1", "t2"], ["o2"], [3])
         front(1, T.sc)
         tt(T.fr[:, 16:24], T.fr[:, 8:16], b0, A.add, 16, ["fr1", "s1"], ["fr2"])
@@ -510,18 +566,30 @@ def rank_program(g, core, T, topo):
         Mm = nb[:, 128:256]
         tt(Mm, T.pm[:, 0:4112].indirect(T.u3[:, 0:8]), T.e2[:], A.min, 128 * GC + 40, pmk + ["ul2", "e2"], [mkey])
         tt(T.fr[:, 24:32], B[7][:, 80:88], T.fr[:, 0:8], A.mult, 8, ["fr0"], ["fr3"], [7])
-        mm(grp(B[3][:, 256:512], [(T.KT1[0:8, 128:256], T.RE[:]), (T.KT2[0:8, 128:256], T.RF[:]), (T.KT3[0:33, 0:128], T.RUb[:])]), 768,
-           ["KT1", "KT2", "KT3", "K13", "RUb1", "RUb2", "RE", "RF"], [], [3])
+        gl = grp(B[3][:, 256:512], [(T.KT1[0:8, 128:256], T.RE[:]), (T.KT2[0:8, 128:256], T.RF[:]), (T.KT3[0:33, 0:128], T.RUa[:])])
+        mm(gl[:2], 512, ["KT1", "KT2", "RE", "RF"], [], [3])
+        mm(gl[2:], 256, ["KT3", "K13", "RUa1", "RUa2"], [], [3])
         front(2, T.sc)
         tt(T.fr[:, 32:40], T.fr[:, 24:32], b0, A.add, 16, ["fr3", "s1"], ["fr4"])
         tt(B[2][:, 0:256], B[3][:, 256:512], T.A3[:, 5:261], A.min, 256, ["A3"], ["t3"], [2, 3])
-        for j, (src, sk) in enumerate(((T.fr[:, 32:40], "fr4"), (T.fr[:, 16:24], "fr2"), (a12, "s0"))):
+        for j, src, sk in ((1, T.fr[:, 16:24], "fr2"), (2, a12, "s0")):
             tt(B[2][:, j:256:32], B[3][:, 256 + j:512:32], src, A.min, 8, [sk, "t3"], ["t3%d" % j], [2, 3])
-        t3 = ["t3", "t30", "t31", "t32"]
+        t3 = ["t3", "t31", "t32"]
         tt(T.i3[:], B[2][:, 0:256], T.o2[:], A.max, 256, t3 + ["o2"], ["i3"], [2])
-        tt(T.i4[:], B[2][:, 0:256], T.EE[:], A.max, 256, t3 + ["EE"], ["i4"], [2])
+        mm(grp(B[6][:, 0:256], [(T.KT1[0:33, 128:256], T.RX[:])]), 256, ["KT1", "K11", "RX1", "RX2"], [], [6])
+        tt(B[6][:, 0:256], B[6][:, 0:256], T.A1[:, 8:264], A.min, 256, ["A1"], ["te"], [6])
+        tt(T.EE[:], B[6][:, 0:256], T.Cf[:], A.max, 256, ["Cf", "te"], ["EE"], [6])
+        if t < RO - 1:
+            add("s", 200, ["KT1"], ["th1", "nT"], [lambda: S.activation(T.nT[0:8, 0:128], T.KT1[0:8, 128:256], F.Identity, accum_out=T.thf[:, 1:2])])
+            mm(grp(B[6][:, 256:257], [(T.ONf[:], T.thf[:, 1:2])]), 256, ["ONf", "th1"], [], [6])
+            ts(T.ti[:, 0:1], B[6][:, 256:257], 1.0 / 8192, None, A.mult, None, 1, [], ["ti0"], [6])
+            ts(T.ti[:, 1:2], T.ti[:, 0:1], 63, None, A.bitwise_and, None, 1, ["ti0"], ["ti1"])
+            tt(col(12), T.ti[:, 1:2], col(11), A.add, 1, ["ti1", "c11"], ["thr"])
+        tt(B[2][:, 0:256:32], B[3][:, 256:512:32], T.fr[:, 32:40], A.min, 8, ["fr4", "t3", "i3"], ["t30"], [2, 3])
+        tt(T.i4[:], B[2][:, 0:256], T.EE[:], A.max, 256, t3 + ["t30", "EE"], ["i4"], [2])
         ts(T.Ni[:], T.i3[:], 4095, None, A.bitwise_and, None, 256, ["i3"], ["Ni"])
         cp(T["Nu%d" % t][:], T.Ni[:], 256, ["Ni"], ["Nu%d" % t])
+        ts(T["Nu%d" % t][:, 0:256:32], T.fr[:, 32:40], -12288.0, None, A.add, None, 8, ["fr4"], ["Nu%d" % t])
         ts(T.Pi[:], T.i4[:], 4095, None, A.bitwise_and, None, 256, ["i4"], ["Pi"])
         if t < RO - 1: cp(T.Pu[:], T.Pi[:], 256, ["Pi"], allpu)
         else: cp(T.pq[:], T.Pi[:], 256, ["Pi"], ["pq"])
@@ -529,10 +597,10 @@ def rank_program(g, core, T, topo):
         cp(T.si[:, 0:8], B[7][:, 128:136], 8, [], ["si0"], [7])
         ts(T.si[:, 8:16], T.si[:, 0:8], 31, None, A.bitwise_and, None, 8, ["si0"], ["si1"])
         tt(T.si[:, 16:24], T.si[:, 8:16], T.sb[:], A.add, 16, ["si1", "sb"], ["si2"])
-        cp(T.us[:], T.si[:, 16:24], 8, ["si2"], ["us"])
+        cp(T.us[:, 0:8], T.si[:, 16:24], 8, ["si2"], ["us"])
         tt(T.v1[:], Mm, nn, A.add, 256, [mkey, nkey], ["v1"])
         ts(T.v2[:], T.v1[:], 1, None, A.arith_shift_right, None, 128, ["v1"], ["v2"])
-        cp(T.X[:, 0:4096].indirect(T.us[:]), T.v2[:], 128 * 3.8, ["us", "v2"], ["Xa", "Xb"])
+        cp(T.X[:, 0:4096].indirect(T.us[:, 0:8]), T.v2[:], 128 * 3.8, ["us", "v2"], ["Xa", "Xb"])
         act(T["mo%d" % t][:], nb[:, 0:256].indirect(T.u1[:, 16:24]), F.Copy, 128 * GC, ["um", mkey, nkey], ["mo%d" % t])
         dst = cores[(rank + 1 + t % 3) % len(cores)]
         hlp = helper_of(topo, cores, core, dst); to = dst if hlp is None else hlp

@@ -1,42 +1,24 @@
-from concourse.mybir import AluOpType as A, AxisListType, ActivationFunctionType as F
+from concourse.mybir import AluOpType as A, ActivationFunctionType as F
 
 RO = 4
 BF, F32, I32, U16 = "bfloat16", "float32", "int32", "uint16"
-SCRATCH = {
-    "X": ("sbuf", [128, 4112], BF), "xg": ("sbuf", [128, 4096], BF), "dg": ("sbuf", [128, 4096], BF),
-    "rg": ("sbuf", [128, 4096], BF), "zg": ("sbuf", [128, 4096], BF), "ll": ("sbuf", [128, 4112], BF),
-    "pm": ("sbuf", [128, 4112], BF), "ind": ("sbuf", [128, 4096], BF),
-    "pin": ("sbuf", [128, 256], I32), "cin": ("sbuf", [128, 256], I32), "wi": ("sbuf", [128, 1], I32), "thi": ("sbuf", [8, 1], I32),
-    "ON": ("sbuf", [128, 2048], BF), "Bm": ("sbuf", [128, 2048], BF), "nS": ("sbuf", [64, 2048], BF),
-    "Pm": ("sbuf", [128, 1920], BF), "TB": ("sbuf", [8, 128], BF), "TR": ("sbuf", [8, 1024], BF), "OH": ("sbuf", [8, 256], BF),
-    "jo": ("sbuf", [128, 144], F32), "j16": ("sbuf", [128, 128], F32), "jb": ("sbuf", [128, 128], F32),
-    "em": ("sbuf", [128, 128], I32), "eb": ("sbuf", [128, 128], BF),
-    "ci": ("sbuf", [128, 8], I32), "cf": ("sbuf", [128, 24], F32),
-    "Id": ("sbuf", [128, 128], BF), "I64": ("sbuf", [128, 128], BF), "In": ("sbuf", [128, 128], BF),
-    "S2": ("sbuf", [128, 144], BF), "Sn": ("sbuf", [128, 288], BF), "Sw": ("sbuf", [128, 288], BF),
-    "dia": ("sbuf", [128, 128], F32), "c16": ("sbuf", [128, 128], F32), "ctl": ("sbuf", [128, 1024], BF),
-    "G1": ("sbuf", [128, 8], BF), "G64": ("sbuf", [128, 16], BF), "L1": ("sbuf", [128, 12], BF), "LE": ("sbuf", [128, 16], BF),
-    "RA": ("sbuf", [33, 72], BF), "RB": ("sbuf", [8, 56], BF),
-    "RUa": ("sbuf", [33, 256], BF), "RUb": ("sbuf", [1, 520], BF), "RX": ("sbuf", [33, 256], BF),
-    "RE": ("sbuf", [8, 256], BF), "RF": ("sbuf", [8, 256], BF),
-    "KT1": ("sbuf", [33, 256], BF), "KT2": ("sbuf", [33, 256], BF), "KT3": ("sbuf", [33, 256], BF),
-    "ONf": ("sbuf", [8, 128], F32), "G8": ("sbuf", [8, 128], F32), "thf": ("sbuf", [8, 2], F32),
-    "fpi": ("sbuf", [128, 8], F32), "fpl": ("sbuf", [128, 8], U16), "sb": ("sbuf", [128, 8], F32),
-    "Pu": ("sbuf", [128, 256], U16), "Hu": ("sbuf", [128, 256], U16), "pq": ("sbuf", [128, 256], F32),
-    "i1": ("sbuf", [128, 256], I32), "i2": ("sbuf", [128, 256], I32), "hh": ("sbuf", [128, 256], I32),
-    "i3": ("sbuf", [128, 256], I32), "i4": ("sbuf", [128, 256], I32), "Ni": ("sbuf", [128, 256], I32), "Pi": ("sbuf", [128, 256], I32),
-    "hp": ("sbuf", [128, 256], F32), "nk": ("sbuf", [128, 256], BF), "nk2": ("sbuf", [128, 256], BF), "Cf": ("sbuf", [128, 256], F32),
-    "AA": ("sbuf", [128, 272], F32), "A1": ("sbuf", [128, 264], F32), "A2": ("sbuf", [128, 264], F32), "A3": ("sbuf", [128, 272], F32),
-    "o1": ("sbuf", [128, 256], F32), "o2": ("sbuf", [128, 256], F32), "EE": ("sbuf", [128, 256], F32),
-    "nT": ("sbuf", [64, 256], BF), "mK": ("sbuf", [128, 256], BF),
-    "ct0": ("sbuf", [128, 1024], BF), "f1": ("sbuf", [128, 128], BF), "f2": ("sbuf", [128, 128], BF), "fa": ("sbuf", [128, 128], BF),
-    "bb": ("sbuf", [128, 128], BF), "sg": ("sbuf", [128, 1024], BF), "qq": ("sbuf", [128, 128], BF),
-    "e1": ("sbuf", [128, 128], BF), "e2": ("sbuf", [128, 128], BF),
-    "u1": ("sbuf", [128, 24], U16), "u2": ("sbuf", [128, 16], U16), "u3": ("sbuf", [128, 16], U16), "us": ("sbuf", [128, 16], U16),
-    "gd": ("sbuf", [128, 128], F32), "sa": ("sbuf", [128, 128], F32), "sc": ("sbuf", [128, 128], F32),
-    "fr": ("sbuf", [128, 40], F32), "si": ("sbuf", [128, 24], I32), "v1": ("sbuf", [128, 128], I32), "v2": ("sbuf", [128, 128], I32),
-    "ti": ("sbuf", [128, 2], I32), "op": ("sbuf", [128, 256], F32), "oc": ("sbuf", [128, 256], F32), "ox": ("sbuf", [128, 128], F32),
+SB = {
+    BF: {"X": 4112, "xg": 4096, "dg": 4096, "rg": 4096, "zg": 4096, "ll": 4128, "pm": 4128, "ind": 4096,
+         "ON": 1024, "Bm": 2048, "nS": 2048, "Pa": 1920, "Pn": 1024, "TB": 128, "TR": 1024, "OH": 256, "eb": 128,
+         "Id": 128, "In": 128, "I64": 128, "I4": 128, "Ia": 128, "S2": 144, "Sn": 288, "Sw": 144, "c0": 128, "ctl": 1024, "ct0": 512,
+         "G1": 8, "L1": 12, "LE": 16, "RA": 40, "RB": 32, "RU": 256, "RV": 256, "RE": 256, "CR": 272,
+         "KT1": 256, "KT2": 128, "KT3": 128, "nk": 256, "nT": 256, "mK": 256, "fb": 128, "b1": 128, "b2": 128, "sg": 1024, "qq": 128,
+         "e1": 128, "e2": 128, "e3": 128},
+    F32: {"jo": 144, "j16": 128, "jb": 128, "cf": 24, "Idf": 128, "ONf": 128, "G8": 128, "thf": 2, "fpi": 8, "sb": 8,
+          "hp": 256, "Cf": 256, "Cm": 256, "pc": 256, "tq": 256, "AA": 272, "A1": 272, "A2": 272, "A3": 272, "o1": 256, "o2": 256,
+          "gd": 128, "sc": 128, "pq": 256, "op": 256, "oc": 256, "ox": 128, "oy": 128, "dl": 128},
+    I32: {"pin": 256, "cin": 256, "wi": 1, "thi": 1, "em": 128, "ci": 8, "i2": 256, "hh": 256, "i3": 256, "i4": 256, "Ni": 256, "Pi": 256,
+          "si": 24, "v1": 128, "v2": 128, "ti": 2},
+    U16: {"fpl": 8, "Pu": 256, "Hu": 256, "ul": 24, "un": 32, "us": 8},
 }
+PARTS = {"nS": 64, "nT": 64, "TB": 8, "TR": 8, "OH": 8, "RA": 33, "RB": 8, "RU": 33, "RV": 33, "RE": 8, "CR": 1,
+         "KT1": 33, "KT2": 33, "KT3": 33, "ONf": 8, "G8": 8, "thf": 8, "thi": 8}
+SCRATCH = {n: ("sbuf", [PARTS.get(n, 128), w], d) for d, t in SB.items() for n, w in t.items()}
 for _t in range(RO + 1):
     SCRATCH["Cu%d" % _t] = ("sbuf", [128, 256], U16)
     SCRATCH["nb%d" % _t] = ("sbuf", [128, 256], BF)
@@ -49,41 +31,24 @@ SEMAPHORES = (["sv", "ss", "sp", "sg", "sent"] + ["d%d" % i for i in range(16)]
               + ["ac%d" % t for t in range(RO)] + ["an%d" % t for t in range(RO)])
 
 NENG = 8
-R_ON = "sssv"
-X_ON = "sssv"
-PH, PN = 0.0, 500.0
-MXB = ((0, 1, 2, 3), (0, 1, 2, 3))
-PK, PT, PO = 0.0, 4000.0, 500.0
-X_ON0, R_ON0 = "ssss", "vvsv"
-ORDER0 = {"v": "x0 x1 d0 r0 h d1 h2 nk0 r1 x2 d2 r2 nk1 x3 d3 r3 nk2 l0 l1 nk3 pm0 l2 l3 pm1 l4 l5 pm2 l6 l7 pm3 fs0 mK0 fs1 tq fs2 AA fs3",
-          "s": "x0 x1 x2 r0 x3 r1 z0 r2 nT Cf z1 r3 z2 z3 in0 in1 in2 in3 in4 in5 in6 in7"}
-PMB, PC, LOOK = (6, 4, 6, 4, 0, 1, 2, 3), 1000.0, 0.7
-ORDER = {"v": "x0 x1 x2 x3 hp d0 h d1 h2 nk0 d2 nk1 d3 r3 nk2 l0 l1 nk3 pm0 l2 l3 pm1 l4 l5 pm2 l6 l7 pm3 fs0 fs1 tq AA",
-         "s": "x0 x1 x2 x3 r0 nT Cf r1 z0 r2 z1 r3 z2 z3 in0 in1 in2 in3 in4 in5 in6 in7"}
-ORDER["p"] = ORDER0["p"] = ("su2a mx0 su2b mx1 su3a su3b mx2 mx3 nn0 nn1 mx4 mx5 pq0 pq1 mx6 nn2 pq2 mx7 nn3 pq3 "
-                            "nn4 pq4 nn5 pq5 ct0 ct1 nn6 ct2 nn7 ct3 pq6 pq7 ct4 ct5 ct6 ct7 TB@0#0 k1d k1m TB@1#0 of0")
-FCH = ((0, 2), (2, 4), (4, 6), (6, 7), (7, 8))
-KT_ON, GATE = "ssv", "v"
-TAIL = {"v": "mK1 ul0 bb#0 f2 un0 um gd#0 sg1#0 s0 fr0 t1 qq#0 o1 ud bb#1 f1 ul1 un1 gd#1 fr1 sg1#1 s1#0 fr2 t2 qq#1 o2 KT3 e2 "
-             "ul2 un2 t3 gd#2 t31 t32 s1#1 i3 fr3 Ni fr4 Nu%#0 Nu%#1 M% te v1 EE si0 t30 si1 i4 si2 v2 us Pi Xa Pu0a ti0 ti1 thr",
-        "s": "A1 A3 f1 KT1 fb sg0#0 fa A2 e1 KT2 f2 sg0#1 th1 mo%",
-        "p": "KT1@2 Pm@0#0 Pm@1#0 Id@5#0 K11@7#1 K11@4#0 Pm@5#0 Pm@5#1 TB@0#1 S64@7 qq@4#0 TB@1#1 of1 KT1@3#0 Pm@0#1 Pm@1#1 "
-             "K11@4#1 Id@5#1 Pm@5#2 Pm@5#3 qq@4#1 KT1@3#1 of2 KT3@3 KT1@6 Sw@7 ONf@6"}
-R_ON, X_ON = "spsv", "svsv"
-ORDER = {"v": "hp x3 x1 d0 d2 h h2 nk0 nk1 d3 r3 nk2 l0 l1 nk3 pm0 l3 l2 pm1 l5 l7 l4 l6 pm2 pm3 tq fs0 fs1 mK0 fs2 fs3 AA",
-         "s": "x0 x2 d1 r0 r1 r2 nT z0 z1 z2 Cf z3 in1 in0 nkc in2 in3 in5 in4 in6 in7",
-         "p": "su0a su0b su1a su1b su2a su2b nn0 mx1 mx0 su3a nn1 su3b mx3 mx2 mx5 pq1 pq0 mx7 mx4 mx6 nn2 pq2 ct0 nn3 nn5 pq3 nn4 pq5 ct1 pq4 "
-              "nn6 ct2 pq6 ct3 nn7 pq7 ct4 ct5 ct6 ct7 TB@0#0 k1d k1m TB@1#0 of0"}
-ORDER0 = {"v": "h d0 h2 r0 d1 nk0 r1 d2 nk1 d3 nk2 r3 l1 l0 nk3 pm0 l3 l2 pm1 l5 l4 pm2 l7 l6 pm3 fs1 tq fs0 mK0 AA fs2 fs3",
-          "s": "x0 nT x1 x3 x2 z0 r2 z1 z2 Cf z3 in0 in1 in2 in3 in4 in5 in6 in7",
-          "p": "su0a su0b su1a su1b su2a mx1 su2b mx2 su3a mx0 su3b nn0 nn1 mx3 mx5 mx4 pq0 mx7 pq1 nn2 nn5 pq2 ct0 mx6 nn3 pq3 nn4 pq4 pq5 ct1 ct2 "
-               "nn6 pq6 ct3 nn7 pq7 ct4 ct5 ct6 TB@1#0 ct7 TB@0#0 k1d k1m of0"}
-TAIL = {"v": "mK1 ul0 bb#0 f2 un0 um gd#0 sg1#0 t1 qq#0 s0 fr0 ud bb#1 f1 ul1 un1 o1 sg1#1 t2 gd#1 qq#1 s1#0 fr1 o2 KT3 fr2 e2 ul2 un2 t3 gd#2 "
-             "t31 t32 s1#1 i3 fr3 Ni fr4 Nu%#0 M% Nu%#1 te v1 EE si0 t30 si1 i4 si2 ti0 Pi us v2 Xa Pu0a ti1 thr",
-        "s": "A3 A1 f1 KT1 e1 sg0#0 th1 A2 fb fa KT2 f2 sg0#1 mo%",
-        "p": "Pm@0#0 Pm@1#0 KT1@2 Id@5#0 K11@7#1 Pm@5#0 Pm@5#1 K11@4#0 S64@7 qq@4#0 TB@1#1 TB@0#1 K11@4#1 of1 Pm@0#1 Pm@1#1 KT1@3#0 Id@5#1 "
-             "Pm@5#2 Pm@5#3 qq@4#1 KT1@6 KT1@3#1 of2 KT3@3 Sw@7 ONf@6"}
-HOP, LAT, GC = 130.0, 5600.0, 1.56
+PMB = (6, 4, 6, 4, 0, 1, 6, 4)
+SUB = ((4, 0), (4, 64), (5, 0), (4, 128))
+SG_ON = "svsv"
+AL, LO, HI = 4096.0, -7936.0, 64.0
+QC = -7 * LO - 8 * HI
+LOOKUP = "x1s x3s x0v sums"
+JOIN = ("y1 dx x2v d0 xa1 cm xa2 xa0 xa3 r0s su0a dy su0b i1 d2a ib nk0 hh hp0 d2b r1a Hu0 r1b Cm nT su1 r2v su2a mr1 nn0 su2b nk1 hp1 mr0 mw1 mr2 "
+        "z0 Hu1 d3 nk2 z1 r3v hp2 mw0 mw2 mr3 su3a l0 Hu2 su3b mw3 nk3 l2 hp3 mx4 l1 z2 Hu3 pm0 mx6 l3 mx5 nn1 pq0 tqb pm1 pq1 z3 in0 mx7 nn2 pq2 "
+        "l5 in1 l4 in2 nn5 nn3 ct1 pq3 pm2 l7 nn6 pm3b nn4 pq5 in3 pq4 ct0 l6 pm3a in5 ct3 nn7 pq7 ct5 ct2 TB1 pq6 in4 fs4 fs5 AA mK0 f0 ct4 in7 "
+        "in6 ct7 k1a ct6 fc TB0 TB3 TB2 fs7 fs6")
+CUTS = ("mK1 fb k1b ul0 b1 k1m pf KT1 pb1 rk1 sg1b rv1 sg1a rs1a of0 sg1d sg1c A2 A1 rs1b un0 rs1c A3 fr0 rs1d q1 g1 lo1 ls1 t1 kt1 ul1 sc0 b2 o1 pt0 "
+        "e2 KT2 rk2 ps pb2 of1 rv2 sg2b sg2a g2 rs2a sg2c sg2d rs2b un1 t2 um e1 fr1 rs2c rs2d g3a lo2 q2 kt2 ls2 sc1 o2 pt1 e3 ul2 KT3 g3b t3 of2 "
+        "un2 i3 M g4 th1 fr2 Ni vv Sw sc2 Nu th2 Nu0 sendN th3 t4 si0 i4 si1 i40 si2 mo Pi v2 pa+ Pu us pb+ put sendM pc+ th4 tqa+")
+FIRST = "cm kPa pa x0s tqa pb x1s kth kSw kRB pc"
+JOIN0 = ("d0 su0a x2s i1 r0v su0b ib d1 nk0 xa3 su1a hh xa1 r1v hp0 Hu0 xa2 x3s mr2 mr3 xa0 z0 su1b mr0 d2 r2s mr1 kc0 nk1 hp1 Hu1 z1 mw2 su2a su2b "
+         "mw0 d3 r3s nT mw1 nk2 mw3 hp2 su3a su3b l0 nn0 Hu2 kfp l1 nk3 hp3 mx4 nn1 mx5 Hu3 z2 l2 pm0 z3 l3 pq1 kg mx6 pq0 mx7 in1 kc1 pm1 in0 kRU "
+         "Cm nn3 nn2 pq2 pq3 l5 l6 ct1 l4 tqb pm3a in2 pm2 AA nn5 in3 ct0 ct2 nn4 l7 pq5 kPn nn6 pq6 nn7 in6 in5 pq4 ct3 f0 pm3b in4 mK0 fs6 pq7 "
+         "TB1 TB2 TB3 in7 fs4 fs5 TB0 ct6 ct4 fs7 ct5 k1a ct7 fc")
 
 
 def engines_mask(topo, src, dst):
@@ -121,91 +86,46 @@ def helper_program(g, core, T, topo):
 
 def run(ops, g, T):
     n = len(ops)
-    lastw, reads, bank = {}, {}, {}
-    pre = [dict() for _ in range(n)]
+    pre = [set() for _ in range(n)]
+    acc, bank, lastg = {}, {}, None
     for i, o in enumerate(ops):
         e = o["e"]
-
-        def edge(j, raw):
-            if j != i:
-                need = ops[j]["e"] != e or ops[j]["sem"] is not None or e != "p"
-                pre[i][j] = pre[i].get(j, False) or need
-        for k in o["r"]:
-            if k in lastw: edge(lastw[k], True)
-        for k in o["w"]:
-            if k in lastw: edge(lastw[k], False)
-            for j in reads.get(k, []): edge(j, False)
-        for k in o["b"]:
-            if k in bank:
-                j = bank[k]
-                pre[i][j] = pre[i].get(j, False) or ops[j]["e"] != e
-            bank[k] = i
-        for j in o["after"]:
-            pre[i].setdefault(j, False)
-        for k in o["r"]: reads.setdefault(k, []).append(i)
-        for k in o["w"]:
-            lastw[k] = i; reads[k] = []
-    tags = {}
-    for i, o in enumerate(ops): tags.setdefault((o["tag"], o["e"]), []).append(i)
-    for t in range(RO):
-        for e, names in (ORDER0 if t == 0 else ORDER).items():
-            seq = []
-            for nm in (names + " " + TAIL[e]).replace("%", str(t)).split():
-                nm, _, k = nm.partition("#"); found = tags.get(((t, nm), e), [])
-                seq += found[int(k):int(k) + 1] if k else found
-            for j, i in zip(seq, seq[1:]): pre[i].setdefault(j, False)
-    suc = [[] for _ in range(n)]
-    for i in range(n):
-        for j in pre[i]: suc[j].append(i)
-    left = [len(p) for p in pre]; topo_order = [i for i in range(n) if left[i] == 0]
-    for i in topo_order:
-        for j in suc[i]:
-            left[j] -= 1
-            if left[j] == 0: topo_order.append(j)
-    assert len(topo_order) == n
-    tail = [0.0] * n
-    for i in reversed(topo_order):
-        tail[i] = ops[i]["c"] + ops[i]["lat"] + max([tail[j] + HOP for j in suc[i]] + [0.0]) + ops[i]["pri"]
-    free, fin, left = {}, [0.0] * n, [len(p) for p in pre]
-    rdy = [0.0] * n
-    ready = [i for i in range(n) if left[i] == 0]
-    order = []
-    while ready:
-        st = {i: max(rdy[i], free.get(ops[i]["e"], 0.0)) for i in ready}
-        first = min(ready, key=lambda i: (st[i], -tail[i]))
-        e = ops[first]["e"]
-        cand = [i for i in ready if ops[i]["e"] == e and st[i] <= st[first] + LOOK * ops[first]["c"] and (st[i] <= st[first] or tail[i] > tail[first] + ops[first]["c"])]
-        i = max(cand, key=lambda i: (tail[i], -i))
-        ready.remove(i); order.append(i)
-        free[e] = st[i] + ops[i]["c"]; fin[i] = free[e] + ops[i]["lat"]
-        for j in suc[i]:
-            rdy[j] = max(rdy[j], fin[i] + (HOP if pre[j][i] else 0.0)); left[j] -= 1
-            if left[j] == 0: ready.append(j)
-    if g is None:
-        return max(fin)
-    pos, cnt = {}, {}
-    for i in order:
-        e = ops[i]["e"]; cnt[e] = cnt.get(e, 0) + 1; pos[i] = cnt[e]
-    know, clock, waits, sig, lastg = {}, {}, {}, set(), None
-    for i in order:
-        kn = know.setdefault(ops[i]["e"], {}); wl = []
-        if ops[i]["e"] == "g" and ops[i]["sem"] is None and not ops[i]["rem"]:
-            if lastg is not None: pre[i][lastg] = True
+        for isw, regs in ((False, o["r"]), (True, o["w"])):
+            for nm, m, p0, p1 in regs:
+                for j, w2, m2, q0, q1 in acc.get(nm, []):
+                    if j != i and (isw or w2) and m & m2 and p0 < q1 and q0 < p1 and not ops[j]["e"] == e == "p":
+                        pre[i].add(j)
+        for isw, regs in ((False, o["r"]), (True, o["w"])):
+            for nm, m, p0, p1 in regs:
+                old = acc.setdefault(nm, [])
+                if isw: old[:] = [x for x in old if x[2] & ~m or x[3] < p0 or x[4] > p1]
+                old.append((i, isw, m, p0, p1))
+        for k in {x[0] for x in o["r"] + o["w"] if SCRATCH[x[0]][0] == "psum"}:
+            last = bank.setdefault(k, {})
+            pre[i].update(j for e2, j in last.items() if e2 != e)
+            last[e] = i
+        if e == "g" and o["sem"] is None and not o["rem"]:
+            if lastg is not None: pre[i].add(lastg)
             lastg = i
-        for j in sorted(pre[i], key=lambda j: -fin[j]):
-            if not pre[i][j]: continue
+    pos, cnt = {}, {}
+    for i, o in enumerate(ops):
+        cnt[o["e"]] = cnt.get(o["e"], 0) + 1; pos[i] = cnt[o["e"]]
+    know, clock, waits, sig = {}, {}, {}, set()
+    for i, o in enumerate(ops):
+        kn = know.setdefault(o["e"], {}); wl = []
+        for j in sorted(pre[i], reverse=True):
             key = ("x", j) if ops[j]["sem"] is not None else ops[j]["e"]
             val = 1 if ops[j]["sem"] is not None else pos[j]
             if kn.get(key, 0) >= val: continue
             wl.append(j); sig.add(j); kn[key] = val
             for k2, v2 in clock[j].items():
                 if kn.get(k2, 0) < v2: kn[k2] = v2
-        waits[i] = wl; clock[i] = dict(kn) if ops[i]["e"] != "x" else {}
+        waits[i] = wl; clock[i] = dict(kn) if o["e"] != "x" else {}
     q = {"v": g.vector, "s": g.scalar, "p": g.tensor, "g": g, "y": g.sync}
     sems = {"v": T.sem.sv, "s": T.sem.ss, "p": T.sem.sp, "g": T.sem.sg}
     num, tot = {}, {}
-    for i in order:
-        o = ops[i]; e = o["e"]
+    for i, o in enumerate(ops):
+        e = o["e"]
         if e == "x": continue
         for j in waits[i]:
             if ops[j]["sem"] is not None: q[e].wait_ge(ops[j]["sem"], ops[j]["val"])
@@ -216,8 +136,8 @@ def run(ops, g, T):
             ins.then_inc(o["sem"], 16)
         elif i in sig:
             tot[e] = tot.get(e, 0) + 1; num[i] = tot[e]; ins.then_inc(sems[e], 1)
-    for i in order:
-        if ops[i]["sem"] is not None and i not in sig: g.wait_ge(ops[i]["sem"], ops[i]["val"])
+    for i, o in enumerate(ops):
+        if o["sem"] is not None and i not in sig: g.wait_ge(o["sem"], o["val"])
 
 
 def rank_program(g, core, T, topo):
@@ -225,399 +145,338 @@ def rank_program(g, core, T, topo):
     if rank is None:
         helper_program(g, core, T, topo)
         return
-    cores = list(T.cores); ops = []; nd = [0]; pri = [0.0]; rnd = [-1]
-
-    def tag_of(w, e):
-        k = w[0] if len(w) else ""
-        if k in ("pa", "pb", "pc"): return "hp"
-        if k in ("cm", "i1"): return "h"
-        if k in ("ib", "hh"): return "h2"
-        if k[:2] in ("hp", "Hu"): return "nk" + k[2:]
-        return k
-
+    cores = list(T.cores); ops = []; nd = [0]; masks = {}; nsent = [0]
     V, S, P = g.vector, g.scalar, g.tensor
-    B = [T["B%d" % b] for b in range(8)]
 
-    def add(e, c, r, w, fs, b=(), lat=0.0, sem=None, val=0, after=(), rem=False):
-        ops.append({"e": e, "c": float(c), "r": list(r), "w": list(w), "f": fs, "b": list(b), "lat": lat, "sem": sem, "val": val, "after": list(after),
-                    "pri": pri[0], "rem": rem, "tag": (rnd[0], tag_of(w, e) if len(w) or not len(b) else "%s@%d" % (r[0], b[0]))})
-        return len(ops) - 1
+    def R(nm, c0=0, c1=None, st=1, p0=0, p1=None):
+        sh = SCRATCH[nm][1]
+        c1 = sh[1] if c1 is None else c1; p1 = sh[0] if p1 is None else p1
+        if (c0, c1, st) not in masks:
+            masks[(c0, c1, st)] = ((1 << (c1 - c0)) - 1) << c0 if st == 1 else sum(1 << c for c in range(c0, c1, st))
+        ps = slice(None) if (p0, p1) == (0, sh[0]) else slice(p0, p1)
+        return {"ap": T[nm][ps, slice(c0, c1) if st == 1 else slice(c0, c1, st)], "rg": [(nm, masks[(c0, c1, st)], p0, p1)]}
 
-    def vc(n): return 20 + 0.83 * max(64, n)
-    def ts(out, in0, s1, s2, o0, o1, n, r, w, b=()):
-        if o1 is None: add("v", vc(n), r, w, [lambda: V.tensor_scalar(out, in0, s1, None, o0)], b)
-        else: add("v", vc(n), r, w, [lambda: V.tensor_scalar(out, in0, s1, s2, o0, o1)], b)
-    def tt(out, a, c, op, n, r, w, b=()): add("v", vc(n), r, w, [lambda: V.tensor_tensor(out, a, c, op)], b)
-    def cp(out, a, n, r, w, b=()): add("v", vc(n), r, w, [lambda: V.tensor_copy(out, a)], b)
-    def ms(out, val, n, w): add("v", vc(n), [], w, [lambda: V.memset(out, val)])
-    def scan(out, d0, d1, o0, o1, n, r, w): add("v", vc(n), r, w, [lambda: V.tensor_tensor_scan(out, d0, d1, 0.0, o0, o1)])
-    def act(out, a, fn, n, r, w, b=(), bias=0.0, scale=1.0):
-        add("s", 65 + 0.83 * n, r, w, [lambda: S.activation(out, a, fn, bias=bias, scale=scale)], b)
-    def mm(lst, cyc, r, w, b):
-        add("p", 20 + 0.42 * cyc, r, w, [(lambda x=x: P.matmul(x[0], x[1], x[2], x[3], x[4])) for x in lst], b)
-    def grp(out, pairs): return [(out, l, rr, i == 0, i == len(pairs) - 1) for i, (l, rr) in enumerate(pairs)]
-    def iota(out, pat, base, cm, n, w, flt=True, r=()):
-        if flt: add("g", 130 + 1.66 * n, r, w, [lambda: g.iota(out, pat, base, cm, allow_small_or_imprecise_dtypes=True)])
-        else: add("g", 130 + 1.66 * n, r, w, [lambda: g.iota(out, pat, base, cm)])
-    def asel(out, a, pat, op, fill, base, cm, n, r, w): add("g", 170 + 1.66 * n, r, w, [lambda: g.affine_select(out, a, pat, op, fill, base, cm)])
-    def dma(e, out, a, r, w, lat, slow=False):
+    def IX(win, off): return {"ap": win["ap"].indirect(off["ap"]), "rg": win["rg"] + off["rg"]}
+    def Bk(b, c0=0, c1=512, st=1, p1=128): return R("B%d" % b, c0, c1, st, 0, p1)
+    def ap(x): return x["ap"] if isinstance(x, dict) else x
+    def rgs(*xs): return [r for x in xs if isinstance(x, dict) for r in x["rg"]]
+    def add(e, r, w, fs, sem=None, val=0, rem=False): ops.append({"e": e, "r": r, "w": w, "f": fs, "sem": sem, "val": val, "rem": rem})
+
+    def ts(out, a, s1, o0, s2=None, o1=None):
+        f = (lambda: V.tensor_scalar(out["ap"], a["ap"], ap(s1), None, o0)) if o1 is None else (lambda: V.tensor_scalar(out["ap"], a["ap"], ap(s1), ap(s2), o0, o1))
+        add("v", rgs(a, s1, s2), rgs(out), [f])
+    def tt(out, a, b, op): add("v", rgs(a, b), rgs(out), [lambda: V.tensor_tensor(out["ap"], a["ap"], b["ap"], op)])
+    def cp(out, a): add("v", rgs(a), rgs(out), [lambda: V.tensor_copy(out["ap"], a["ap"])])
+    def ms(out, val): add("v", [], rgs(out), [lambda: V.memset(out["ap"], val)])
+    def scan(out, d0, d1, o0, o1): add("v", rgs(d0, d1), rgs(out), [lambda: V.tensor_tensor_scan(out["ap"], d0["ap"], d1["ap"], 0.0, o0, o1)])
+    def act(out, a, fn=F.Identity, bias=0.0, scale=1.0):
+        if fn == F.Copy: add("s", rgs(a), rgs(out), [lambda: S.activation(out["ap"], a["ap"], fn)])
+        else: add("s", rgs(a, scale), rgs(out), [lambda: S.activation(out["ap"], a["ap"], fn, bias=bias, scale=ap(scale))])
+    def mm(trip, first=True, last=True, alone=False):
+        add("p", [r for x in trip for r in rgs(x[1], x[2])], [r for x in trip for r in rgs(x[0])],
+            [(lambda x=x, i=i: P.matmul(x[0]["ap"], x[1]["ap"], x[2]["ap"], alone or (first and i == 0), alone or (last and i == len(trip) - 1)))
+             for i, x in enumerate(trip)])
+    def iota(out, pat, base, cm=0, whole=False):
+        if whole: f = lambda: g.iota(out["ap"], pat, base, cm)
+        else: f = lambda: g.iota(out["ap"], pat, base, cm, allow_small_or_imprecise_dtypes=True)
+        add("g", [], rgs(out), [f])
+    def asel(out, a, pat, op, fill, base, cm): add("g", rgs(a), rgs(out), [lambda: g.affine_select(out["ap"], a["ap"], pat, op, fill, base, cm)])
+    def dma(e, out, a, slow=False):
         sem = T.sem["d%d" % nd[0]]; nd[0] += 1
         qq = {"g": g, "s": S, "y": g.sync}[e]
-        if slow: f = lambda: qq.dma_start(out, a, allow_slow_non_contiguous=True)
-        else: f = lambda: qq.dma_start(out, a)
-        add(e, 60, r, w, [f], lat=lat, sem=sem, val=16)
+        f = (lambda: qq.dma_start(ap(out), ap(a), allow_slow_non_contiguous=True)) if slow else (lambda: qq.dma_start(ap(out), ap(a)))
+        add(e, rgs(a), rgs(out), [f], sem=sem, val=16)
+    def col(j): return R("cf", j, j + 1)
+    def fill(nm, val, c0=0, c1=None, st=1, p0=0, p1=None):
+        c1 = SCRATCH[nm][1][1] if c1 is None else c1; p1 = SCRATCH[nm][1][0] if p1 is None else p1
+        act(R(nm, c0, c1, st, p0, p1), R("ON", 0, len(range(c0, c1, st)), 1, p0, p1), scale=val)
 
-    dma("y", T.pin[:], T.pn[:], [], ["pin"], 2200)
-    dma("s", T.X[:, 0:2048], T.lit[:, 0:2048], [], ["Xa"], 4500)
-    dma("y", T.X[:, 2048:4096], T.lit[:, 2048:4096], [], ["Xb"], 4500)
-    dma("s", T.cin[:], T.cn[:], [], ["cin"], 4500)
-    dma("y", T.nb0[:, 0:128], T.neg[:], [], ["n0"], 4500)
-    pri[0] = 1e6
-    dma("g", T.wi[:], T.wt[:], [], ["wi"], 3000, True)
-    dma("g", T.thi[:], T.th[:], [], ["thi"], 3000, True)
-    cf, ci = T.cf, T.ci
-    def col(j): return cf[:, j:j + 1]
-    iota(ci[:, 0:1], [[0, 1]], 0, 1, 1, ["ci0"], False)
-    iota(T.jo[:], [[1, 144]], 0, 0, 144, ["jo"])
-    iota(T.j16[:], [[0, 8], [1, 16]], 0, 0, 128, ["j16"])
-    iota(T.jb[:], [[16, 8], [0, 16]], 0, 0, 128, ["jb"])
-    iota(T.em[:], [[-1, 128]], 0, 1, 128, ["em"], False)
-    iota(T.fpi[:], [[2048, 2], [32, 4]], 31, 0, 8, ["fpi"])
-    iota(T.sb[:], [[512, 8]], 0, 0, 8, ["sb"])
-    pri[0] = 0.0
-    iota(T.ON[:], [[0, 2048]], 1, 0, 2048, ["ON"])
-    asel(T.Bm[:], T.ON[:], [[-1, 16], [-16, 8], [0, 16]], A.is_equal, 0.0, 0, 1, 2048, ["ON"], ["Bm"])
-    asel(T.nS[:], T.ON[0:64, :], [[-1, 16], [-16, 4], [0, 32]], A.is_equal, 0.0, 0, 1, 2048, ["ON"], ["nS"])
-    asel(T.ct0[:], T.ON[:, 0:1024], [[0, 32], [1, 32]], A.is_gt, 0.0, 0, 0, 1024, ["ON"], ["cz"])
-    asel(T.OH[:], T.ON[0:8, 0:256], [[-1, 8], [0, 32]], A.is_equal, 0.0, 0, 1, 256, ["ON"], ["OH"])
-    asel(T.TR[:], T.ON[0:8, 0:1024], [[-1, 8], [0, 128]], A.is_equal, 0.0, 0, 1, 1024, ["ON"], ["TR"])
-    ms(T.TB[:], 0.5, 64, ["TB"])
-    asel(T.TB[:], T.TB[:], [[0, 8], [-1, 16]], A.is_ge, -0.5, 14, -1, 128, ["TB"], ["TB"])
-    ms(T.ONf[:], 1.0, 128, ["ONf"])
-    asel(T.G8[:], T.ONf[:], [[-1, 8], [0, 16]], A.is_equal, 0.0, 0, 1, 128, ["ONf"], ["G8"])
-    ts(ci[:, 1:2], ci[:, 0:1], 15, None, A.bitwise_and, None, 1, ["ci0"], ["ci1"])
-    ts(ci[:, 2:3], ci[:, 0:1], 5, None, A.arith_shift_right, None, 1, ["ci0"], ["ci2"])
-    ts(ci[:, 3:4], ci[:, 0:1], 31, None, A.bitwise_and, None, 1, ["ci0"], ["ci3"])
-    cp(col(0), ci[:, 0:1], 1, ["ci0"], ["c0"])
-    cp(col(1), ci[:, 1:2], 1, ["ci1"], ["c1"])
-    tt(col(2), col(0), col(1), A.subtract, 1, ["c0", "c1"], ["c2"])
-    ts(col(3), col(2), 15.0, None, A.add, None, 1, ["c2"], ["c3"])
-    cp(col(4), T.wi[:], 1, ["wi"], ["c4"])
-    ts(col(5), ci[:, 2:3], 4.0, None, A.add, None, 1, ["ci2"], ["c5"])
-    ts(col(6), ci[:, 3:4], 31.0, 8192.0, A.is_equal, A.mult, 1, ["ci3"], ["c6"])
-    for j, off in ((7, -1.0), (8, 0.0), (9, -1.0), (10, -2.0)):
-        ts(col(j), col(1), 128.0, off, A.mult, A.add, 1, ["c1"], ["c%d" % j])
-    ts(col(13), col(1), 32.0, None, A.mult, None, 1, ["c1"], ["c13"])
-    ts(T.sb[:], T.sb[:], col(13), None, A.add, None, 8, ["sb", "c13"], ["sb"])
-    ts(T.fpl[:], T.fpi[:], col(8), None, A.add, None, 8, ["fpi", "c8"], ["fpl"])
-    ts(T.Id[:], T.jo[:, 0:128], col(0), None, A.is_equal, None, 128, ["jo", "c0"], ["Id"])
-    ts(T.I64[:], T.Id[:], 1.0 / 64, None, A.mult, None, 64, ["Id"], ["I64"])
-    ts(T.In[:], T.Id[:], -1.0, None, A.mult, None, 64, ["Id"], ["In"])
-    ts(T.S2[:], T.jo[:], col(3), 2.0, A.is_equal, A.mult, 144, ["jo", "c3"], ["S2"])
-    ts(T.Sn[:, 0:144], T.S2[:], -0.5, None, A.mult, None, 72, ["S2"], ["Sn"])
-    ts(T.Sn[:, 144:288], T.S2[:], 0.5, None, A.mult, None, 72, ["S2"], ["S1"])
-    ts(T.Sw[:, 0:144], T.S2[:], 0.5, col(4), A.mult, A.mult, 72, ["S2", "c4"], ["Sw"])
-    ts(T.Sw[:, 144:288], T.S2[:], 32.0, None, A.mult, None, 72, ["S2"], ["S64"])
-    ts(T.dia[:], T.j16[:], col(1), None, A.is_equal, None, 128, ["j16", "c1"], ["dia"])
-    ts(T.c16[:], T.j16[:], 0.0, None, A.is_gt, None, 128, ["j16"], ["c16"])
-    ms(T.ctl[:], 0.0, 512, ["ctl"])
-    ms(T.ctl[:, 0:1024:32], 512.0, 32, ["ctl"])
-    ts(T.G1[:], T.jo[:, 0:128:16], col(2), None, A.is_equal, None, 8, ["jo", "c2"], ["G1"])
-    ts(T.G64[:, 0:8], T.G1[:], 64.0, None, A.mult, None, 8, ["G1"], ["G64a"])
-    ts(T.G64[:, 8:16], T.G1[:], -64.0 * 8192, None, A.mult, None, 8, ["G1"], ["G64b"])
-    ts(T.L1[:], T.jo[:, 0:12], col(5), None, A.is_equal, None, 12, ["jo", "c5"], ["L1"])
-    ts(T.LE[:, 0:12], T.L1[:], col(6), None, A.mult, None, 12, ["L1", "c6"], ["LE"])
-    tt(T.LE[:, 12:16], T.LE[:, 4:8], T.L1[:, 4:8], A.max, 8, ["L1", "LE"], ["LD"])
-    ts(T.RB[:, 48:56], T.Id[0:8, 0:8], -31.0 / 8192, None, A.mult, None, 8, ["Id"], ["RB6"])
-    ts(T.v1[:], T.em[:], 15, None, A.bitwise_and, None, 128, ["em"], ["v1"])
-    ts(T.jb[:], T.jb[:], col(2), 16.0, A.not_equal, A.mult, 128, ["jb", "c2"], ["jb"])
-    tt(T.eb[:], T.v1[:], T.jb[:], A.add, 256, ["v1", "jb"], ["eb"])
-    if GATE != "v": cp(T.jb[:], T.Id[:], 128, ["Id"], ["jb"])
-    for u in range(1, 16):
-        ts(T.Pm[:, 128 * (u - 1):128 * u], T.eb[:], float(u), None, A.is_equal, None, 64, ["eb"], ["Pm%d" % u])
-    pk = ["Pm%d" % u for u in range(1, 16)]
-    asel(T.Pm[:], T.Pm[:], [[0, 15], [-1, 128]], A.not_equal, -1.0, 0, 1, 1920, pk, pk + ["Pm"])
-    oh = T.Id[0:8, 0:8]
-    ms(T.RA[:], 0.0, 36, ["RA"])
-    for c in range(3):
+    dma("y", R("pin"), T.pn[:])
+    dma("s", R("cin"), T.cn[:])
+    dma("y", R("X", 0, 2048), T.lit[:, 0:2048])
+    dma("s", R("X", 2048, 4096), T.lit[:, 2048:4096])
+    dma("y", R("nb0", 0, 128), T.neg[:])
+    ms(R("ON"), 1.0)
+    iota(R("ci", 0, 1), [[0, 1]], 0, 1, True)
+    iota(R("jo"), [[1, 144]], 0)
+    dma("g", R("wi"), T.wt[:], True)
+    dma("g", R("thi"), T.th[:], True)
+    iota(R("jb"), [[16, 8], [0, 16]], 0)
+    iota(R("em"), [[-1, 128]], 0, 1, True)
+    iota(R("j16"), [[0, 8], [1, 16]], 0)
+    ms(R("ONf"), 1.0); ms(R("X", 4096, 4112), 255.0)
+    asel(R("G8"), R("ONf"), [[-1, 8], [0, 16]], A.is_equal, 0.0, 0, 1)
+    for j in range(2): asel(R("Bm", 1024 * j, 1024 * j + 1024), R("ON"), [[-1, 8], [-16, 8], [0, 16]], A.is_equal, 0.0, -8 * j, 1)
+    for j in range(2): asel(R("nS", 1024 * j, 1024 * j + 1024), R("ON", p1=64), [[-1, 8], [-16, 4], [0, 32]], A.is_equal, 0.0, -8 * j, 1)
+    ts(R("ci", 1, 2), R("ci", 0, 1), 15, A.bitwise_and)
+    ts(R("ci", 2, 3), R("ci", 0, 1), 5, A.arith_shift_right)
+    ts(R("ci", 3, 4), R("ci", 0, 1), 31, A.bitwise_and)
+    cp(R("cf", 0, 2), R("ci", 0, 2))
+    tt(col(2), col(0), col(1), A.subtract)
+    ts(R("Id"), R("jo", 0, 128), col(0), A.is_equal)
+    ts(col(5), R("ci", 2, 3), 4.0, A.add)
+    ts(col(6), R("ci", 3, 4), 31.0, A.is_equal, 8192.0, A.mult)
+    ts(col(3), col(2), 15.0, A.add)
+    ts(col(15), col(1), 15.0, A.is_lt, 16384.0, A.mult)
+    ts(R("G1"), R("jo", 0, 128, 16), col(2), A.is_equal)
+    ts(R("L1"), R("jo", 0, 12), col(5), A.is_equal)
+    ts(R("S2"), R("jo"), col(3), A.is_equal, 2.0, A.mult)
+    fill("ctl", 0.0); fill("ct0", 1.0); fill("ctl", 512.0, 0, 1024, 32); fill("ct0", 0.0, 0, 512, 32)
+    for j, mul, off in ((7, 4.0, 0.0), (8, 128.0, 0.0), (9, 128.0, 16.0), (10, 128.0, 16.0 + QC), (13, 32.0, 0.0), (14, 1.0, 1.0)):
+        act(col(j), col(1), bias=off, scale=mul)
+    for nm, sc in (("In", -1.0), ("Idf", 1.0)): act(R(nm), R("Id"), scale=sc)
+    act(R("Sn", 0, 144), R("S2"), scale=-0.5); act(R("Sn", 144, 288), R("S2"), scale=0.5)
+    act(col(16), col(15), bias=-12288.0)
+    for nm, sc in (("I64", 64.0), ("I4", 4 * AL), ("Ia", -AL)): act(R(nm), R("Id"), scale=sc)
+    for nm, at, val in (("ll", 0, -256.0), ("ll", 4112, 255.0), ("pm", 0, 255.0), ("pm", 4112, 255.0)): fill(nm, val, at, at + 16)
+    fill("AA", 0.0, 0, 8); fill("AA", 0.0, 264, 272); fill("TB", 1.0 / 128)
+    ts(R("LE", 0, 12), R("L1"), col(6), A.mult)
+    ts(R("v1"), R("em"), 15, A.bitwise_and)
+    ts(R("jb"), R("jb"), col(2), A.not_equal, 16.0, A.mult)
+    tt(R("LE", 12, 16), R("LE", 4, 8), R("L1", 4, 8), A.max)
+    tt(R("eb"), R("v1"), R("jb"), A.add)
+    for r in range(8): cp(R("Pu", 32 * r, 32 * r + 32), R("pin", r, 256, 8))
+    for r in range(8): cp(R("Cu0", 32 * r, 32 * r + 32), R("cin", r, 256, 8))
+    cp(R("Pi"), R("Pu"))
+    iota(R("fpi", 0, 4), [[1, 4]], 0)
+    iota(R("fpi", 4, 8), [[32, 4]], 2048 + 31)
+    iota(R("CR", 256, 264), [[2048, 2], [32, 4]], 0)
+    asel(R("TR"), R("ON", p1=8), [[-1, 8], [0, 128]], A.is_equal, 0.0, 0, 1)
+    asel(R("TB"), R("TB"), [[0, 8], [-1, 16]], A.is_ge, -1.0 / 128, 14, -1)
+    iota(R("sb"), [[512, 8]], 0)
+    oh = R("Id", 0, 8, p1=8)
+
+    def gates():
+        asel(R("OH"), R("ON", 0, 256, p1=8), [[-1, 8], [0, 32]], A.is_equal, 0.0, 0, 1)
+        for nm in ("RU", "RV", "RA"): iota(R(nm), [[0, SCRATCH[nm][1][1]]], 0)
+        iota(R("RU", p0=32, p1=33), [[0, 8], [-32768, 32]], 16384)
+        iota(R("RV", p0=32, p1=33), [[0, 256]], 32768)
+        iota(R("RV", 1, 256, 32, p0=32, p1=33), [[0, 8]], 0)
+        for nm in ("KT1", "KT2", "KT3"):
+            w = SCRATCH[nm][1][1]; asel(R(nm), R("ON", 0, w, p1=33), [[0, w]], A.is_equal, 0.0, -32, 1)
+        iota(R("CR", 0, 256), [[int(-4 * AL), 2], [0, 128]], int((-2 if SG_ON[3] == "v" else -3) * AL))
+        for j, st, base in ((0, 32, 0), (1, 16, 128), (2, 32, 0), (3, 32, 0)): iota(R("RA", 8 * j, 8 * j + 8, p0=32, p1=33), [[st, 8]], base)
+        for j in (0, 2, 3): asel(R("RA", 8 * j, 8 * j + 8, p1=8), R("ON", 0, 8, p1=8), [[-1, 8]], A.is_equal, 0.0, 0, 1)
+
+    late = {
+        "kg": gates,
+        "kth": lambda: (cp(R("thf", 0, 1), R("thi")), cp(col(4), R("wi")), mm([(Bk(4, 0, 1), R("G8"), R("thf", 0, 1))]), act(col(11), Bk(4, 0, 1)), act(col(12), Bk(4, 0, 1))),
+        "kPa": lambda: ([ts(R("Pa", 128 * (u - 1), 128 * u), R("eb"), float(u), A.is_equal, AL, A.mult) for u in range(1, 16)],
+                        asel(R("Pa"), R("Pa"), [[0, 15], [-1, 128]], A.not_equal, -AL, 0, 1)),
+        "kPn": lambda: act(R("Pn"), R("Pa", 0, 1024), scale=1.0 / AL),
+        "kc0": lambda: (ts(R("c0"), R("j16"), col(1), A.is_equal, 32768.0, A.mult), ts(R("e1"), R("j16"), col(14), A.is_equal, -16384.0, A.mult)),
+        "kc1": lambda: tt(R("c0"), R("c0"), R("e1"), A.add),
+        "kfp": lambda: (ts(R("fpl", 0, 4), R("fpi", 0, 4), col(7), A.add), ts(R("fpl", 4, 8), R("fpi", 4, 8), col(8), A.add), ts(R("sb"), R("sb"), col(13), A.add)),
+        "kSw": lambda: act(R("Sw"), R("Sn", 144, 288), scale=col(4)),
+        "kRB": lambda: [act(R("RB", 8 * j, 8 * j + 8), oh, scale=sc) for j, sc in enumerate((-1.0 / 64, 1.0, -1.0 / 8192, -32.0 / 8192))],
+        "kRU": lambda: (act(R("RU", p1=8), R("OH"), scale=32768.0), act(R("RV", 1, 256, 32, p1=8), oh, scale=32768.0), act(R("RE"), R("OH"), scale=-512.0)),
+    }
+
+    Xw, lw, pw, Id, ones = R("X"), R("ll"), R("pm"), R("Id"), R("ON", 0, 128, p1=1)
+    kv, ke, base = [R("KT%d" % c, 0, 128) for c in (1, 2, 3)], R("KT1", 128, 256, p1=8), R("CR", 256, 264)
+    pa, tq, rk, g1, g2, g4 = Bk(7, 0, 256), Bk(7, 256, 512), Bk(5, 0, 128), Bk(6, 0, 256), Bk(6, 256, 512), Bk(4, 256, 512)
+    lane = R("sc", 15, 128, 16)
+
+    def steps(t):
+        cu, nb, nu, mo = "Cu%d" % t, "nb%d" % t, "Nu%d" % t, "mo%d" % t
+        nn, Mm = R(nb, 0, 128), R(nb, 128, 256)
+        st = {}
+        def Q(nm, q, a=0, b=1024): return R(nm, 1024 * q + a, 1024 * q + b)
+        def L(nm, q, a=0, b=64): return R(nm, 64 * q + a, 64 * q + b)
+        st["pa"] = lambda: ts(pa, R("Pi"), 1184.0, A.add)
+        st["pb"] = lambda: ts(R("i2"), R("Pi"), 63, A.bitwise_and)
+        st["pc"] = lambda: ts(R("pc"), R("i2"), 2048.0, A.mult, 27648.0, A.add)
+        st["tqa"] = lambda: (act(R("tq"), pa, bias=2912.0), mm([(tq, R("Idf"), R("tq"))], True, False))
+        st["cm"] = lambda: ts(R("Cf"), R(cu), -2016.0, A.add)
+        st["i1"] = lambda: tt(pa, pa, R("Cf"), A.mult)
+        st["ib"] = lambda: tt(R("i2"), pa, R("pc"), A.add)
+        st["hh"] = lambda: ts(R("hh"), R("i2"), 5, A.arith_shift_right, 4095, A.bitwise_and)
+        st["Cm"] = lambda: act(R("Cm"), R("Cf"), bias=-2080.0)
+        st["nT"] = lambda: (mm([(Bk(6, 128 * h, 128 * h + 128, p1=64), R(nb, 64 * h, 64 * h + 64), Id) for h in range(2)], alone=True),
+                            act(R("nT"), Bk(6, 0, 256, p1=64), scale=-1.0))
+        st["sums"] = lambda: t == RO - 1 and (mm([(Bk(4, 0, 128), Id, R("X", k, 4096, 32)) for k in range(32)]), act(R("ox"), Bk(4, 0, 128)))
+
+        def sums(q, terms, first, last):
+            b, c = SUB[q]
+            for j, (a, o, x) in enumerate(terms):
+                mm([(Bk(b, c, c + 64), R(a, o + 15 - s, o + 143 - s), R(x, 1024 * q + s, 1024 * q + 1024, 16)) for s in range(16)],
+                   first and j == 0, last and j == len(terms) - 1)
+
+        for q in range(4):
+            st["x%dv" % q] = lambda q=q: cp(Q("xg", q), IX(Xw, L("Pu", q)))
+            st["x%ds" % q] = lambda q=q: act(Q("xg", q), IX(Xw, L("Pu", q)), F.Copy)
+            st["d%d" % q] = lambda q=q: tt(Q("dg", q), IX(Xw, L(cu, q)), Q("xg", q), A.subtract)
+            for j in range(2):
+                st["d%d%s" % (q, "ab"[j])] = lambda q=q, j=j: tt(Q("dg", q, 512 * j, 512 * j + 512), IX(Xw, L(cu, q, 32 * j, 32 * j + 32)),
+                                                                 Q("xg", q, 512 * j, 512 * j + 512), A.subtract)
+            st["r%ds" % q] = lambda q=q: act(Q("rg", q), Q("dg", q), F.Relu)
+            st["r%dv" % q] = lambda q=q: ts(Q("rg", q), Q("dg", q), 0.0, A.max)
+            st["su%da" % q] = lambda q=q: sums(q, [("Sn", 0, "dg")], True, False)
+            st["su%db" % q] = lambda q=q: sums(q, [("S2", 0, "rg")], False, True)
+            st["nk%d" % q] = lambda q=q: ts(L("nk", q), Bk(SUB[q][0], SUB[q][1], SUB[q][1] + 64), col(12), A.is_gt, 4096.0, A.mult)
+            st["hp%d" % q] = lambda q=q: tt(L("hp", q), L("hh", q), L("nk", q), A.max)
+            st["Hu%d" % q] = lambda q=q: cp(L("Hu", q), L("hp", q))
+            st["z%d" % q] = lambda q=q: act(Q("zg", q), IX(Xw, L("Hu", q)), F.Copy)
+            st["pm%d" % q] = lambda q=q: scan(Q("pm", q, 16, 1040), R("ctl"), Q("ll", q, 16, 1040), A.add, A.min)
+            for j in range(2):
+                st["pm%d%s" % (q, "ab"[j])] = lambda q=q, j=j: scan(Q("pm", q, 16 + 512 * j, 528 + 512 * j), R("ctl", 0, 512), Q("ll", q, 16 + 512 * j, 528 + 512 * j), A.add, A.min)
+        st["y1"] = lambda: act(Q("dg", 1), IX(Xw, L(cu, 1)), F.Copy)
+        st["dx"] = lambda: [mm([(Bk(6 - j), R("In"), Q("xg", 1, 512 * j, 512 * j + 512))], True, False) for j in range(2)]
+        st["dy"] = lambda: [mm([(Bk(6 - j), Id, Q("dg", 1, 512 * j, 512 * j + 512))], False, True) for j in range(2)]
+        for j in range(2): st["r1" + "ab"[j]] = lambda j=j: act(Q("rg", 1, 512 * j, 512 * j + 512), Bk(6 - j), F.Relu)
+        st["su1"] = lambda: sums(1, [("Sn", 144, "xg"), ("Sn", 0, "dg"), ("S2", 0, "rg")], True, True)
+        st["tqb"] = lambda: mm([(tq, R("In"), R("nk"))], False, True)
+        st["AA"] = lambda: tt(R("AA", 8, 264), tq, R("hp"), A.min)
+        for j in (1, 2, 3):
+            st["A%d" % j] = lambda j=j: act(R("A%d" % j), R("AA"), bias=4096.0 * j)
+
+        def mx(i8, parts):
+            h, b = i8 // 4, i8 % 4
+            for part in parts:
+                trip = []
+                for s in range(4 * b, 4 * b + 4):
+                    o = Bk(b, 128 * (s % 4), 128 * (s % 4) + 128)
+                    if part == 2: trip.append((o, R("Bm", 128 * s, 128 * s + 128), R("nk", 128 * h, 128 * h + 128)))
+                    else: trip.append((o, Id, R(("xg", "rg")[part], 2048 * h + s, 2048 * h + 2048, 16)))
+                mm(trip, part == 0, part == 2)
+
+        def lmin(i8):
+            h, b = i8 // 4, i8 % 4
+            trip = [(R("ll", 16 + 2048 * h + 128 * s, 144 + 2048 * h + 128 * s), Bk(b, 128 * (s % 4), 128 * (s % 4) + 128),
+                     R("zg", 2048 * h + s, 2048 * h + 2048, 16)) for s in range(4 * b, 4 * b + 4)]
+            add("v", [r for x in trip for r in rgs(x[1], x[2])], [r for x in trip for r in rgs(x[0])],
+                [(lambda x=x: V.tensor_tensor(x[0]["ap"], x[1]["ap"], x[2]["ap"], A.min)) for x in trip])
+        for i in range(8):
+            h, c, bk, e0 = i // 4, i % 4, Bk(PMB[i]), 512 * i
+            for nm, parts in (("xa", (0,)), ("mr", (1,)), ("mw", (2,)), ("mx", (0, 1, 2))): st["%s%d" % (nm, i)] = lambda i=i, parts=parts: mx(i, parts)
+            st["l%d" % i] = lambda i=i: lmin(i)
+            st["nn%d" % i] = lambda h=h, c=c, bk=bk: mm([(bk, R("nT", 128 * h, 128 * h + 128), R("nS", 512 * c, 512 * c + 512))], True, False)
+            st["pq%d" % i] = lambda e0=e0, bk=bk: mm([(bk, Id, R("pm", 16 + e0, 528 + e0))], False, True)
+            st["in%d" % i] = lambda e0=e0, bk=bk: act(R("ind", e0, e0 + 512), bk, F.Sign, bias=0.5)
+            st["ct%d" % i] = lambda h=h, c=c: mm([(Bk(5, 256 + 128 * h + s, 384 + 128 * h, 16), R("ind", 2048 * h + 128 * s, 2048 * h + 128 * s + 128), R("G1"))
+                                                  for s in range(4 * c, 4 * c + 4)], alone=True)
+            st["fs%d" % i] = lambda e0=e0: scan(R("zg", e0, e0 + 512), R("ct0"), R("ind", e0, e0 + 512), A.mult, A.add)
         for h in range(2):
-            cp(T.RA[0:8, 24 * c + 8 * h:24 * c + 8 * h + 8], oh, 8, ["Id", "RA"], ["RA%d%d" % (c, h)])
-        iota(T.RA[32:33, 24 * c:24 * c + 8], [[2048, 2], [32, 4]], 0, 0, 8, ["RAx%d" % c], r=["RA"])
-        iota(T.RA[32:33, 24 * c + 8:24 * c + 16], [[32, 8]], 0, 0, 8, ["RAy%d" % c], r=["RA"])
-        iota(T.RA[32:33, 24 * c + 16:24 * c + 24], [[16 if c == 0 else 0, 8]], 128 if c == 0 else 0, 0, 8, ["RAz%d" % c], r=["RA"])
-    def rak(c): return ["RA%d0" % c, "RA%d1" % c, "RAx%d" % c, "RAy%d" % c, "RAz%d" % c]
-    for j, sc in enumerate((1.0, 1.0, -1.0 / 64, 1.0, 1.0, 1.0 / 8192)):
-        ts(T.RB[:, 8 * j:8 * j + 8], oh, sc, None, A.mult, None, 8, ["Id"], ["RB%d" % j])
-    for nm, sc in (("RUa", 32768.0), ("RX", 4.0)):
-        ms(T[nm][:], 0.0, 128, [nm + "0"])
-        ts(T[nm][0:8, :], T.OH[:], sc, None, A.mult, None, 128, ["OH", nm + "0"], [nm + "1"])
-    iota(T.RUa[32:33, :], [[0, 8], [-32768, 32]], 16384, 0, 256, ["RUa2"], r=["RUa0"])
-    for c in (1, 2): iota(T.RUb[0:1, 256 * c - 256:256 * c], [[8192 * c, 2], [0, 128]], 0, 0, 256, ["RUb%d" % c])
-    iota(T.RUb[0:1, 512:520], [[2048, 2], [32, 4]], 0, 0, 8, ["RUb0"])
-    iota(T.RX[32:33, :], [[0, 256]], -16384, 0, 256, ["RX2"], r=["RX0"])
-    ts(T.RE[:], T.OH[:], -256.0, None, A.mult, None, 128, ["OH"], ["RE"])
-    ts(T.RF[:], T.OH[:], -4.0, None, A.mult, None, 128, ["OH"], ["RF"])
-    for c in (1, 2, 3):
-        ms(T["KT%d" % c][:], 0.0, 128, ["KT%d" % c, "K0%d" % c])
-        iota(T["KT%d" % c][32:33, :], [[0, 256]], 1, 0, 256, ["K1%d" % c], r=["K0%d" % c])
-    ms(T.X[:, 4096:4112], 255.0, 8, ["Xp"])
-    ms(T.ll[:, 4096:4112], 255.0, 8, ["lp"])
-    ms(T.pm[:, 4096:4112], 255.0, 8, ["pp"])
-    ms(T.AA[:, 0:8], 0.0, 8, ["A0"])
-    ms(T.AA[:, 264:272], 0.0, 8, ["Ap"])
-    cp(T.thf[:, 0:1], T.thi[:], 1, ["thi"], ["thf"])
-    mm(grp(B[6][:, 0:1], [(T.G8[:], T.thf[:, 0:1])]), 256, ["G8", "thf"], [], [6])
-    cp(col(11), B[6][:, 0:1], 1, [], ["c11"], [6])
-    cp(col(12), col(11), 1, ["c11"], ["thr"])
-    for r in range(8):
-        cp(T.Pu[:, 32 * r:32 * r + 32], T.pin[:, r:256:8], 32, ["pin"], ["Pu%d" % (r // 2) + "ab"[r % 2]])
-        cp(T.Cu0[:, 32 * r:32 * r + 32], T.cin[:, r:256:8], 32, ["cin"], ["Cu0_%d" % r])
-    pu = [["Pu%da" % qn, "Pu%db" % qn] for qn in range(4)]
-    allpu = [k for x in pu for k in x]
-    cp(T.Pi[:], T.Pu[:], 256, allpu, ["Pi"])
-    XK = ["Xa", "Xb", "Xp"]
-    Xw = T.X[:, 0:4112]
-    nsent = 0
+            st["mK%d" % h] = lambda h=h: ts(R("mK", 128 * h, 128 * h + 128), Bk(5, 256 + 128 * h, 384 + 128 * h), 0.0, A.is_gt)
+        st["f0"] = lambda: mm([(Bk(2, 256, 320), Id, R("ind", k, 2048, 32)) for k in range(32)])
+        st["fc"] = lambda: act(R("zg", 0, 64), Bk(2, 256, 320))
+        st["fb"] = lambda: act(R("fb"), IX(R("zg"), R("fpl")), bias=0.25, scale=1.0 / 128)
+        for b in range(4): st["TB%d" % b] = lambda b=b: mm([(Bk(b, 0, 256), R("TB"), R("TR", 256 * b, 256 * b + 256))], True, False)
+        st["k1a"] = lambda: mm([(Bk(7, 0, 8), ones, base), (Bk(7, 0, 4), R("mK", 0, 128), R("LE", 12, 16))], True, False)
+        st["k1b"] = lambda: mm([(Bk(7, 4, 8), R("mK", 128, 256), R("LE", 12, 16))], False, True)
+        st["ul0"] = lambda: ts(R("ul", 0, 8), Bk(7, 0, 8), col(9), A.add, 4112.0, A.min)
+        st["k1m"] = lambda: [mm([(Bk(4, 128 * j, 128 * j + 128, p1=8), R(a, 4 - 4 * h, 12 - 4 * h), R("mK", 128 * h, 128 * h + 128)) for h in range(2)])
+                             for j, a in enumerate(("L1", "LE"))]
+        st["KT1"] = lambda: act(R("KT1", p1=8), Bk(4, 0, 256, p1=8))
 
-    for t in range(RO):
-        Cu, nb = T["Cu%d" % t], T["nb%d" % t]
-        ck = ["Cu0_%d" % r for r in range(8)] if t == 0 else ["C%d" % t]
-        nn, nkey, mkey = nb[:, 0:128], "n%d" % t, "M%d" % t
-        pri[0] = PH; rnd[0] = t
-        X_E, R_E = (X_ON0, R_ON0) if t == 0 else (X_ON, R_ON)
-        ts(B[7][:, 0:256], T.Pi[:], 1184.0, None, A.add, None, 256, ["Pi"], ["pa"], [7])
-        ts(T.i2[:], T.Pi[:], 63, None, A.bitwise_and, None, 256, ["Pi"], ["pb", "i2"])
-        ts(B[7][:, 256:512], T.i2[:], 2048.0, 27648.0, A.mult, A.add, 256, ["i2"], ["pc"], [7])
-        ts(T.Cf[:], Cu[:], -2016.0, None, A.add, None, 256, ck, ["cm", "Cf"])
-        tt(T.i1[:], B[7][:, 0:256], T.Cf[:], A.mult, 256, ["pa", "Cf"], ["i1"], [7])
-        tt(T.i2[:], B[7][:, 256:512], T.i1[:], A.add, 256, ["pc", "i1"], ["ib", "i2"], [7])
-        ts(T.hh[:], T.i2[:], 5, 4095, A.arith_shift_right, A.bitwise_and, 256, ["i2"], ["hh"])
-        pri[0] = 0.0
-        act(T.Cf[:], T.Cf[:], F.Identity, 256, ["Cf"], ["Cf"], bias=2016.0)
-        mm([(B[6][0:64, 128 * h:128 * h + 128], nb[:, 64 * h:64 * h + 64], T.Id[:], True, True) for h in range(2)], 256, [nkey, "Id"], [], [6])
-        act(T.nT[:], B[6][0:64, 0:256], F.Identity, 256, [], ["nT"], [6], scale=-1.0)
-        for qn in range(4):
-            e, li = slice(1024 * qn, 1024 * qn + 1024), slice(64 * qn, 64 * qn + 64)
-            xk, dk, rk = "x%d" % qn, "d%d" % qn, "r%d" % qn
-            if X_E[qn] == "s": act(T.xg[:, e], Xw.indirect(T.Pu[:, li]), F.Copy, 1024 * GC, XK + pu[qn], [xk])
-            else: cp(T.xg[:, e], Xw.indirect(T.Pu[:, li]), 1024 * GC + 40, XK + pu[qn], [xk])
-            ym = R_E[qn] == "y"
-            pm_ = R_E[qn] == "p"
-            if pm_: act(T.dg[:, e], Xw.indirect(Cu[:, li]), F.Copy, 1024 * GC, XK + ck, [dk])
-            else: tt(T.dg[:, e], Xw.indirect(Cu[:, li]), T.xg[:, e], A.max if ym else A.subtract, 1024 * GC + 40, XK + ck + [xk], [dk])
-            if pm_:
-                for j in range(2):
-                    e2 = slice(1024 * qn + 512 * j, 1024 * qn + 512 * j + 512)
-                    mm([(B[j][:], T.In[:], T.xg[:, e2], True, False)], 512, ["In", xk], [], [j])
-                    mm([(B[j][:], T.Id[:], T.dg[:, e2], False, True)], 512, ["Id", dk], [], [j])
-                    act(T.rg[:, e2], B[j][:], F.Relu, 512, [], [rk], [j])
-            elif ym: act(T.rg[:, e], Xw.indirect(Cu[:, li]), F.Copy, 1024 * GC, XK + ck, [rk])
-            elif R_E[qn] == "s": act(T.rg[:, e], T.dg[:, e], F.Relu, 1024, [dk], [rk])
-            else: ts(T.rg[:, e], T.dg[:, e], 0.0, None, A.max, None, 512, [dk], [rk])
-            bk = 4 + qn % 2
-            so = B[bk][:, 0:64]
-            terms = ((T.Sn, T.xg, xk), (T.Sn, T.rg, rk), (T.S2, T.dg, dk)) if ym else ((T.Sn, T.dg, dk), (T.S2, T.rg, rk))
-            if pm_: terms = ((None, T.xg, xk),) + terms
-            gl = grp(so, [(T.Sn[:, 159 - s:287 - s] if a is None else a[:, 15 - s:143 - s], c[:, 1024 * qn + s:1024 * qn + 1024:16])
-                          for a, c, k in terms for s in range(16)])
-            for j, (a, c, k) in enumerate(terms):
-                mm(gl[16 * j:16 * j + 16], 1024, [k, "Sn", "S2", "S1"], ["su%d%s" % (qn, "ab"[j == len(terms) - 1])], [bk])
-            pri[0] = PN
-            ts(T.nk[:, li], so, col(12), 4096.0, A.is_gt, A.mult, 64, ["thr"], ["nk%d" % qn], [bk])
-            tt(T.hp[:, li], T.hh[:, li], T.nk[:, li], A.max, 128, ["hh", "nk%d" % qn], ["hp%d" % qn])
-            cp(T.Hu[:, li], T.hp[:, li], 64, ["hp%d" % qn], ["Hu%d" % qn])
-            pri[0] = 0.0
-            act(T.zg[:, e], Xw.indirect(T.Hu[:, li]), F.Copy, 1024 * GC, XK + ["Hu%d" % qn], ["z%d" % qn])
-        nks, hps = ["nk%d" % i for i in range(4)], ["hp%d" % i for i in range(4)]
-        for h in range(2):
-            qa, qb = 2 * h, 2 * h + 1
-            for sb4 in range(4):
-                bk = MXB[h][sb4]; lst = []
-                for s in range(4 * sb4, 4 * sb4 + 4):
-                    st = slice(2048 * h + s, 2048 * h + 2048, 16)
-                    lst += grp(B[bk][:, 128 * (s % 4):128 * (s % 4) + 128],
-                               ([(T.Id[:], T.dg[:, st])] if R_E[qa] == "y" else [(T.Id[:], T.xg[:, st]), (T.Id[:], T.rg[:, st])])
-                               + [(T.Bm[:, 128 * s:128 * s + 128], T.nk[:, 128 * h:128 * h + 128])])
-                mm(lst, 128 * len(lst), ["Id", "Bm"] + ["%s%d" % (a, x) for a in ("x", "r", "d", "nk") for x in (qa, qb)], ["mx%d" % (4 * h + sb4)], [bk])
-                fs = [(lambda s=s, bk=bk, h=h: V.tensor_tensor(T.ll[:, 2048 * h + 128 * s:2048 * h + 128 * s + 128], B[bk][:, 128 * (s % 4):128 * (s % 4) + 128],
-                                                              T.zg[:, 2048 * h + s:2048 * h + 2048:16], A.min)) for s in range(4 * sb4, 4 * sb4 + 4)]
-                add("v", 4 * vc(128), ["z%d" % qa, "z%d" % qb], ["l%d" % (4 * h + sb4)], fs, [bk])
-            for c in range(2):
-                e = slice(2048 * h + 1024 * c, 2048 * h + 1024 * c + 1024)
-                scan(T.pm[:, e], T.ctl[:], T.ll[:, e], A.add, A.min, 512, ["ctl", "l%d" % (4 * h + 2 * c), "l%d" % (4 * h + 2 * c + 1)], ["pm%d" % (2 * h + c)])
-            for c in range(4):
-                i8 = 4 * h + c; bk = PMB[i8]; e = slice(512 * i8, 512 * i8 + 512)
-                gl = grp(B[bk][:], [(T.nT[:, 128 * h:128 * h + 128], T.nS[:, 512 * c:512 * c + 512]), (T.Id[:], T.pm[:, e])])
-                mm(gl[:1], 512, ["nT", "nS"], ["nn%d" % i8], [bk])
-                mm(gl[1:], 512, ["Id", "pm%d" % (i8 // 2)], ["pq%d" % i8], [bk])
-                act(T.ind[:, e], B[bk][:], F.Sign, 512, [], ["in%d" % i8], [bk], bias=0.5)
-                pri[0] = PC / 5
-                mm([(B[5][:, 256 + 128 * h + s:256 + 128 * h + 128:16], T.ind[:, 2048 * h + 128 * s:2048 * h + 128 * s + 128], T.G1[:], True, True)
-                    for s in range(4 * c, 4 * c + 4)], 256, ["in%d" % i8, "G1"], ["ct%d" % i8], [5])
-                pri[0] = 0.0
-            pri[0] = PC
-            ts(T.mK[:, 128 * h:128 * h + 128], B[5][:, 256 + 128 * h:256 + 128 * h + 128], 0.0, None, A.is_gt, None, 128, [], ["mK%d" % h], [5])
-            pri[0] = 0.0
-        lk, pmk = ["l%d" % i for i in range(8)] + ["lp"], ["pm%d" % i for i in range(4)] + ["pp"]
-        for j, (a0, a1) in enumerate(FCH):
-            e = slice(512 * a0, 512 * a1)
-            scan(T.zg[:, e], T.ct0[:, 0:512 * (a1 - a0)], T.ind[:, e], A.mult, A.add, 256 * (a1 - a0),
-                 ["cz"] + ["in%d" % i for i in range(a0, a1)], ["fs%d" % j, "z%d" % (a0 // 2)])
-        act(T.f1[:], T.zg[:, 0:4096].indirect(T.fpl[:]), F.Identity, 128 * GC, ["fpl"] + ["z%d" % i for i in range(4)], ["f1"], bias=17.0, scale=0.5)
-        act(T.nk2[:], T.nk[:], F.Identity, 256, nks, ["nkc"], bias=2912.0, scale=-1.0)
-        tt(B[7][:, 0:256], B[7][:, 0:256], T.nk2[:], A.add, 256, ["pa", "nkc"], ["tq"], [7])
-        tt(T.AA[:, 8:264], B[7][:, 0:256], T.hp[:], A.min, 256, hps + ["tq"], ["AA"], [7])
-        act(T.A3[:], T.AA[:], F.Identity, 272, ["AA", "A0", "Ap"], ["A3"], bias=12288.0)
-        act(T.A1[:], T.AA[:, 0:264], F.Identity, 264, ["AA", "A0"], ["A1"], bias=4096.0)
-        act(T.A2[:], T.AA[:, 0:264], F.Identity, 264, ["AA", "A0"], ["A2"], bias=8192.0)
-        KT = [T.KT1, T.KT2, T.KT3]; uu = [T.u1, T.u2, T.u3]
+        def pairs(src, mat, last):
+            for b in range(4):
+                mm([(Bk(b, 128 * j, 128 * j + 128), R(mat, 128 * (2 * b + j), 128 * (2 * b + j) + 128), src) for j in range(2)], False, last)
 
-        def offsets(c):
-            o = B[7][:, 32 * c:32 * c + 24]; rb = 0 if c == 0 else 24
-            lst = [(o, KT[c][0:33, 0:128], T.RA[:, 24 * c:24 * c + 24], True, False)]
-            if c == 1: lst.append((B[7][:, 32:48], T.KT1[0:8, 128:256], T.RB[:, 0:16], False, False))
-            if c == 2: lst.append((B[7][:, 72:80], T.KT1[0:8, 128:256], T.RB[:, 48:56], False, False))
-            lst.append((o, KT[c][0:8, 128:256], T.RB[:, rb:rb + 24], False, True))
-            pri[0] = PO if c == 0 else 0.0
-            mm(lst, 192, ["KT%d" % (c + 1), "K1%d" % (c + 1), "KT1"] + rak(c) + ["RB%d" % j for j in range(7)], ["of%d" % c], [7])
-            pri[0] = 0.0
-            if c: ts(uu[c][:, 0:8], B[7][:, 32 * c:32 * c + 8], col(8 + c), 4096.0, A.add, A.min, 8, ["c%d" % (8 + c)], ["ul%d" % c], [7])
-            ts(uu[c][:, 8:16], B[7][:, 32 * c + 8:32 * c + 16], (8.0, 7.0, 6.0)[c], 264.0, A.add, A.min, 8, [], ["un%d" % c], [7])
+        def sign(b, c):
+            o = R("sg", 256 * b, 256 * b + 256)
+            if SG_ON[b] == "s": act(o, Bk(b, 0, 256), F.Sign)
+            else: ts(o, Bk(b, 0, 256), c - 1.0, A.is_gt, 2.0, A.mult)
 
-        def front(c, dst):
-            tt(T.gd[:], T.A3[:, 0:272].indirect(uu[c][:, 8:16]), T.dia[:], A.mult, 128 * GC + 40, ["A3", "un%d" % c, "dia"], ["gd"])
-            scan(dst[:], T.c16[:], T.gd[:], A.mult, A.add, 128, ["c16", "gd"], ["s%d" % min(c, 1)])
+        def ranks(b):
+            mm([(rk, R("Pa", 128 * (14 - j), 128 * (15 - j)) if j < 7 else R("Ia"), R("sg", 128 * j, 128 * j + 128)) for j in (2 * b, 2 * b + 1)], False, b == 3)
+        st["pf"] = lambda: pairs(R("fb"), "Pn", False)
+        st["pb1"] = lambda: pairs(R("b1"), "Pn", True)
+        st["ps"] = lambda: [mm([(Bk(b, 0, 256), Id, R("sg", 256 * b, 256 * b + 256))], True, False) for b in range(4)]
+        st["pb2"] = lambda: pairs(R("b2"), "Pa", True)
+        for c in (1, 2):
+            lo = Bk(7, 8 * c, 8 * c + 8)
+            st["b%d" % c] = lambda c=c: tt(R("b%d" % c), IX(lw, R("ul", 8 * c - 8, 8 * c)), nn, A.is_ge)
+            st["e%d" % c] = lambda c=c: act(R("e%d" % c), IX(lw, R("ul", 8 * c - 8, 8 * c)), F.Abs)
+            st["rk%d" % c] = lambda c=c: mm([(rk, ones, R("CR", 128 * c - 128, 128 * c)), (rk, R("I64"), R("fb"))] + [(rk, R("I4"), R("b1"))] * (c - 1), True, False)
+            st["rv%d" % c] = lambda c=c: mm([(rk, R("I4"), R("b%d" % c))], False, False)
+            for b in range(4):
+                st["sg%d%s" % (c, "abcd"[b])] = lambda b=b, c=c: sign(b, c)
+                st["rs%d%s" % (c, "abcd"[b])] = lambda b=b: ranks(b)
+            st["lo%d" % c] = lambda c=c, lo=lo: mm([(lo, ones, base), (lo, ke, R("RB", 8 * c, 8 * c + 8))], True, False)
+            st["q%d" % c] = lambda: ts(R("qq"), rk, LO, A.max, HI, A.min)
+            st["ls%d" % c] = lambda lo=lo: mm([(lo, R("Sn", 159 - s, 287 - s), R("qq", s, 128, 16)) for s in range(16)], False, True)
+            st["kt%d" % c] = lambda: mm([(Bk(4, s, 128, 16, p1=8), R("qq", s, 128, 16), R("G1")) for s in range(16)], alone=True)
+            st["ul%d" % c] = lambda c=c, lo=lo: ts(R("ul", 8 * c, 8 * c + 8), lo, col(10), A.add, 4112.0, A.min)
+            st["KT%d" % (c + 1)] = lambda c=c: act(R("KT%d" % (c + 1), p1=8), Bk(4, 0, 128, p1=8), F.Relu, bias=QC + 1)
+        st["e3"] = lambda: tt(R("e3"), R("e1"), R("e2"), A.min)
+        st["M"] = lambda: tt(Mm, IX(pw, R("ul", 16, 24)), R("e3"), A.min)
+        st["of0"] = lambda: mm([(Bk(7, 32, 48), kv[0], R("RA", 0, 16)), (Bk(7, 40, 48), ke, R("RB", 0, 8))])
+        st["of1"] = lambda: mm([(Bk(7, 48, 56), kv[1], R("RA", 16, 24))])
+        st["of2"] = lambda: mm([(Bk(7, 56, 64), kv[2], R("RA", 24, 32)), (Bk(7, 56, 64), ke, R("RB", 24, 32))])
+        st["um"] = lambda: ts(R("un", 24, 32), Bk(7, 40, 48), col(1), A.add)
+        for c in range(3):
+            at = (32, 48, 56)[c]
+            st["un%d" % c] = lambda c=c, at=at: ts(R("un", 8 * c, 8 * c + 8), Bk(7, at, at + 8), 7.0 if c else 8.0, A.add)
+            st["fr%d" % c] = lambda c=c: act(R("gd"), IX(R("A3"), R("un", 8 * c, 8 * c + 8)), F.Copy)
+            st["sc%d" % c] = lambda: scan(R("sc"), R("c0"), R("gd"), A.add, A.min)
+            st["pt%d" % c] = lambda c=c: ts(R("A3", 7 - c, 263 - c, 32), lane, col(15), A.add)
+        st["g1"] = lambda: mm([(g1, kv[0], R("RU")), (g1, ke, R("RE"))])
+        for j, gj in ((1, g1), (2, g2)): st["t%d" % j] = lambda j=j, gj=gj: tt(gj, gj, R("A%d" % j, 8 - j, 264 - j), A.min)
+        st["o1"] = lambda: tt(R("o1"), g1, R("AA", 8, 264), A.max)
+        st["g2"] = lambda: mm([(g2, kv[1], R("RU")), (g2, ke, R("RE"))])
+        st["o2"] = lambda: tt(R("o2"), g2, R("o1"), A.max)
+        st["g3a"] = lambda: mm([(g1, kv[1], R("RV")), (g1, ke, R("RE"))], True, False)
+        st["g3b"] = lambda: mm([(g1, kv[2], R("RU"))], False, True)
+        st["t3"] = lambda: tt(g1, g1, R("A3", 5, 261), A.min)
+        st["i3"] = lambda: tt(R("i3"), g1, R("o2"), A.max)
+        st["Ni"] = lambda: ts(R("Ni"), R("i3"), 4095, A.bitwise_and)
+        st["Nu"] = lambda: cp(R(nu), R("Ni"))
+        st["Nu0"] = lambda: ts(R(nu, 0, 256, 32), lane, col(16), A.add)
+        st["g4"] = lambda: mm([(g4, kv[1], R("RV")), (g4, kv[2], R("RU"))])
+        st["t4"] = lambda: tt(g4, g4, R("Cm"), A.max)
+        st["i4"] = lambda: tt(R("i4"), g4, R("i3"), A.min)
+        st["i40"] = lambda: ts(R("i4", 0, 256, 32), lane, col(16), A.add)
+        st["Pi"] = lambda: ts(R("Pi"), R("i4"), 4095, A.bitwise_and)
+        st["Pu"] = lambda: cp(R("Pu" if t < RO - 1 else "pq"), R("Pi"))
+        st["th1"] = lambda: t < RO - 1 and (
+            add("s", rgs(ke), rgs(R("nT", 0, 128, p1=8), R("thf", 1, 2)),
+                [lambda: S.activation(T.nT[0:8, 0:128], T.KT1[0:8, 128:256], F.Identity, accum_out=T.thf[:, 1:2])]),
+            mm([(Bk(2, 256, 257), R("ONf"), R("thf", 1, 2))]))
+        st["th2"] = lambda: t < RO - 1 and ts(R("ti", 0, 1), Bk(2, 256, 257), 1.0 / 8192, A.mult)
+        st["th3"] = lambda: t < RO - 1 and ts(R("ti", 1, 2), R("ti", 0, 1), 63, A.bitwise_and)
+        st["th4"] = lambda: t < RO - 1 and tt(col(12), R("ti", 1, 2), col(11), A.add)
+        st["Sw"] = lambda: mm([(Bk(7, 64, 72), R("Sw", 15 - s, 143 - s), R(nb, 128 + s, 256, 16)) for s in range(16)])
+        st["vv"] = lambda: mm([(rk, Id, nn), (rk, Id, Mm)])
+        st["si0"] = lambda: cp(R("si", 0, 8), Bk(7, 64, 72))
+        st["si1"] = lambda: ts(R("si", 8, 16), R("si", 0, 8), 31, A.bitwise_and)
+        st["si2"] = lambda: tt(R("si", 16, 24), R("si", 8, 16), R("sb"), A.add)
+        st["us"] = lambda: cp(R("us"), R("si", 16, 24))
+        st["v2"] = lambda: ts(R("v2"), rk, 0.5, A.mult, -0.25, A.add)
 
-        def cut(src, sk, c):
-            for hb in range(2):
-                lst = [(B[hb][:], T.TB[:], T.TR[:, 512 * hb:512 * hb + 512], True, False)]
-                lst += [(B[hb][:, 128 * j:128 * j + 128], T.Pm[:, 128 * (4 * hb + j):128 * (4 * hb + j) + 128], src, False, j == 3) for j in range(4)]
-                mm(lst[:1], 512, ["TB", "TR"], [], [hb])
-                mm(lst[1:], 512, ["Pm", sk], [], [hb])
-            prs = [(T.Id[:], T.ON[:, 0:128])]
-            if c == 2:
-                act(T.f2[:], src, F.Relu, 128, [sk], ["f2"], bias=-1.0); src, sk = T.f2[:], "f2"
-                prs.append((T.I64[:], T.ON[:, 0:128]))
-            act(T.sg[:, 0:512], B[0][:], F.Sign, 512, [], ["sg0"], [0])
-            ts(T.sg[:, 512:1024], B[1][:], 0.0, 2.0, A.is_gt, A.mult, 512, [], ["sg1"], [1])
-            prs.append((T.Id[:], T.ON[:, 0:128]))
-            prs.append((T.I64[:], src))
-            prs += [(T.Pm[:, 128 * (14 - j):128 * (15 - j)] if j < 7 else T.In[:], T.sg[:, 128 * j:128 * j + 128]) for j in range(8)]
-            gl = grp(B[5][:, 0:128], prs)
-            mm(gl[:-8], 384, ["Id", "ON", "I64", sk], [], [5])
-            mm(gl[-8:-4], 512, ["Pm", "sg0"], [], [5])
-            mm(gl[-4:], 512, ["Pm", "In", "sg1"], [], [5])
-            ts(T.qq[:], B[5][:, 0:128], -40.0 / 64, 35.0 / 64, A.max, A.min, 128, [], ["qq"], [5])
-            if c == 1:
-                gl = grp(B[7][:, 104:112], [(T.ON[0:1, 0:128], T.RUb[0:1, 512:520]), (T.KT1[0:8, 128:256], T.RB[:, 0:8])]
-                         + [(T.Sw[:, 159 - s:287 - s], T.qq[:, s:128:16]) for s in range(16)])
-                mm(gl[:2], 128, ["K11", "ON", "RUb0", "KT1", "RB0"], [], [7])
-                mm(gl[2:], 1024, ["S64", "qq"], [], [7])
-                ts(T.us[:, 8:16], B[7][:, 104:112], col(7), 4096.0, A.add, A.min, 8, ["c7"], ["ud"], [7])
-            mm([(B[4][0:8, 0:256], T.ON[0:1, 0:8], T.RUb[0:1, 256 * c - 256:256 * c], True, False)], 256, ["K11", "ON", "RUb%d" % c], [], [4])
-            mm([(B[4][0:8, s:256:16], T.qq[:, s:128:16], T.G64[:], False, s == 15) for s in range(16)], 16 * 24, ["qq", "G64a", "G64b"], [], [4])
-            if KT_ON[c] == "s": act(KT[c][0:8, :], B[4][0:8, 0:256], F.Relu, 256, [], ["KT%d" % (c + 1)], [4])
-            else: ts(KT[c][0:8, :], B[4][0:8, 0:256], 0.0, None, A.max, None, 256, [], ["KT%d" % (c + 1)], [4])
-            offsets(c)
-
-        lst = grp(B[4][0:8, 0:128], [(T.L1[:, 4 - 4 * h:12 - 4 * h], T.mK[:, 128 * h:128 * h + 128]) for h in range(2)])
-        lst += grp(B[4][0:8, 128:256], [(T.LE[:, 4 - 4 * h:12 - 4 * h], T.mK[:, 128 * h:128 * h + 128]) for h in range(2)])
-        mm([(B[7][:, 96:104], T.ON[0:1, 0:128], T.RUb[0:1, 512:520], True, False), (B[7][:, 96:100], T.mK[:, 0:128], T.LE[:, 12:16], False, False)],
-           128, ["K11", "ON", "RUb0", "LD", "mK0"], [], [7])
-        mm([(B[7][:, 100:104], T.mK[:, 128:256], T.LE[:, 12:16], False, True)], 64, ["LD", "mK1"], ["k1d"], [7])
-        ts(T.u1[:, 0:8], B[7][:, 96:104], col(8), 4096.0, A.add, A.min, 8, ["c8"], ["ul0"], [7])
-        pri[0] = PK
-        mm(lst, 512, ["L1", "LE", "mK0", "mK1"], ["k1m"], [4])
-        pri[0] = 0.0
-        act(T.KT1[0:8, :], B[4][0:8, 0:256], F.Identity, 256, [], ["KT1"], [4])
-        offsets(0)
-        ts(T.u1[:, 16:24], B[7][:, 16:24], col(1), None, A.add, None, 8, ["c1"], ["um"], [7])
-        lw = T.ll[:, 0:4112]
-        tt(T.bb[:], lw.indirect(T.u1[:, 0:8]), nn, A.is_ge, 128 * GC + 40, lk + ["ul0", nkey], ["bb"])
-        tt(T.f2[:], T.bb[:], T.f1[:], A.mult, 256, ["bb", "f1"], ["f2"])
-        act(T.e1[:], lw.indirect(T.u1[:, 0:8]), F.Copy, 128 * GC, lk + ["ul0"], ["e1"])
-        act(T.fa[:], T.f2[:], F.Relu, 128, ["f2"], ["fb"], bias=32.0, scale=-1.0)
-        act(B[6][:, 384:512], T.fa[:], F.Identity, 128, ["fb"], ["fa"], [6], bias=33.0, scale=-1.0)
-        lst = grp(B[2][:, 0:256], [(T.KT1[0:33, 0:128], T.RUa[:]), (T.KT1[0:8, 128:256], T.RE[:])])
-        mm(lst, 512, ["KT1", "K11", "RUa1", "RUa2", "RE"], [], [2])
-
-        def gate(reg, bk, src, sk, pen, pk, key):
-            if GATE == "v":
-                tt(reg, reg, src, A.min, 256, [sk], [key], [bk])
+        def put():
+            if t < RO - 1:
+                add("v", rgs(R("us"), R("v2")), rgs(R("X", 0, 4096)), [lambda: V.tensor_copy(T.X[:, 0:4096].indirect(T.us[:]), T.v2[:])])
             else:
-                act(pen, reg, F.Relu, 256, [], [pk], [bk], scale=-1.0)
-                mm(grp(reg, [(T.jb[:], src), (T.In[:], pen)]), 1280, [sk, pk, "jb", "In"], [key], [bk])
-        gate(B[2][:, 0:256], 2, T.A1[:, 7:263], "A1", T.nk2[:], "nkc", "t1")
-        tt(T.o1[:], B[2][:, 0:256], T.AA[:, 8:264], A.max, 256, ["AA", "t1"], ["o1"], [2])
-        front(0, T.sa)
-        a12 = T.sa[:, 15:128:16]; b0 = T.sc[:, 15:128:16]
-        ts(T.fr[:, 0:8], a12, -12288.0, None, A.add, None, 8, ["s0"], ["fr0"])
-        cut(T.f2[:], "f2", 1)
-        tt(T.bb[:], lw.indirect(T.us[:, 8:16]), nn, A.is_ge, 128 * GC + 40, lk + ["ud", nkey], ["bb"])
-        tt(T.f1[:], B[6][:, 384:512], T.bb[:], A.mult, 128, ["bb", "fa"], ["f1"], [6])
-        tt(T.fr[:, 8:16], B[7][:, 48:56], T.fr[:, 0:8], A.mult, 8, ["fr0"], ["fr1"], [7])
-        tt(T.e2[:], lw.indirect(T.u2[:, 0:8]), T.e1[:], A.min, 128 * GC + 40, lk + ["ul1", "e1"], ["e2"])
-        mm(grp(B[3][:, 0:256], [(T.KT2[0:33, 0:128], T.RUa[:]), (T.KT1[0:8, 128:256], T.RE[:])]), 512, ["KT1", "KT2", "K12", "RUa1", "RUa2", "RE"], [], [3])
-        gate(B[3][:, 0:256], 3, T.A2[:, 6:262], "A2", T.nk2[:], "nkc", "t2")
-        tt(T.o2[:], B[3][:, 0:256], T.o1[:], A.max, 256, ["o1", "t2"], ["o2"], [3])
-        front(1, T.sc)
-        tt(T.fr[:, 16:24], T.fr[:, 8:16], b0, A.add, 16, ["fr1", "s1"], ["fr2"])
-        cut(T.f1[:], "f1", 2)
-        Mm = nb[:, 128:256]
-        tt(Mm, T.pm[:, 0:4112].indirect(T.u3[:, 0:8]), T.e2[:], A.min, 128 * GC + 40, pmk + ["ul2", "e2"], [mkey])
-        tt(T.fr[:, 24:32], B[7][:, 80:88], T.fr[:, 0:8], A.mult, 8, ["fr0"], ["fr3"], [7])
-        gl = grp(B[3][:, 256:512], [(T.KT1[0:8, 128:256], T.RE[:]), (T.KT2[0:8, 128:256], T.RF[:]), (T.KT3[0:33, 0:128], T.RUa[:])])
-        mm(gl[:2], 512, ["KT1", "KT2", "RE", "RF"], [], [3])
-        mm(gl[2:], 256, ["KT3", "K13", "RUa1", "RUa2"], [], [3])
-        front(2, T.sc)
-        tt(T.fr[:, 32:40], T.fr[:, 24:32], b0, A.add, 16, ["fr3", "s1"], ["fr4"])
-        tt(B[2][:, 0:256], B[3][:, 256:512], T.A3[:, 5:261], A.min, 256, ["A3"], ["t3"], [2, 3])
-        for j, src, sk in ((1, T.fr[:, 16:24], "fr2"), (2, a12, "s0")):
-            tt(B[2][:, j:256:32], B[3][:, 256 + j:512:32], src, A.min, 8, [sk, "t3"], ["t3%d" % j], [2, 3])
-        t3 = ["t3", "t31", "t32"]
-        tt(T.i3[:], B[2][:, 0:256], T.o2[:], A.max, 256, t3 + ["o2"], ["i3"], [2])
-        mm(grp(B[6][:, 0:256], [(T.KT1[0:33, 128:256], T.RX[:])]), 256, ["KT1", "K11", "RX1", "RX2"], [], [6])
-        tt(B[6][:, 0:256], B[6][:, 0:256], T.A1[:, 8:264], A.min, 256, ["A1"], ["te"], [6])
-        tt(T.EE[:], B[6][:, 0:256], T.Cf[:], A.max, 256, ["Cf", "te"], ["EE"], [6])
-        if t < RO - 1:
-            add("s", 200, ["KT1"], ["th1", "nT"], [lambda: S.activation(T.nT[0:8, 0:128], T.KT1[0:8, 128:256], F.Identity, accum_out=T.thf[:, 1:2])])
-            mm(grp(B[6][:, 256:257], [(T.ONf[:], T.thf[:, 1:2])]), 256, ["ONf", "th1"], [], [6])
-            ts(T.ti[:, 0:1], B[6][:, 256:257], 1.0 / 8192, None, A.mult, None, 1, [], ["ti0"], [6])
-            ts(T.ti[:, 1:2], T.ti[:, 0:1], 63, None, A.bitwise_and, None, 1, ["ti0"], ["ti1"])
-            tt(col(12), T.ti[:, 1:2], col(11), A.add, 1, ["ti1", "c11"], ["thr"])
-        tt(B[2][:, 0:256:32], B[3][:, 256:512:32], T.fr[:, 32:40], A.min, 8, ["fr4", "t3", "i3"], ["t30"], [2, 3])
-        tt(T.i4[:], B[2][:, 0:256], T.EE[:], A.max, 256, t3 + ["t30", "EE"], ["i4"], [2])
-        ts(T.Ni[:], T.i3[:], 4095, None, A.bitwise_and, None, 256, ["i3"], ["Ni"])
-        cp(T["Nu%d" % t][:], T.Ni[:], 256, ["Ni"], ["Nu%d" % t])
-        ts(T["Nu%d" % t][:, 0:256:32], T.fr[:, 32:40], -12288.0, None, A.add, None, 8, ["fr4"], ["Nu%d" % t])
-        ts(T.Pi[:], T.i4[:], 4095, None, A.bitwise_and, None, 256, ["i4"], ["Pi"])
-        if t < RO - 1: cp(T.Pu[:], T.Pi[:], 256, ["Pi"], allpu)
-        else: cp(T.pq[:], T.Pi[:], 256, ["Pi"], ["pq"])
-        mm(grp(B[7][:, 128:136], [(T.Sw[:, 15 - s:143 - s], nb[:, 128 + s:256:16]) for s in range(16)]), 1024, ["Sw", mkey], [], [7])
-        cp(T.si[:, 0:8], B[7][:, 128:136], 8, [], ["si0"], [7])
-        ts(T.si[:, 8:16], T.si[:, 0:8], 31, None, A.bitwise_and, None, 8, ["si0"], ["si1"])
-        tt(T.si[:, 16:24], T.si[:, 8:16], T.sb[:], A.add, 16, ["si1", "sb"], ["si2"])
-        cp(T.us[:, 0:8], T.si[:, 16:24], 8, ["si2"], ["us"])
-        tt(T.v1[:], Mm, nn, A.add, 256, [mkey, nkey], ["v1"])
-        ts(T.v2[:], T.v1[:], 1, None, A.arith_shift_right, None, 128, ["v1"], ["v2"])
-        cp(T.X[:, 0:4096].indirect(T.us[:, 0:8]), T.v2[:], 128 * 3.8, ["us", "v2"], ["Xa", "Xb"])
-        act(T["mo%d" % t][:], nb[:, 0:256].indirect(T.u1[:, 16:24]), F.Copy, 128 * GC, ["um", mkey, nkey], ["mo%d" % t])
+                tt(R("dl"), IX(Xw, R("us")), R("v2"), A.subtract)
+                tt(R("oy"), R("ox"), R("dl"), A.subtract)
+        st["put"] = put
+        st["mo"] = lambda: act(R(mo), IX(R(nb), R("un", 24, 32)), F.Copy)
         dst = cores[(rank + 1 + t % 3) % len(cores)]
         hlp = helper_of(topo, cores, core, dst); to = dst if hlp is None else hlp
         rid, pid = topo.addr(to, core); mask = engines_mask(topo, core, to)
-        for src, sk, land, wk, sem in ((T["Nu%d" % t][:], "Nu%d" % t, T["Cu%d" % (t + 1)][:, 0:256], "C%d" % (t + 1), T.sem["ac%d" % t]),
-                                       (T["mo%d" % t][:], "mo%d" % t, T["nb%d" % (t + 1)][:, 0:128], "n%d" % (t + 1), T.sem["an%d" % t])):
-            j = add("g", 300, [sk], [], [lambda src=src, land=land, sem=sem, rid=rid, pid=pid, mask=mask: g.remote_dma(land, src, sem, T.sem.sent, pid, rid, mask)], rem=True)
-            add("x", 0, [], [wk], [], lat=LAT, sem=sem, val=NENG, after=[j])
-            nsent += NENG
-    for r in range(8):
-        act(T.op[:, r:256:8], T.pq[:, 32 * r:32 * r + 32], F.Identity, 32, ["pq"], ["op%d" % r])
-        cp(T.oc[:, r:256:8], T["Cu%d" % RO][:, 32 * r:32 * r + 32], 32, ["C%d" % RO], ["oc%d" % r])
-    mm(grp(B[6][:, 0:128], [(T.Id[:], T.X[:, k:4096:32]) for k in range(32)]), 4096, ["Id", "Xa", "Xb"], [], [6])
-    act(T.ox[:], B[6][:, 0:128], F.Identity, 128, [], ["ox"], [6])
-    dma("y", T.yp[:], T.op[:], ["op%d" % r for r in range(8)], [], 2500)
-    dma("s", T.yx[:], T.ox[:], ["ox"], [], 2500)
-    dma("y", T.yc[:], T.oc[:], ["oc%d" % r for r in range(8)], [], 2500)
-    dma("y", T.yn[:], T["nb%d" % RO][:, 0:128], ["n%d" % RO], [], 2500)
+
+        def send(src, land, sem):
+            add("g", rgs(src), [], [lambda: g.remote_dma(land["ap"], src["ap"], sem, T.sem.sent, pid, rid, mask)], rem=True)
+            add("x", [], rgs(land), [], sem=sem, val=NENG)
+            nsent[0] += NENG
+        st["sendN"] = lambda: send(R(nu), R("Cu%d" % (t + 1)), T.sem["ac%d" % t])
+        st["sendM"] = lambda: send(R(mo), R("nb%d" % (t + 1), 0, 128), T.sem["an%d" % t])
+        st.update(late)
+        return st
+
+    rounds = [steps(t) for t in range(RO)]
+    for t in range(RO):
+        for nm in " ".join((FIRST, JOIN0, CUTS) if t == 0 else (LOOKUP, JOIN, CUTS)).split():
+            at = len(ops)
+            if nm[-1] != "+": rounds[t][nm]()
+            elif t + 1 < RO: rounds[t + 1][nm[:-1]]()
+            for o in ops[at:]: o["step"] = (t, nm)
+    dma("s", T.yx[:], R("oy"))
+    for r in range(8): act(R("op", r, 256, 8), R("pq", 32 * r, 32 * r + 32))
+    dma("y", T.yp[:], R("op"))
+    for r in range(8): cp(R("oc", r, 256, 8), R("Cu%d" % RO, 32 * r, 32 * r + 32))
+    dma("s", T.yn[:], R("nb%d" % RO, 0, 128))
+    dma("y", T.yc[:], R("oc"))
     run(ops, g, T)
-    g.wait_ge(T.sem.sent, nsent)
+    g.wait_ge(T.sem.sent, nsent[0])

from concourse.mybir import AluOpType as A, ActivationFunctionType as F

RO = 4
BF, F32, I32, U16 = "bfloat16", "float32", "int32", "uint16"
SB = {
    BF: {"X": 4112, "xg": 4096, "dg": 4096, "rg": 4096, "zg": 4096, "ll": 4128, "pm": 4128, "ind": 4096,
         "ON": 1024, "Bm": 2048, "nS": 2048, "Pa": 1920, "Pn": 1024, "TB": 128, "TR": 1024, "OH": 256, "eb": 128,
         "Id": 128, "In": 128, "I64": 128, "I4": 128, "Ia": 128, "S2": 144, "Sn": 288, "Sw": 144, "c0": 128, "ctl": 1024, "ct0": 512,
         "G1": 8, "L1": 12, "LE": 16, "RA": 40, "RB": 32, "RU": 256, "RV": 256, "RE": 256, "CR": 272,
         "KT1": 256, "KT2": 128, "KT3": 128, "nk": 256, "nT": 256, "mK": 256, "fb": 128, "b1": 128, "b2": 128, "sg": 1024, "qq": 128,
         "e1": 128, "e2": 128, "e3": 128},
    F32: {"jo": 144, "j16": 128, "jb": 128, "cf": 24, "Idf": 128, "ONf": 128, "G8": 128, "thf": 2, "fpi": 8, "sb": 8,
          "hp": 256, "Cf": 256, "Cm": 256, "pc": 256, "tq": 256, "AA": 272, "A1": 272, "A2": 272, "A3": 272, "o1": 256, "o2": 256,
          "gd": 128, "sc": 128, "pq": 256, "op": 256, "oc": 256, "ox": 128, "oy": 128, "dl": 128},
    I32: {"pin": 256, "cin": 256, "wi": 1, "thi": 1, "em": 128, "ci": 8, "i2": 256, "hh": 256, "i3": 256, "i4": 256, "Ni": 256, "Pi": 256,
          "si": 24, "v1": 128, "v2": 128, "ti": 2},
    U16: {"fpl": 8, "Pu": 256, "Hu": 256, "ul": 24, "un": 32, "us": 8},
}
PARTS = {"nS": 64, "nT": 64, "TB": 8, "TR": 8, "OH": 8, "RA": 33, "RB": 8, "RU": 33, "RV": 33, "RE": 8, "CR": 1,
         "KT1": 33, "KT2": 33, "KT3": 33, "ONf": 8, "G8": 8, "thf": 8, "thi": 8}
SCRATCH = {n: ("sbuf", [PARTS.get(n, 128), w], d) for d, t in SB.items() for n, w in t.items()}
for _t in range(RO + 1):
    SCRATCH["Cu%d" % _t] = ("sbuf", [128, 256], U16)
    SCRATCH["nb%d" % _t] = ("sbuf", [128, 256], BF)
for _t in range(RO):
    SCRATCH["Nu%d" % _t] = ("sbuf", [128, 256], U16)
    SCRATCH["mo%d" % _t] = ("sbuf", [128, 128], BF)
for _b in range(8):
    SCRATCH["B%d" % _b] = ("psum", [128, 512], F32)
SEMAPHORES = (["sv", "ss", "sp", "sg", "sent"] + ["d%d" % i for i in range(16)]
              + ["ac%d" % t for t in range(RO)] + ["an%d" % t for t in range(RO)])

NENG = 8
PMB = (6, 4, 6, 4, 0, 1, 6, 4)
SUB = ((4, 0), (4, 64), (5, 0), (4, 128))
SG_ON = "svsv"
AL, LO, HI = 4096.0, -7936.0, 64.0
QC = -7 * LO - 8 * HI
LOOKUP = "x1s x3s x0v sums"
JOIN = ("y1 dx x2v d0 xa1 cm xa2 xa0 xa3 r0s su0a dy su0b i1 d2a ib nk0 hh hp0 d2b r1a Hu0 r1b Cm nT su1 r2v su2a mr1 nn0 su2b nk1 hp1 mr0 mw1 mr2 "
        "z0 Hu1 d3 nk2 z1 r3v hp2 mw0 mw2 mr3 su3a l0 Hu2 su3b mw3 nk3 l2 hp3 mx4 l1 z2 Hu3 pm0 mx6 l3 mx5 nn1 pq0 tqb pm1 pq1 z3 in0 mx7 nn2 pq2 "
        "l5 in1 l4 in2 nn5 nn3 ct1 pq3 pm2 l7 nn6 pm3b nn4 pq5 in3 pq4 ct0 l6 pm3a in5 ct3 nn7 pq7 ct5 ct2 TB1 pq6 in4 fs4 fs5 AA mK0 f0 ct4 in7 "
        "in6 ct7 k1a ct6 fc TB0 TB3 TB2 fs7 fs6")
CUTS = ("mK1 fb k1b ul0 b1 k1m pf KT1 pb1 rk1 sg1b rv1 sg1a rs1a of0 sg1d sg1c A2 A1 rs1b un0 rs1c A3 fr0 rs1d q1 g1 lo1 ls1 t1 kt1 ul1 sc0 b2 o1 pt0 "
        "e2 KT2 rk2 ps pb2 of1 rv2 sg2b sg2a g2 rs2a sg2c sg2d rs2b un1 t2 um e1 fr1 rs2c rs2d g3a lo2 q2 kt2 ls2 sc1 o2 pt1 e3 ul2 KT3 g3b t3 of2 "
        "un2 i3 M g4 th1 fr2 Ni vv Sw sc2 Nu th2 Nu0 sendN th3 t4 si0 i4 si1 i40 si2 mo Pi v2 pa+ Pu us pb+ put sendM pc+ th4 tqa+")
FIRST = "cm kPa pa x0s tqa pb x1s kth kSw kRB pc"
JOIN0 = ("d0 su0a x2s i1 r0v su0b ib d1 nk0 xa3 su1a hh xa1 r1v hp0 Hu0 xa2 x3s mr2 mr3 xa0 z0 su1b mr0 d2 r2s mr1 kc0 nk1 hp1 Hu1 z1 mw2 su2a su2b "
         "mw0 d3 r3s nT mw1 nk2 mw3 hp2 su3a su3b l0 nn0 Hu2 kfp l1 nk3 hp3 mx4 nn1 mx5 Hu3 z2 l2 pm0 z3 l3 pq1 kg mx6 pq0 mx7 in1 kc1 pm1 in0 kRU "
         "Cm nn3 nn2 pq2 pq3 l5 l6 ct1 l4 tqb pm3a in2 pm2 AA nn5 in3 ct0 ct2 nn4 l7 pq5 kPn nn6 pq6 nn7 in6 in5 pq4 ct3 f0 pm3b in4 mK0 fs6 pq7 "
         "TB1 TB2 TB3 in7 fs4 fs5 TB0 ct6 ct4 fs7 ct5 k1a ct7 fc")


def engines_mask(topo, src, dst):
    m = 0
    for e in topo.engines(src, dst)[:NENG]:
        m |= 1 << e
    return m


def helper_of(topo, cores, src, dst):
    if topo.may_write(src, dst):
        return None
    for same in (True, False):
        for h in topo.cores_of(src):
            if h not in cores and (topo.die(h) == topo.die(src)) == same and topo.may_write(h, dst):
                return h
    return None


def helper_program(g, core, T, topo):
    cores = list(T.cores); n = len(cores); sent = 0
    for t in range(RO):
        for r in range(n):
            dst = cores[(r + 1 + t % 3) % n]
            if helper_of(topo, cores, cores[r], dst) != core:
                continue
            rid, pid = topo.addr(dst, core); mask = engines_mask(topo, core, dst)
            for sem, ap in ((T.sem["ac%d" % t], T["Cu%d" % (t + 1)][:, 0:256]), (T.sem["an%d" % t], T["nb%d" % (t + 1)][:, 0:128])):
                g.wait_ge(sem, NENG)
                g.remote_dma(ap, ap, sem, T.sem.sent, pid, rid, mask)
                sent += NENG
    if sent:
        g.wait_ge(T.sem.sent, sent)


def run(ops, g, T):
    n = len(ops)
    pre = [set() for _ in range(n)]
    acc, bank, lastg = {}, {}, None
    for i, o in enumerate(ops):
        e = o["e"]
        for isw, regs in ((False, o["r"]), (True, o["w"])):
            for nm, m, p0, p1 in regs:
                for j, w2, m2, q0, q1 in acc.get(nm, []):
                    if j != i and (isw or w2) and m & m2 and p0 < q1 and q0 < p1 and not ops[j]["e"] == e == "p":
                        pre[i].add(j)
        for isw, regs in ((False, o["r"]), (True, o["w"])):
            for nm, m, p0, p1 in regs:
                old = acc.setdefault(nm, [])
                if isw: old[:] = [x for x in old if x[2] & ~m or x[3] < p0 or x[4] > p1]
                old.append((i, isw, m, p0, p1))
        for k in {x[0] for x in o["r"] + o["w"] if SCRATCH[x[0]][0] == "psum"}:
            last = bank.setdefault(k, {})
            pre[i].update(j for e2, j in last.items() if e2 != e)
            last[e] = i
        if e == "g" and o["sem"] is None and not o["rem"]:
            if lastg is not None: pre[i].add(lastg)
            lastg = i
    pos, cnt = {}, {}
    for i, o in enumerate(ops):
        cnt[o["e"]] = cnt.get(o["e"], 0) + 1; pos[i] = cnt[o["e"]]
    know, clock, waits, sig = {}, {}, {}, set()
    for i, o in enumerate(ops):
        kn = know.setdefault(o["e"], {}); wl = []
        for j in sorted(pre[i], reverse=True):
            key = ("x", j) if ops[j]["sem"] is not None else ops[j]["e"]
            val = 1 if ops[j]["sem"] is not None else pos[j]
            if kn.get(key, 0) >= val: continue
            wl.append(j); sig.add(j); kn[key] = val
            for k2, v2 in clock[j].items():
                if kn.get(k2, 0) < v2: kn[k2] = v2
        waits[i] = wl; clock[i] = dict(kn) if o["e"] != "x" else {}
    q = {"v": g.vector, "s": g.scalar, "p": g.tensor, "g": g, "y": g.sync}
    sems = {"v": T.sem.sv, "s": T.sem.ss, "p": T.sem.sp, "g": T.sem.sg}
    num, tot = {}, {}
    for i, o in enumerate(ops):
        e = o["e"]
        if e == "x": continue
        for j in waits[i]:
            if ops[j]["sem"] is not None: q[e].wait_ge(ops[j]["sem"], ops[j]["val"])
            else: q[e].wait_ge(sems[ops[j]["e"]], num[j])
        ins = None
        for f in o["f"]: ins = f()
        if o["sem"] is not None:
            ins.then_inc(o["sem"], 16)
        elif i in sig:
            tot[e] = tot.get(e, 0) + 1; num[i] = tot[e]; ins.then_inc(sems[e], 1)
    for i, o in enumerate(ops):
        if o["sem"] is not None and i not in sig: g.wait_ge(o["sem"], o["val"])


def rank_program(g, core, T, topo):
    rank = T.rank_of(core)
    if rank is None:
        helper_program(g, core, T, topo)
        return
    cores = list(T.cores); ops = []; nd = [0]; masks = {}; nsent = [0]
    V, S, P = g.vector, g.scalar, g.tensor

    def R(nm, c0=0, c1=None, st=1, p0=0, p1=None):
        sh = SCRATCH[nm][1]
        c1 = sh[1] if c1 is None else c1; p1 = sh[0] if p1 is None else p1
        if (c0, c1, st) not in masks:
            masks[(c0, c1, st)] = ((1 << (c1 - c0)) - 1) << c0 if st == 1 else sum(1 << c for c in range(c0, c1, st))
        ps = slice(None) if (p0, p1) == (0, sh[0]) else slice(p0, p1)
        return {"ap": T[nm][ps, slice(c0, c1) if st == 1 else slice(c0, c1, st)], "rg": [(nm, masks[(c0, c1, st)], p0, p1)]}

    def IX(win, off): return {"ap": win["ap"].indirect(off["ap"]), "rg": win["rg"] + off["rg"]}
    def Bk(b, c0=0, c1=512, st=1, p1=128): return R("B%d" % b, c0, c1, st, 0, p1)
    def ap(x): return x["ap"] if isinstance(x, dict) else x
    def rgs(*xs): return [r for x in xs if isinstance(x, dict) for r in x["rg"]]
    def add(e, r, w, fs, sem=None, val=0, rem=False): ops.append({"e": e, "r": r, "w": w, "f": fs, "sem": sem, "val": val, "rem": rem})

    def ts(out, a, s1, o0, s2=None, o1=None):
        f = (lambda: V.tensor_scalar(out["ap"], a["ap"], ap(s1), None, o0)) if o1 is None else (lambda: V.tensor_scalar(out["ap"], a["ap"], ap(s1), ap(s2), o0, o1))
        add("v", rgs(a, s1, s2), rgs(out), [f])
    def tt(out, a, b, op): add("v", rgs(a, b), rgs(out), [lambda: V.tensor_tensor(out["ap"], a["ap"], b["ap"], op)])
    def cp(out, a): add("v", rgs(a), rgs(out), [lambda: V.tensor_copy(out["ap"], a["ap"])])
    def ms(out, val): add("v", [], rgs(out), [lambda: V.memset(out["ap"], val)])
    def scan(out, d0, d1, o0, o1): add("v", rgs(d0, d1), rgs(out), [lambda: V.tensor_tensor_scan(out["ap"], d0["ap"], d1["ap"], 0.0, o0, o1)])
    def act(out, a, fn=F.Identity, bias=0.0, scale=1.0):
        if fn == F.Copy: add("s", rgs(a), rgs(out), [lambda: S.activation(out["ap"], a["ap"], fn)])
        else: add("s", rgs(a, scale), rgs(out), [lambda: S.activation(out["ap"], a["ap"], fn, bias=bias, scale=ap(scale))])
    def mm(trip, first=True, last=True, alone=False):
        add("p", [r for x in trip for r in rgs(x[1], x[2])], [r for x in trip for r in rgs(x[0])],
            [(lambda x=x, i=i: P.matmul(x[0]["ap"], x[1]["ap"], x[2]["ap"], alone or (first and i == 0), alone or (last and i == len(trip) - 1)))
             for i, x in enumerate(trip)])
    def iota(out, pat, base, cm=0, whole=False):
        if whole: f = lambda: g.iota(out["ap"], pat, base, cm)
        else: f = lambda: g.iota(out["ap"], pat, base, cm, allow_small_or_imprecise_dtypes=True)
        add("g", [], rgs(out), [f])
    def asel(out, a, pat, op, fill, base, cm): add("g", rgs(a), rgs(out), [lambda: g.affine_select(out["ap"], a["ap"], pat, op, fill, base, cm)])
    def dma(e, out, a, slow=False):
        sem = T.sem["d%d" % nd[0]]; nd[0] += 1
        qq = {"g": g, "s": S, "y": g.sync}[e]
        f = (lambda: qq.dma_start(ap(out), ap(a), allow_slow_non_contiguous=True)) if slow else (lambda: qq.dma_start(ap(out), ap(a)))
        add(e, rgs(a), rgs(out), [f], sem=sem, val=16)
    def col(j): return R("cf", j, j + 1)
    def fill(nm, val, c0=0, c1=None, st=1, p0=0, p1=None):
        c1 = SCRATCH[nm][1][1] if c1 is None else c1; p1 = SCRATCH[nm][1][0] if p1 is None else p1
        act(R(nm, c0, c1, st, p0, p1), R("ON", 0, len(range(c0, c1, st)), 1, p0, p1), scale=val)

    dma("y", R("pin"), T.pn[:])
    dma("s", R("cin"), T.cn[:])
    dma("y", R("X", 0, 2048), T.lit[:, 0:2048])
    dma("s", R("X", 2048, 4096), T.lit[:, 2048:4096])
    dma("y", R("nb0", 0, 128), T.neg[:])
    ms(R("ON"), 1.0)
    iota(R("ci", 0, 1), [[0, 1]], 0, 1, True)
    iota(R("jo"), [[1, 144]], 0)
    dma("g", R("wi"), T.wt[:], True)
    dma("g", R("thi"), T.th[:], True)
    iota(R("jb"), [[16, 8], [0, 16]], 0)
    iota(R("em"), [[-1, 128]], 0, 1, True)
    iota(R("j16"), [[0, 8], [1, 16]], 0)
    ms(R("ONf"), 1.0); ms(R("X", 4096, 4112), 255.0)
    asel(R("G8"), R("ONf"), [[-1, 8], [0, 16]], A.is_equal, 0.0, 0, 1)
    for j in range(2): asel(R("Bm", 1024 * j, 1024 * j + 1024), R("ON"), [[-1, 8], [-16, 8], [0, 16]], A.is_equal, 0.0, -8 * j, 1)
    for j in range(2): asel(R("nS", 1024 * j, 1024 * j + 1024), R("ON", p1=64), [[-1, 8], [-16, 4], [0, 32]], A.is_equal, 0.0, -8 * j, 1)
    ts(R("ci", 1, 2), R("ci", 0, 1), 15, A.bitwise_and)
    ts(R("ci", 2, 3), R("ci", 0, 1), 5, A.arith_shift_right)
    ts(R("ci", 3, 4), R("ci", 0, 1), 31, A.bitwise_and)
    cp(R("cf", 0, 2), R("ci", 0, 2))
    tt(col(2), col(0), col(1), A.subtract)
    ts(R("Id"), R("jo", 0, 128), col(0), A.is_equal)
    ts(col(5), R("ci", 2, 3), 4.0, A.add)
    ts(col(6), R("ci", 3, 4), 31.0, A.is_equal, 8192.0, A.mult)
    ts(col(3), col(2), 15.0, A.add)
    ts(col(15), col(1), 15.0, A.is_lt, 16384.0, A.mult)
    ts(R("G1"), R("jo", 0, 128, 16), col(2), A.is_equal)
    ts(R("L1"), R("jo", 0, 12), col(5), A.is_equal)
    ts(R("S2"), R("jo"), col(3), A.is_equal, 2.0, A.mult)
    fill("ctl", 0.0); fill("ct0", 1.0); fill("ctl", 512.0, 0, 1024, 32); fill("ct0", 0.0, 0, 512, 32)
    for j, mul, off in ((7, 4.0, 0.0), (8, 128.0, 0.0), (9, 128.0, 16.0), (10, 128.0, 16.0 + QC), (13, 32.0, 0.0), (14, 1.0, 1.0)):
        act(col(j), col(1), bias=off, scale=mul)
    for nm, sc in (("In", -1.0), ("Idf", 1.0)): act(R(nm), R("Id"), scale=sc)
    act(R("Sn", 0, 144), R("S2"), scale=-0.5); act(R("Sn", 144, 288), R("S2"), scale=0.5)
    act(col(16), col(15), bias=-12288.0)
    for nm, sc in (("I64", 64.0), ("I4", 4 * AL), ("Ia", -AL)): act(R(nm), R("Id"), scale=sc)
    for nm, at, val in (("ll", 0, -256.0), ("ll", 4112, 255.0), ("pm", 0, 255.0), ("pm", 4112, 255.0)): fill(nm, val, at, at + 16)
    fill("AA", 0.0, 0, 8); fill("AA", 0.0, 264, 272); fill("TB", 1.0 / 128)
    ts(R("LE", 0, 12), R("L1"), col(6), A.mult)
    ts(R("v1"), R("em"), 15, A.bitwise_and)
    ts(R("jb"), R("jb"), col(2), A.not_equal, 16.0, A.mult)
    tt(R("LE", 12, 16), R("LE", 4, 8), R("L1", 4, 8), A.max)
    tt(R("eb"), R("v1"), R("jb"), A.add)
    for r in range(8): cp(R("Pu", 32 * r, 32 * r + 32), R("pin", r, 256, 8))
    for r in range(8): cp(R("Cu0", 32 * r, 32 * r + 32), R("cin", r, 256, 8))
    cp(R("Pi"), R("Pu"))
    iota(R("fpi", 0, 4), [[1, 4]], 0)
    iota(R("fpi", 4, 8), [[32, 4]], 2048 + 31)
    iota(R("CR", 256, 264), [[2048, 2], [32, 4]], 0)
    asel(R("TR"), R("ON", p1=8), [[-1, 8], [0, 128]], A.is_equal, 0.0, 0, 1)
    asel(R("TB"), R("TB"), [[0, 8], [-1, 16]], A.is_ge, -1.0 / 128, 14, -1)
    iota(R("sb"), [[512, 8]], 0)
    oh = R("Id", 0, 8, p1=8)

    def gates():
        asel(R("OH"), R("ON", 0, 256, p1=8), [[-1, 8], [0, 32]], A.is_equal, 0.0, 0, 1)
        for nm in ("RU", "RV", "RA"): iota(R(nm), [[0, SCRATCH[nm][1][1]]], 0)
        iota(R("RU", p0=32, p1=33), [[0, 8], [-32768, 32]], 16384)
        iota(R("RV", p0=32, p1=33), [[0, 256]], 32768)
        iota(R("RV", 1, 256, 32, p0=32, p1=33), [[0, 8]], 0)
        for nm in ("KT1", "KT2", "KT3"):
            w = SCRATCH[nm][1][1]; asel(R(nm), R("ON", 0, w, p1=33), [[0, w]], A.is_equal, 0.0, -32, 1)
        iota(R("CR", 0, 256), [[int(-4 * AL), 2], [0, 128]], int((-2 if SG_ON[3] == "v" else -3) * AL))
        for j, st, base in ((0, 32, 0), (1, 16, 128), (2, 32, 0), (3, 32, 0)): iota(R("RA", 8 * j, 8 * j + 8, p0=32, p1=33), [[st, 8]], base)
        for j in (0, 2, 3): asel(R("RA", 8 * j, 8 * j + 8, p1=8), R("ON", 0, 8, p1=8), [[-1, 8]], A.is_equal, 0.0, 0, 1)

    late = {
        "kg": gates,
        "kth": lambda: (cp(R("thf", 0, 1), R("thi")), cp(col(4), R("wi")), mm([(Bk(4, 0, 1), R("G8"), R("thf", 0, 1))]), act(col(11), Bk(4, 0, 1)), act(col(12), Bk(4, 0, 1))),
        "kPa": lambda: ([ts(R("Pa", 128 * (u - 1), 128 * u), R("eb"), float(u), A.is_equal, AL, A.mult) for u in range(1, 16)],
                        asel(R("Pa"), R("Pa"), [[0, 15], [-1, 128]], A.not_equal, -AL, 0, 1)),
        "kPn": lambda: act(R("Pn"), R("Pa", 0, 1024), scale=1.0 / AL),
        "kc0": lambda: (ts(R("c0"), R("j16"), col(1), A.is_equal, 32768.0, A.mult), ts(R("e1"), R("j16"), col(14), A.is_equal, -16384.0, A.mult)),
        "kc1": lambda: tt(R("c0"), R("c0"), R("e1"), A.add),
        "kfp": lambda: (ts(R("fpl", 0, 4), R("fpi", 0, 4), col(7), A.add), ts(R("fpl", 4, 8), R("fpi", 4, 8), col(8), A.add), ts(R("sb"), R("sb"), col(13), A.add)),
        "kSw": lambda: act(R("Sw"), R("Sn", 144, 288), scale=col(4)),
        "kRB": lambda: [act(R("RB", 8 * j, 8 * j + 8), oh, scale=sc) for j, sc in enumerate((-1.0 / 64, 1.0, -1.0 / 8192, -32.0 / 8192))],
        "kRU": lambda: (act(R("RU", p1=8), R("OH"), scale=32768.0), act(R("RV", 1, 256, 32, p1=8), oh, scale=32768.0), act(R("RE"), R("OH"), scale=-512.0)),
    }

    Xw, lw, pw, Id, ones = R("X"), R("ll"), R("pm"), R("Id"), R("ON", 0, 128, p1=1)
    kv, ke, base = [R("KT%d" % c, 0, 128) for c in (1, 2, 3)], R("KT1", 128, 256, p1=8), R("CR", 256, 264)
    pa, tq, rk, g1, g2, g4 = Bk(7, 0, 256), Bk(7, 256, 512), Bk(5, 0, 128), Bk(6, 0, 256), Bk(6, 256, 512), Bk(4, 256, 512)
    lane = R("sc", 15, 128, 16)

    def steps(t):
        cu, nb, nu, mo = "Cu%d" % t, "nb%d" % t, "Nu%d" % t, "mo%d" % t
        nn, Mm = R(nb, 0, 128), R(nb, 128, 256)
        st = {}
        def Q(nm, q, a=0, b=1024): return R(nm, 1024 * q + a, 1024 * q + b)
        def L(nm, q, a=0, b=64): return R(nm, 64 * q + a, 64 * q + b)
        st["pa"] = lambda: ts(pa, R("Pi"), 1184.0, A.add)
        st["pb"] = lambda: ts(R("i2"), R("Pi"), 63, A.bitwise_and)
        st["pc"] = lambda: ts(R("pc"), R("i2"), 2048.0, A.mult, 27648.0, A.add)
        st["tqa"] = lambda: (act(R("tq"), pa, bias=2912.0), mm([(tq, R("Idf"), R("tq"))], True, False))
        st["cm"] = lambda: ts(R("Cf"), R(cu), -2016.0, A.add)
        st["i1"] = lambda: tt(pa, pa, R("Cf"), A.mult)
        st["ib"] = lambda: tt(R("i2"), pa, R("pc"), A.add)
        st["hh"] = lambda: ts(R("hh"), R("i2"), 5, A.arith_shift_right, 4095, A.bitwise_and)
        st["Cm"] = lambda: act(R("Cm"), R("Cf"), bias=-2080.0)
        st["nT"] = lambda: (mm([(Bk(6, 128 * h, 128 * h + 128, p1=64), R(nb, 64 * h, 64 * h + 64), Id) for h in range(2)], alone=True),
                            act(R("nT"), Bk(6, 0, 256, p1=64), scale=-1.0))
        st["sums"] = lambda: t == RO - 1 and (mm([(Bk(4, 0, 128), Id, R("X", k, 4096, 32)) for k in range(32)]), act(R("ox"), Bk(4, 0, 128)))

        def sums(q, terms, first, last):
            b, c = SUB[q]
            for j, (a, o, x) in enumerate(terms):
                mm([(Bk(b, c, c + 64), R(a, o + 15 - s, o + 143 - s), R(x, 1024 * q + s, 1024 * q + 1024, 16)) for s in range(16)],
                   first and j == 0, last and j == len(terms) - 1)

        for q in range(4):
            st["x%dv" % q] = lambda q=q: cp(Q("xg", q), IX(Xw, L("Pu", q)))
            st["x%ds" % q] = lambda q=q: act(Q("xg", q), IX(Xw, L("Pu", q)), F.Copy)
            st["d%d" % q] = lambda q=q: tt(Q("dg", q), IX(Xw, L(cu, q)), Q("xg", q), A.subtract)
            for j in range(2):
                st["d%d%s" % (q, "ab"[j])] = lambda q=q, j=j: tt(Q("dg", q, 512 * j, 512 * j + 512), IX(Xw, L(cu, q, 32 * j, 32 * j + 32)),
                                                                 Q("xg", q, 512 * j, 512 * j + 512), A.subtract)
            st["r%ds" % q] = lambda q=q: act(Q("rg", q), Q("dg", q), F.Relu)
            st["r%dv" % q] = lambda q=q: ts(Q("rg", q), Q("dg", q), 0.0, A.max)
            st["su%da" % q] = lambda q=q: sums(q, [("Sn", 0, "dg")], True, False)
            st["su%db" % q] = lambda q=q: sums(q, [("S2", 0, "rg")], False, True)
            st["nk%d" % q] = lambda q=q: ts(L("nk", q), Bk(SUB[q][0], SUB[q][1], SUB[q][1] + 64), col(12), A.is_gt, 4096.0, A.mult)
            st["hp%d" % q] = lambda q=q: tt(L("hp", q), L("hh", q), L("nk", q), A.max)
            st["Hu%d" % q] = lambda q=q: cp(L("Hu", q), L("hp", q))
            st["z%d" % q] = lambda q=q: act(Q("zg", q), IX(Xw, L("Hu", q)), F.Copy)
            st["pm%d" % q] = lambda q=q: scan(Q("pm", q, 16, 1040), R("ctl"), Q("ll", q, 16, 1040), A.add, A.min)
            for j in range(2):
                st["pm%d%s" % (q, "ab"[j])] = lambda q=q, j=j: scan(Q("pm", q, 16 + 512 * j, 528 + 512 * j), R("ctl", 0, 512), Q("ll", q, 16 + 512 * j, 528 + 512 * j), A.add, A.min)
        st["y1"] = lambda: act(Q("dg", 1), IX(Xw, L(cu, 1)), F.Copy)
        st["dx"] = lambda: [mm([(Bk(6 - j), R("In"), Q("xg", 1, 512 * j, 512 * j + 512))], True, False) for j in range(2)]
        st["dy"] = lambda: [mm([(Bk(6 - j), Id, Q("dg", 1, 512 * j, 512 * j + 512))], False, True) for j in range(2)]
        for j in range(2): st["r1" + "ab"[j]] = lambda j=j: act(Q("rg", 1, 512 * j, 512 * j + 512), Bk(6 - j), F.Relu)
        st["su1"] = lambda: sums(1, [("Sn", 144, "xg"), ("Sn", 0, "dg"), ("S2", 0, "rg")], True, True)
        st["tqb"] = lambda: mm([(tq, R("In"), R("nk"))], False, True)
        st["AA"] = lambda: tt(R("AA", 8, 264), tq, R("hp"), A.min)
        for j in (1, 2, 3):
            st["A%d" % j] = lambda j=j: act(R("A%d" % j), R("AA"), bias=4096.0 * j)

        def mx(i8, parts):
            h, b = i8 // 4, i8 % 4
            for part in parts:
                trip = []
                for s in range(4 * b, 4 * b + 4):
                    o = Bk(b, 128 * (s % 4), 128 * (s % 4) + 128)
                    if part == 2: trip.append((o, R("Bm", 128 * s, 128 * s + 128), R("nk", 128 * h, 128 * h + 128)))
                    else: trip.append((o, Id, R(("xg", "rg")[part], 2048 * h + s, 2048 * h + 2048, 16)))
                mm(trip, part == 0, part == 2)

        def lmin(i8):
            h, b = i8 // 4, i8 % 4
            trip = [(R("ll", 16 + 2048 * h + 128 * s, 144 + 2048 * h + 128 * s), Bk(b, 128 * (s % 4), 128 * (s % 4) + 128),
                     R("zg", 2048 * h + s, 2048 * h + 2048, 16)) for s in range(4 * b, 4 * b + 4)]
            add("v", [r for x in trip for r in rgs(x[1], x[2])], [r for x in trip for r in rgs(x[0])],
                [(lambda x=x: V.tensor_tensor(x[0]["ap"], x[1]["ap"], x[2]["ap"], A.min)) for x in trip])
        for i in range(8):
            h, c, bk, e0 = i // 4, i % 4, Bk(PMB[i]), 512 * i
            for nm, parts in (("xa", (0,)), ("mr", (1,)), ("mw", (2,)), ("mx", (0, 1, 2))): st["%s%d" % (nm, i)] = lambda i=i, parts=parts: mx(i, parts)
            st["l%d" % i] = lambda i=i: lmin(i)
            st["nn%d" % i] = lambda h=h, c=c, bk=bk: mm([(bk, R("nT", 128 * h, 128 * h + 128), R("nS", 512 * c, 512 * c + 512))], True, False)
            st["pq%d" % i] = lambda e0=e0, bk=bk: mm([(bk, Id, R("pm", 16 + e0, 528 + e0))], False, True)
            st["in%d" % i] = lambda e0=e0, bk=bk: act(R("ind", e0, e0 + 512), bk, F.Sign, bias=0.5)
            st["ct%d" % i] = lambda h=h, c=c: mm([(Bk(5, 256 + 128 * h + s, 384 + 128 * h, 16), R("ind", 2048 * h + 128 * s, 2048 * h + 128 * s + 128), R("G1"))
                                                  for s in range(4 * c, 4 * c + 4)], alone=True)
            st["fs%d" % i] = lambda e0=e0: scan(R("zg", e0, e0 + 512), R("ct0"), R("ind", e0, e0 + 512), A.mult, A.add)
        for h in range(2):
            st["mK%d" % h] = lambda h=h: ts(R("mK", 128 * h, 128 * h + 128), Bk(5, 256 + 128 * h, 384 + 128 * h), 0.0, A.is_gt)
        st["f0"] = lambda: mm([(Bk(2, 256, 320), Id, R("ind", k, 2048, 32)) for k in range(32)])
        st["fc"] = lambda: act(R("zg", 0, 64), Bk(2, 256, 320))
        st["fb"] = lambda: act(R("fb"), IX(R("zg"), R("fpl")), bias=0.25, scale=1.0 / 128)
        for b in range(4): st["TB%d" % b] = lambda b=b: mm([(Bk(b, 0, 256), R("TB"), R("TR", 256 * b, 256 * b + 256))], True, False)
        st["k1a"] = lambda: mm([(Bk(7, 0, 8), ones, base), (Bk(7, 0, 4), R("mK", 0, 128), R("LE", 12, 16))], True, False)
        st["k1b"] = lambda: mm([(Bk(7, 4, 8), R("mK", 128, 256), R("LE", 12, 16))], False, True)
        st["ul0"] = lambda: ts(R("ul", 0, 8), Bk(7, 0, 8), col(9), A.add, 4112.0, A.min)
        st["k1m"] = lambda: [mm([(Bk(4, 128 * j, 128 * j + 128, p1=8), R(a, 4 - 4 * h, 12 - 4 * h), R("mK", 128 * h, 128 * h + 128)) for h in range(2)])
                             for j, a in enumerate(("L1", "LE"))]
        st["KT1"] = lambda: act(R("KT1", p1=8), Bk(4, 0, 256, p1=8))

        def pairs(src, mat, last):
            for b in range(4):
                mm([(Bk(b, 128 * j, 128 * j + 128), R(mat, 128 * (2 * b + j), 128 * (2 * b + j) + 128), src) for j in range(2)], False, last)

        def sign(b, c):
            o = R("sg", 256 * b, 256 * b + 256)
            if SG_ON[b] == "s": act(o, Bk(b, 0, 256), F.Sign)
            else: ts(o, Bk(b, 0, 256), c - 1.0, A.is_gt, 2.0, A.mult)

        def ranks(b):
            mm([(rk, R("Pa", 128 * (14 - j), 128 * (15 - j)) if j < 7 else R("Ia"), R("sg", 128 * j, 128 * j + 128)) for j in (2 * b, 2 * b + 1)], False, b == 3)
        st["pf"] = lambda: pairs(R("fb"), "Pn", False)
        st["pb1"] = lambda: pairs(R("b1"), "Pn", True)
        st["ps"] = lambda: [mm([(Bk(b, 0, 256), Id, R("sg", 256 * b, 256 * b + 256))], True, False) for b in range(4)]
        st["pb2"] = lambda: pairs(R("b2"), "Pa", True)
        for c in (1, 2):
            lo = Bk(7, 8 * c, 8 * c + 8)
            st["b%d" % c] = lambda c=c: tt(R("b%d" % c), IX(lw, R("ul", 8 * c - 8, 8 * c)), nn, A.is_ge)
            st["e%d" % c] = lambda c=c: act(R("e%d" % c), IX(lw, R("ul", 8 * c - 8, 8 * c)), F.Abs)
            st["rk%d" % c] = lambda c=c: mm([(rk, ones, R("CR", 128 * c - 128, 128 * c)), (rk, R("I64"), R("fb"))] + [(rk, R("I4"), R("b1"))] * (c - 1), True, False)
            st["rv%d" % c] = lambda c=c: mm([(rk, R("I4"), R("b%d" % c))], False, False)
            for b in range(4):
                st["sg%d%s" % (c, "abcd"[b])] = lambda b=b, c=c: sign(b, c)
                st["rs%d%s" % (c, "abcd"[b])] = lambda b=b: ranks(b)
            st["lo%d" % c] = lambda c=c, lo=lo: mm([(lo, ones, base), (lo, ke, R("RB", 8 * c, 8 * c + 8))], True, False)
            st["q%d" % c] = lambda: ts(R("qq"), rk, LO, A.max, HI, A.min)
            st["ls%d" % c] = lambda lo=lo: mm([(lo, R("Sn", 159 - s, 287 - s), R("qq", s, 128, 16)) for s in range(16)], False, True)
            st["kt%d" % c] = lambda: mm([(Bk(4, s, 128, 16, p1=8), R("qq", s, 128, 16), R("G1")) for s in range(16)], alone=True)
            st["ul%d" % c] = lambda c=c, lo=lo: ts(R("ul", 8 * c, 8 * c + 8), lo, col(10), A.add, 4112.0, A.min)
            st["KT%d" % (c + 1)] = lambda c=c: act(R("KT%d" % (c + 1), p1=8), Bk(4, 0, 128, p1=8), F.Relu, bias=QC + 1)
        st["e3"] = lambda: tt(R("e3"), R("e1"), R("e2"), A.min)
        st["M"] = lambda: tt(Mm, IX(pw, R("ul", 16, 24)), R("e3"), A.min)
        st["of0"] = lambda: mm([(Bk(7, 32, 48), kv[0], R("RA", 0, 16)), (Bk(7, 40, 48), ke, R("RB", 0, 8))])
        st["of1"] = lambda: mm([(Bk(7, 48, 56), kv[1], R("RA", 16, 24))])
        st["of2"] = lambda: mm([(Bk(7, 56, 64), kv[2], R("RA", 24, 32)), (Bk(7, 56, 64), ke, R("RB", 24, 32))])
        st["um"] = lambda: ts(R("un", 24, 32), Bk(7, 40, 48), col(1), A.add)
        for c in range(3):
            at = (32, 48, 56)[c]
            st["un%d" % c] = lambda c=c, at=at: ts(R("un", 8 * c, 8 * c + 8), Bk(7, at, at + 8), 7.0 if c else 8.0, A.add)
            st["fr%d" % c] = lambda c=c: act(R("gd"), IX(R("A3"), R("un", 8 * c, 8 * c + 8)), F.Copy)
            st["sc%d" % c] = lambda: scan(R("sc"), R("c0"), R("gd"), A.add, A.min)
            st["pt%d" % c] = lambda c=c: ts(R("A3", 7 - c, 263 - c, 32), lane, col(15), A.add)
        st["g1"] = lambda: mm([(g1, kv[0], R("RU")), (g1, ke, R("RE"))])
        for j, gj in ((1, g1), (2, g2)): st["t%d" % j] = lambda j=j, gj=gj: tt(gj, gj, R("A%d" % j, 8 - j, 264 - j), A.min)
        st["o1"] = lambda: tt(R("o1"), g1, R("AA", 8, 264), A.max)
        st["g2"] = lambda: mm([(g2, kv[1], R("RU")), (g2, ke, R("RE"))])
        st["o2"] = lambda: tt(R("o2"), g2, R("o1"), A.max)
        st["g3a"] = lambda: mm([(g1, kv[1], R("RV")), (g1, ke, R("RE"))], True, False)
        st["g3b"] = lambda: mm([(g1, kv[2], R("RU"))], False, True)
        st["t3"] = lambda: tt(g1, g1, R("A3", 5, 261), A.min)
        st["i3"] = lambda: tt(R("i3"), g1, R("o2"), A.max)
        st["Ni"] = lambda: ts(R("Ni"), R("i3"), 4095, A.bitwise_and)
        st["Nu"] = lambda: cp(R(nu), R("Ni"))
        st["Nu0"] = lambda: ts(R(nu, 0, 256, 32), lane, col(16), A.add)
        st["g4"] = lambda: mm([(g4, kv[1], R("RV")), (g4, kv[2], R("RU"))])
        st["t4"] = lambda: tt(g4, g4, R("Cm"), A.max)
        st["i4"] = lambda: tt(R("i4"), g4, R("i3"), A.min)
        st["i40"] = lambda: ts(R("i4", 0, 256, 32), lane, col(16), A.add)
        st["Pi"] = lambda: ts(R("Pi"), R("i4"), 4095, A.bitwise_and)
        st["Pu"] = lambda: cp(R("Pu" if t < RO - 1 else "pq"), R("Pi"))
        st["th1"] = lambda: t < RO - 1 and (
            add("s", rgs(ke), rgs(R("nT", 0, 128, p1=8), R("thf", 1, 2)),
                [lambda: S.activation(T.nT[0:8, 0:128], T.KT1[0:8, 128:256], F.Identity, accum_out=T.thf[:, 1:2])]),
            mm([(Bk(2, 256, 257), R("ONf"), R("thf", 1, 2))]))
        st["th2"] = lambda: t < RO - 1 and ts(R("ti", 0, 1), Bk(2, 256, 257), 1.0 / 8192, A.mult)
        st["th3"] = lambda: t < RO - 1 and ts(R("ti", 1, 2), R("ti", 0, 1), 63, A.bitwise_and)
        st["th4"] = lambda: t < RO - 1 and tt(col(12), R("ti", 1, 2), col(11), A.add)
        st["Sw"] = lambda: mm([(Bk(7, 64, 72), R("Sw", 15 - s, 143 - s), R(nb, 128 + s, 256, 16)) for s in range(16)])
        st["vv"] = lambda: mm([(rk, Id, nn), (rk, Id, Mm)])
        st["si0"] = lambda: cp(R("si", 0, 8), Bk(7, 64, 72))
        st["si1"] = lambda: ts(R("si", 8, 16), R("si", 0, 8), 31, A.bitwise_and)
        st["si2"] = lambda: tt(R("si", 16, 24), R("si", 8, 16), R("sb"), A.add)
        st["us"] = lambda: cp(R("us"), R("si", 16, 24))
        st["v2"] = lambda: ts(R("v2"), rk, 0.5, A.mult, -0.25, A.add)

        def put():
            if t < RO - 1:
                add("v", rgs(R("us"), R("v2")), rgs(R("X", 0, 4096)), [lambda: V.tensor_copy(T.X[:, 0:4096].indirect(T.us[:]), T.v2[:])])
            else:
                tt(R("dl"), IX(Xw, R("us")), R("v2"), A.subtract)
                tt(R("oy"), R("ox"), R("dl"), A.subtract)
        st["put"] = put
        st["mo"] = lambda: act(R(mo), IX(R(nb), R("un", 24, 32)), F.Copy)
        dst = cores[(rank + 1 + t % 3) % len(cores)]
        hlp = helper_of(topo, cores, core, dst); to = dst if hlp is None else hlp
        rid, pid = topo.addr(to, core); mask = engines_mask(topo, core, to)

        def send(src, land, sem):
            add("g", rgs(src), [], [lambda: g.remote_dma(land["ap"], src["ap"], sem, T.sem.sent, pid, rid, mask)], rem=True)
            add("x", [], rgs(land), [], sem=sem, val=NENG)
            nsent[0] += NENG
        st["sendN"] = lambda: send(R(nu), R("Cu%d" % (t + 1)), T.sem["ac%d" % t])
        st["sendM"] = lambda: send(R(mo), R("nb%d" % (t + 1), 0, 128), T.sem["an%d" % t])
        st.update(late)
        return st

    rounds = [steps(t) for t in range(RO)]
    for t in range(RO):
        for nm in " ".join((FIRST, JOIN0, CUTS) if t == 0 else (LOOKUP, JOIN, CUTS)).split():
            at = len(ops)
            if nm[-1] != "+": rounds[t][nm]()
            elif t + 1 < RO: rounds[t + 1][nm[:-1]]()
            for o in ops[at:]: o["step"] = (t, nm)
    dma("s", T.yx[:], R("oy"))
    for r in range(8): act(R("op", r, 256, 8), R("pq", 32 * r, 32 * r + 32))
    dma("y", T.yp[:], R("op"))
    for r in range(8): cp(R("oc", r, 256, 8), R("Cu%d" % RO, 32 * r, 32 * r + 32))
    dma("s", T.yn[:], R("nb%d" % RO, 0, 128))
    dma("y", T.yc[:], R("oc"))
    run(ops, g, T)
    g.wait_ge(T.sem.sent, nsent[0])
